import numpy as np, ml_dtypes
CORES = [12,28,60,100,156,228]
N = 6
BF = ml_dtypes.bfloat16
V, X, PS, RO, EP = 1280, 256, 128, 4, 2
K = V // PS; W = V + (N - 1) * X
def blocks(a):
    return np.repeat(np.swapaxes(a, -1, -2), PS, axis=-1)
def kin(rng):
    sh = (N, 8, 16, V); u = rng.random(sh)
    a = blocks(rng.integers(0, K, (8, K, 16))) * PS + rng.integers(0, PS, sh)
    return np.where(u > 0.95, np.arange(V), np.where(u < 0.5, a, rng.integers(0, W, sh)))
def parts(rng):
    sh = (N, 8, 16, V)
    p = rng.choice(np.array([0.3, 0.6, 0.8, 0.95]), (8, K, 16))
    s = np.maximum(rng.integers(40, 256, (8, K, 16)) * rng.choice(np.array([0.25, 0.5, 1.0]), (N, 8, K, 16)), 1.0)
    w = np.where(rng.random(sh) < blocks(p), 1 + (rng.random(sh) * blocks(s)).astype(np.int64), 0)
    l = kin(rng); r = kin(rng)
    same = rng.random((8, K)) < 0.25; same[np.arange(8), rng.integers(0, K, 8)] = True
    r = np.where(np.repeat(same, PS, axis=1)[:, None, :], l, r)
    return w, l, r
def pack(w, l, r):
    return {"w": np.ascontiguousarray(w).reshape(N, 128, V).astype(np.float32).astype(BF), "kids": np.ascontiguousarray(l + 4096 * r).reshape(N, 128, V).astype(np.int32)}
def setup_inputs(rng):
    w, l, r = parts(rng)
    return pack(w, l, r)
KL = np.array([1, 2, 6, 4, 5, 6, 6, 7, 6, 9, 11, 11, 13, 14, 12, 11])
KR = np.array([1, 2, 6, 4, 5, 7, 6, 7, 8, 9, 12, 11, 13, 14, 12, 6])
HQ = np.array([100, 100, 100, 100, 100, 100, 100, 60, 60, 0, 120, 20, 100, 100, 100, 120])
def crypt(rng, w, l, r, g):
    ops = [int(i) for i in 1 + rng.permutation(15)[:5]]; q, p, u = ops[:3]
    z = 2 * PS; h = PS // 4; cp = h // 8; s = z + 2 * h; e = z + PS
    w[:, g, :, z:e] = 0; w[:, g, p, z:z + h] = 255
    nul = z + h + rng.integers(0, h, (N, 1, h)); l[:, g, :, z:z + h] = nul; r[:, g, :, z:z + h] = nul
    at = s + np.arange(16)[:, None] * cp + np.arange(cp)
    l[:, g, :, s:e] = at[KL].reshape(-1); r[:, g, :, s:e] = at[KR].reshape(-1)
    w[:, g, q, s:e] = np.repeat(HQ, cp)
    w[:, g, 0, s + 9 * cp:s + 10 * cp] = 100; w[:, g, u, s + 6 * cp:s + 7 * cp] = 50
    return at, ops
def seat(rng, w, l, r, g, k, ops, x, y):
    e = slice(k * PS, k * PS + PS); q, u = ops[0], ops[2]
    w[:, g, :, e] = rng.integers(0, 51, (N, 16, PS)); w[:, g, 0, e] = 0; w[:, g, u, e] = 0
    w[:, g, q, e] = rng.integers(200, 256, (N, PS)); l[:, g, q, e] = x; r[:, g, q, e] = y
def lone(rng, w, l, r, g, n):
    at, ops = crypt(rng, w, l, r, g); cp = at.shape[1]; bl = [k for k in range(K) if k != 2]
    for j in range(N + 1):
        m = rng.random((N, PS)) < 0.5
        if j < N:
            m = np.zeros((N, PS), bool); m[j, rng.integers(0, PS)] = True
        x = at[3 - n + 3 * m, rng.integers(0, cp, (N, PS))]
        seat(rng, w, l, r, g, bl[j], ops, x, x)
def stage(rng, w, l, r, g):
    at, ops = crypt(rng, w, l, r, g); cp = at.shape[1]; q, p, u, a, b = ops; sh = (N, PS)
    def some(j):
        return at[j, rng.integers(0, cp, sh)]
    y = some(6); w[:, g, :, :PS] = 0; w[:, g, u, :PS] = rng.integers(200, 256, sh); l[:, g, u, :PS] = y; r[:, g, u, :PS] = y
    x = some(8); seat(rng, w, l, r, g, 1, ops, x, x)
    x = some(9); seat(rng, w, l, r, g, 3, ops, x, x)
    m = np.argsort(rng.random(sh), axis=1) < 5 * PS // 8; i = rng.integers(0, cp, sh)
    seat(rng, w, l, r, g, 4, ops, at[np.where(m, 14, 10), i], at[np.where(m, 11, 12), i])
    seat(rng, w, l, r, g, 5, ops, some(15), some(12))
    x = V + rng.integers(0, N - 1, sh) * X + rng.integers(0, PS, sh); seat(rng, w, l, r, g, 6, ops, x, x)
    x = some(6); seat(rng, w, l, r, g, 7, ops, x, x + V)
    x = some(6); seat(rng, w, l, r, g, 8, ops, x, x + 2048)
    e = slice(9 * PS, 10 * PS); lo, hi = min(a, b), max(a, b); x = some(6); y = some(7)
    seat(rng, w, l, r, g, 9, ops, x, x); w[:, g, q, e] = rng.integers(100, 150, sh)
    v = rng.integers(150, 255, N * PS); v[0] ^= np.add.reduce(v) & 1
    o = rng.permutation(v); o[np.argmin(o)] += 1
    w[:, g, lo, e] = v.reshape(sh); w[:, g, hi, e] = o.reshape(sh)
    l[:, g, lo, e] = x; r[:, g, lo, e] = x; l[:, g, hi, e] = y; r[:, g, hi, e] = y
def setup_inputs_twin(rng):
    w, l, r = parts(rng); P = PS
    w[:, :2, :, :P] = 255
    w[:, :2, :, P:2 * P] = rng.integers(200, 256, (N, 2, 16, P))
    w[:, :2, :, 2 * P:3 * P] = rng.integers(100, 151, (N, 2, 16, P))
    w[:, :2, :, 3 * P:4 * P] = np.where(rng.random((N, 2, 16, P)) < 0.6, rng.integers(1, 10, (N, 2, 16, P)), 0)
    c = 2 * P + rng.integers(0, P, (N, 2, 1, P))
    l[:, :2, :, :P] = c; r[:, :2, :, :P] = P + np.arange(P)
    l[:, :2, :, P:2 * P] = 3 * P + rng.integers(0, P, (N, 2, 16, P)); r[:, :2, :, P:2 * P] = c
    l[:, :2, :, 2 * P:3 * P] = 3 * P + rng.integers(0, P, (N, 2, 16, P)); r[:, :2, :, 2 * P:3 * P] = 3 * P + rng.integers(0, P, (N, 2, 16, P))
    odd = np.arange(1, K, 2) * P + P - 1
    big = w[N - 1, 4:6]; big[:, :, odd] = 255
    r[:, 4:7] = np.where(w[:, 4:7] == 0, rng.integers(0, W, (N, 3, 16, V)), l[:, 4:7])
    sub = r[N - 1, 4:6]; sub[:, :, odd] = (l[N - 1, 4:6][:, :, odd] + 1) % W
    lone(rng, w, l, r, 2, 1); stage(rng, w, l, r, 3); lone(rng, w, l, r, 7, RO - 1)
    return pack(w, l, r)
def setup_inputs_ties(rng):
    w, l, r = parts(rng); h = (K // 2) * PS
    w[:, 0] = 255
    w[:, 1] = np.where(w[:, 1] > 0, 9, 0)
    for g in (1, 4, 5): w[:, g, 1::2] = w[:, g, 0::2]
    w[:, 6] = np.minimum(w[:, 6], 2)
    w[:, 2:4, :, :h] = 255
    a = h + rng.integers(0, V - h, (N, 2, 16, h)); l[:, 2:4, :, :h] = a
    r[:, 2:4, :, :h] = a.reshape(N, 2, 16, K // 2, PS)[..., rng.permutation(PS)].reshape(N, 2, 16, h)
    e = (K - 2) * PS; f = (K - 1) * PS
    w[:, 7, :, :2 * PS] = 255; w[:, 7, :, e:] = 0
    w[:, 7, 9, e:f] = 100; w[:, 7, 2, f:] = 100
    l[:, 7, :, :2 * PS] = e + rng.integers(0, PS, (N, 16, 2 * PS)); r[:, 7, :, :2 * PS] = f + rng.integers(0, PS, (N, 16, 2 * PS))
    l[:, 7, :, e:f] = f + rng.integers(0, PS, (N, 16, PS)); r[:, 7, :, e:f] = f + rng.integers(0, PS, (N, 16, PS))
    l[:, 7, :, f:] = e + rng.integers(0, PS, (N, 16, PS)); r[:, 7, :, f:] = e + rng.integers(0, PS, (N, 16, PS))
    return pack(w, l, r)
def setup_inputs_scarce(rng):
    w, l, r = parts(rng); q = rng.permutation(N)
    w = np.where(rng.random(w.shape) < blocks(rng.choice(np.array([0.1, 0.3, 0.6]), (8, K, 16))), w, 0)
    w[q[0], 4:] = 0; w[:, 0, :, :PS] = 0
    w[:, 1, :, 2 * PS:3 * PS] = 0; v = 2 * PS + 5
    w[q[1], 1, :, v] = 255; l[q[1], 1, :, v] = V; r[q[1], 1, :, v] = W - 1
    w[:, 1, :, 0] = 200; w[:, 1, :, X - 1] = 100
    return pack(w, l, r)
def setup_inputs_ends(rng):
    w, l, r = parts(rng); e = np.array([0, V - 1, V, W - 1, X - 1])
    for g in (0, 3, 6):
        l[:, g] = rng.choice(e, (N, 16, V)); r[:, g] = rng.choice(e, (N, 16, V))
    for g in (1, 5): l[:, g] = np.where(rng.random((N, 1, V)) < 0.4, np.arange(V), l[:, g])
    l[:, 2] = rng.integers(V, W, (N, 16, V)); r[:, 2] = rng.integers(V, W, (N, 16, V)); w[:, 2] = np.maximum(w[:, 2], 1)
    l[:, 4] = rng.integers(0, V, (N, 16, V)); r[:, 4] = rng.integers(0, V, (N, 16, V))
    r[:, 7] = np.where(rng.random((N, 16, V)) < 0.5, np.arange(V), r[:, 7])
    return pack(w, l, r)
def setup_inputs_spread(rng):
    w, l, r = parts(rng); sh = w.shape
    w = np.minimum((np.exp2(8 * rng.random((N, 8, 1, V))) * rng.random(sh)).astype(np.int64), 255)
    l = np.where(rng.random(sh) < 0.5, np.minimum((W * rng.random(sh) ** 3).astype(np.int64), W - 1), l)
    return pack(w, l, r)
def check_inputs(d):
    bad = []; v = d["w"].astype(np.float32); k = d["kids"].astype(np.int64)
    if not np.all((v >= 0) & (v <= 255) & (v == np.floor(v))): bad.append("whole numbers of w")
    if np.min(k) < 0 or np.max(k & 4095) >= W or np.max(k >> 12) >= W: bad.append("class numbers of kids")
    return bad
def pick(tab, o, c):
    return np.take_along_axis(tab.reshape(N, 8, 16 * W), o * W + c, 2)
def reference(w, kids):
    tw = w.astype(np.float32).astype(np.int64).reshape(N, 8, 16, V); kd = kids.astype(np.int64).reshape(N, 8, 16, V)
    tl = kd & 4095; tr = kd >> 12; own = np.arange(V)
    ghost = np.broadcast_to(np.arange(V, W), (N, 8, 16, W - V))
    for ep in range(EP):
        fw = np.stack([np.concatenate([tw[a]] + [tw[(a - d) % N][:, :, :X] for d in range(1, N)], axis=2) for a in range(N)])
        fl = np.concatenate([tl, ghost], axis=3); fr = np.concatenate([tr, ghost], axis=3)
        live = np.ones((N, 8, V), bool); b = np.zeros((RO + 1, N, 8, V), np.int64); b[0] = own
        have = np.zeros((RO + 1, 8, K), bool); have[0] = True; x = []
        for t in range(1, RO + 1):
            U = np.zeros((8, K, t, 16), np.int64)
            for h in range(t):
                m = np.minimum(np.take_along_axis(fw, b[h][:, :, None, :], 3), tw) * live[:, :, None, :]
                s = np.add.reduce(np.add.reduce(m.reshape(N, 8, 16, K, PS), axis=4), axis=0)
                U[:, :, h] = np.where(have[h][:, :, None], s.transpose(0, 2, 1), -1)
            best = np.argmax(U.reshape(8, K, t * 16), axis=2)
            bh = np.repeat(best >> 4, PS, axis=1); bo = np.repeat(best & 15, PS, axis=1)
            cur = np.take_along_axis(b, np.broadcast_to(bh, (1, N, 8, V)), 0)[0]; x.append(cur)
            live = live & (pick(fw, bo, cur) > 0)
            lk = pick(fl, bo, cur); rk = pick(fr, bo, cur)
            b = np.where(np.arange(RO + 1)[:, None, None, None] == bh, lk, b); b[t] = rk
            drop = np.zeros((8, K), bool)
            for h in range(t):
                differ = np.any((live & (rk != b[h])).reshape(N, 8, K, PS), axis=(0, 3))
                drop = drop | (have[h] & ~differ)
            have[t] = ~drop
        lf = np.concatenate([live, np.zeros((N, 8, W - V), bool)], axis=2); die = np.zeros((N, 8, V), bool)
        for c in x[1:]: die = die | (np.take_along_axis(lf, c, 2) & (c != own))
        go = (live & ~die)[:, :, None, :]
        h0 = b[0]; h1 = b[0]
        for t in range(RO, 0, -1): h1 = np.where(np.repeat(have[t], PS, axis=1), b[t], h1)
        h0 = h0[:, :, None, :]; h1 = h1[:, :, None, :]
        nw = (np.take_along_axis(fw, h0, 3) + np.take_along_axis(fw, h1, 3)) >> 1
        tw = np.where(go, nw, tw); tl = np.where(go, h0, tl); tr = np.where(go, h1, tr)
    return {"yw": tw.reshape(N, 128, V).astype(np.float32).astype(BF), "yk": (tl + 4096 * tr).reshape(N, 128, V).astype(np.float32)}

@@ -1,0 +1,659 @@
+from concourse.bass import DstId, RemoteDMATransfer
+from concourse.mybir import AluOpType as OP, ActivationFunctionType as AF
+
+V, X, NP, RO, EP = 1280, 256, 10, 4, 2
+Z = 2560
+WT = 2576
+DV = float(Z * 4097)
+SL = 2592
+BIG = float(2 ** 21)
+MAGIC = 12582912.0
+MID = 98304.0
+UP = [0, 10, 30, 50]
+CP = [20, 40, 60]
+NX = [10, 30, 50, 70]
+XO = [0, 10, 40, 90]
+KS = [0, 2, 5, 9]
+
+F, B16, I32, U16 = "float32", "bfloat16", "int32", "uint16"
+SB_ = {
+    "W0": (WT, B16), "W1": (WT, B16), "H": (WT, B16), "ONES": (WT, B16), "LT": (WT, B16), "YW": (V, B16),
+    "KP": (WT, F), "WA": (2 * V + WT, I32), "WB": (WT, F), "CI": (V, F), "TL": (7 * SL, F),
+    "G0": (V + 32, F), "G1": (V + 32, F), "M": (4 * V, B16), "NF": (2 * V, F), "AA": (2048, B16),
+    "SND": (320, F), "LAND": (1600, F), "E1": (72, F), "E2": (72, F), "E3": (144, F), "E4": (72, F), "US": (72, F),
+    "PEN": (72, F), "PEN0": (72, F), "MM": (64, F), "KT": (64, F), "T1": (64, F), "S1": (64, F),
+    "BI": (32, F), "BJ": (32, F), "C6": (32, F), "GG": (64, F), "D1": (64, F), "S2": (64, F), "OFF": (12, U16),
+    "PP": (80, I32), "LB": (80, I32), "BB": (400, I32), "LU": (400, U16), "DM": (80, F), "DZ": (80, F),
+    "DZB": (80, B16), "NEQ": (240, B16), "XU": (240, U16), "EQ": (240, B16), "SC": (320, F), "QQ": (16, F),
+    "SBP": (32, F), "SBP0": (32, F), "LC": (80, F), "EQH": (32, F), "EQL": (32, F),
+    "NHT": (40, F), "HD": (40, F), "HS": (40, F), "HT": (24, F), "OFB": (6, U16), "CM": (16, F),
+    "GO": (80, F), "NG": (160, F), "DD": (160, F), "ML": (160, F), "MA": (160, F), "FL": (400, U16), "BS": (480, F),
+    "PI": (8, I32), "PF": (8, F), "PG": (8, F), "CC": (8, F), "J": (128, F), "JG": (128, F), "TH": (72, F),
+    "ID": (128, B16), "NEG": (128, B16), "BO": (128, B16), "M8": (240, F), "M16": (64, F),
+    "RF": (32, F), "REP": (16, U16), "BG": (2, U16), "GR": (4, U16), "TF": (24, F),
+}
+PS_ = ["PU", "PL", "PC", "PD0", "PD1", "PD2", "PD3", "PD4"]
+SCRATCH = {k: ("sbuf", [128, n], d) for k, (n, d) in SB_.items()}
+SCRATCH.update({k: ("psum", [128, 512], F) for k in PS_})
+SEMAPHORES = (["qv", "qs", "qp", "qg", "lw0", "lw1", "lk", "o0", "o1", "o2", "o3", "o4", "sent"]
+              + ["ad%d" % i for i in range(10)] + ["af%d" % i for i in range(10)] + ["rl%d" % i for i in range(10)])
+
+
+def routes(T, topo):
+    cores = list(T.cores)
+    near, help_ = [], []
+    for s, c in enumerate(cores):
+        near.append([r for r, d in enumerate(cores) if r != s and topo.may_write(c, d)])
+        far = [r for r in range(len(cores)) if r != s and r not in near[s]]
+        hs = [h for h in topo.cores_of(c) if T.rank_of(h) is None and topo.die(h) == topo.die(c)
+              and all(topo.may_write(h, cores[r]) for r in far)][:max(1, min(2, len(far)))]
+        help_.append([(h, far[i::len(hs)]) for i, h in enumerate(hs)] if far else [])
+    return near, help_
+
+
+def message(T, m, s, r, near):
+    n_ranks = len(T.cores)
+    if m >= 8:
+        w = T["W%d" % (m - 8)]
+        d = (r - s) % n_ranks
+        return w[:, 0:X], w[:, V + (d - 1) * X:V + d * X]
+    e, t = divmod(m, RO)
+    o, n = 160 * e + XO[t], NX[t]
+    order = [q for q in range(n_ranks) if r in near[q]] + [q for q in range(n_ranks) if q != r and r not in near[q]]
+    k = order.index(s) if s != r else 0
+    return T.SND[:, o:o + n], T.LAND[:, 5 * o + k * n:5 * o + (k + 1) * n]
+
+
+def fan_mask(topo, src_core, dst_cores):
+    mask = -1
+    for d in dst_cores:
+        mask &= topo.mask(src_core, d)
+    return mask
+
+
+def fan_count(topo, src_core, dst_cores):
+    return bin(fan_mask(topo, src_core, dst_cores)).count("1")
+
+
+def fan(g, T, topo, src_core, dsts, src, sem):
+    mask = fan_mask(topo, src_core, [d for d, _ in dsts])
+    ad = [topo.addr(d, src_core) for d, _ in dsts]
+    if len(dsts) == 1:
+        g.remote_dma(dsts[0][1], src, sem, T.sem.sent, ad[0][1], ad[0][0], mask)
+    else:
+        g.remote_dma_fused([RemoteDMATransfer(dst_ids=[DstId(rid=r, pnc=p) for r, p in ad], dma_engine_mask=mask,
+                                              remote_sem=sem, srcs=[src], dsts=[p for _, p in dsts])],
+                           local_sem=T.sem.sent)
+    return bin(mask).count("1")
+
+
+ORDER = [8, 0, 1, 2, 3, 9, 4, 5, 6, 7]
+
+
+def helper_program(g, core, T, topo, s, fars, near, help_):
+    cores = list(T.cores)
+    cnt = fan_count(topo, cores[s], [h for h, _ in help_[s]])
+    sent = 0
+    for m in ORDER:
+        g.wait_ge(T.sem["rl%d" % m], cnt)
+        src = message(T, m, s, s, near)[0]
+        sent += fan(g, T, topo, core, [(cores[r], message(T, m, s, r, near)[1]) for r in fars], src, T.sem["af%d" % m])
+    g.wait_ge(T.sem.sent, sent)
+
+
+def rank_program(g, core, T, topo):
+    near, help_ = routes(T, topo)
+    rank = T.rank_of(core)
+    if rank is None:
+        for s in range(len(help_)):
+            for h, fars in help_[s]:
+                if h == core:
+                    helper_program(g, core, T, topo, s, fars, near, help_)
+        return
+    cores = list(T.cores)
+    NR = len(cores)
+    src_near = [q for q in range(NR) if rank in near[q]]
+    src_far = [q for q in range(NR) if q != rank and q not in src_near]
+    cnt_near = sum(fan_count(topo, cores[q], [cores[r] for r in near[q]]) for q in src_near)
+    cnt_far = 0
+    for q in src_far:
+        for h, fars in help_[q]:
+            if rank in fars:
+                cnt_far += fan_count(topo, h, [cores[r] for r in fars])
+
+    ops = []
+
+    def a(name, lo=0, hi=None, st=1):
+        if hi is None:
+            hi = SB_[name][0]
+        ap = T[name][:, lo:hi] if st == 1 else T[name][:, lo:hi:st]
+        return {"ap": ap, "r": [(name, lo, hi)]}
+
+    def ind(win, off):
+        return {"ap": win["ap"].indirect(off["ap"]), "r": win["r"] + off["r"], "w": win["r"], "o": off["r"]}
+
+    def val(x):
+        return x["ap"] if isinstance(x, dict) else x
+
+    def add(q, outs, ins, fn, sem=None):
+        rd, wr = [], []
+        for x in ins:
+            if isinstance(x, dict):
+                rd += x["r"]
+        for x in outs:
+            wr += x.get("w", x["r"])
+            rd += x.get("o", [])
+        ops.append({"q": q, "rd": rd, "wr": wr, "fn": fn, "sem": sem})
+
+    def arrive(outs, sem, n):
+        add("x", outs, [], None, (sem, n))
+
+    def tt(o, x, y, op):
+        add("v", [o], [x, y], lambda e: e.tensor_tensor(o["ap"], x["ap"], y["ap"], op))
+
+    def ts(o, x, s1, op0, s2=None, op1=None):
+        if op1 is None:
+            add("v", [o], [x, s1], lambda e: e.tensor_scalar(o["ap"], x["ap"], val(s1), None, op0))
+        else:
+            add("v", [o], [x, s1, s2], lambda e: e.tensor_scalar(o["ap"], x["ap"], val(s1), val(s2), op0, op1))
+
+    def whole(o, x):
+        ts(o, x, MAGIC, OP.add, MAGIC, OP.subtract)
+
+    def cp(o, x):
+        add("v", [o], [x], lambda e: e.tensor_copy(o["ap"], x["ap"]))
+
+    def ms(o, c):
+        add("v", [o], [], lambda e: e.memset(o["ap"], c))
+
+    def tr(o, x):
+        add("v", [o], [x], lambda e: e.transpose(o["ap"], x["ap"]))
+
+    def scan(o, d0, d1, op0, op1):
+        add("v", [o], [d0, d1], lambda e: e.tensor_tensor_scan(o["ap"], d0["ap"], d1["ap"], 0.0, op0, op1))
+
+    def act(o, x, f=AF.Identity, bias=0.0, scale=1.0, acc=None):
+        if acc is None:
+            add("s", [o], [x], lambda e: e.activation(o["ap"], x["ap"], f, bias=bias, scale=scale))
+        else:
+            add("s", [o, acc], [x], lambda e: e.activation(o["ap"], x["ap"], f, accum_out=acc["ap"]))
+
+    def mm(o, pairs, start=True, stop=True):
+        def fn(e):
+            last = None
+            for i, (l, r) in enumerate(pairs):
+                last = e.matmul(o["ap"], l["ap"], r["ap"], start and i == 0, stop and i == len(pairs) - 1)
+            return last
+        add("p", [o], [x for p in pairs for x in p], fn)
+
+    def iota(o, pat, base=0, cm=0, fl=True):
+        if fl:
+            add("g", [o], [], lambda e: e.iota(o["ap"], pat, base, cm, allow_small_or_imprecise_dtypes=True))
+        else:
+            add("g", [o], [], lambda e: e.iota(o["ap"], pat, base, cm))
+
+    def dma(q, outs, ins, o, i, sem):
+        add(q, outs, ins, lambda e: e.dma_start(o, i), (sem, 16))
+
+    sent = [0]
+
+    def send(m, src):
+        def fn(e):
+            ap = message(T, m, rank, rank, near)[0]
+            if help_[rank]:
+                sent[0] += fan(e, T, topo, core, [(h, ap) for h, _ in help_[rank]], ap, T.sem["rl%d" % m])
+            if near[rank]:
+                sent[0] += fan(e, T, topo, core, [(cores[r], message(T, m, rank, r, near)[1]) for r in near[rank]],
+                               ap, T.sem["ad%d" % m])
+        add("g", [], [src], fn, "none")
+
+    col = lambda name, j: a(name, j, j + 1)
+    v80 = a("BS", 0, 80)
+
+    def colsum(src, lo, npat, ps, po):
+        mm(a(ps, po, po + 8 * npat), [(a("ID"), a(src, lo + i, lo + 128 * npat, 16)) for i in range(16)])
+
+    def finish(ps, lo, hi, so, dst):
+        scan(a("SC", so + lo, so + hi), a("M8", 0, hi - lo), a(ps, lo, hi), OP.mult, OP.add)
+        for d, n, p in dst:
+            cp(a("SND", d, d + n), a("SC", so + p + 7, so + p + 8 * n, 8))
+
+    def own_votes(w, dst):
+        colsum(w, 0, 6, "PL", 0)
+
+        def rest(k):
+            act(a("M", 128 * k, 128 * k + 128), a(w, 128 * k, 128 * k + 128), acc=col("SND", dst + k))
+        return rest
+
+    dma("y", [a("W0", 0, X)], [], T.W0[:, 0:X], T.w[:, 0:X], "lw0")
+    dma("s", [a("W0", X, V)], [], T.W0[:, X:V], T.w[:, X:V], "lw1")
+    dma("y", [a("WA", 0, V)], [], T.WA[:, 0:V], T.kids[:, 0:V], "lk")
+    iota(col("PI", 0), [[0, 1]], 0, 1, False)
+    iota(a("J"), [[1, 128]])
+    iota(a("TH", 0, 65), [[0, 13], [1, 5]])
+    iota(a("SBP0", 0, 25), [[256, 5], [-(2 * SL - 16), 5]], 3 * (2 * SL - 16) + 63)
+    iota(a("LC", 0, 75), [[2 * SL, 3], [256, 5], [16, 5]], SL + 15)
+    iota(a("RF", 0, 15), [[0, 3], [16, 5]])
+    send(8, a("W0", 0, X))
+    ms(a("M8"), 1.0)
+    ms(a("M16"), 0.0)
+    ms(a("KT"), 0.0)
+    p0 = col("PI", 0)
+    ts(col("PI", 1), p0, 15, OP.bitwise_and)
+    ts(col("PI", 2), p0, 4, OP.arith_shift_right)
+    ts(col("PI", 3), p0, 3, OP.arith_shift_right, 1, OP.bitwise_and)
+    ts(col("PI", 4), p0, 4, OP.arith_shift_right, 1, OP.bitwise_and)
+    ts(col("PI", 5), p0, 1, OP.bitwise_and)
+    ms(a("M8", 0, 240, 8), 0.0)
+    ms(a("M16", 0, 64, 16), -1e9)
+    cp(a("PF", 0, 6), a("PI", 0, 6))
+    ms(a("D1"), 80.0)
+    ms(a("PEN0"), -2.0 ** 18)
+    pa, phi = col("PF", 1), col("PF", 3)
+    ts(a("ID"), a("J"), col("PF", 0), OP.is_equal)
+    tt(col("PG", 0), col("PF", 4), col("PF", 5), OP.not_equal)
+    ts(col("PG", 1), pa, 16.0, OP.mult)
+    ts(col("PG", 2), phi, -1.0, OP.mult, 1.0, OP.add)
+    ts(a("TF", 0, 4), a("J", 0, 4), -16.0, OP.mult, 31.5 - 64 * MID, OP.add)
+    ts(v80, a("J", 0, 80), 16.0, OP.mult, pa, OP.add)
+    ts(col("PG", 3), col("PG", 0), 1296.0, OP.mult, col("PG", 1), OP.add)
+    ts(a("CC", 0, 4), a("TF", 0, 4), pa, OP.subtract, 1.0 / 64, OP.mult)
+    ts(a("TF", 4, 6), a("J", 0, 2), 16.0, OP.mult, 15.0, OP.add)
+    ts(col("PG", 4), phi, 32.0, OP.mult)
+    ts(a("TF", 16, 20), a("BS", 0, 4), -2.0, OP.add, 0.2, OP.mult)
+    ts(a("REP", 0, 15), a("RF", 0, 15), pa, OP.add)
+    ts(a("SBP0", 0, 25), a("SBP0", 0, 25), col("PG", 3), OP.add)
+    whole(a("TF", 20, 24), a("TF", 16, 20))
+    ts(a("LC", 0, 75), a("LC", 0, 75), col("PG", 3), OP.add)
+    ts(a("BG"), a("TF", 4, 6), col("PG", 4), OP.add)
+    ts(a("TF", 8, 12), a("TF", 20, 24), 6.0, OP.is_ge, -6.0, OP.mult)
+    for h in range(4):
+        ts(a("PEN0", UP[h], UP[h] + 10), a("J", 0, 10), 0.0, OP.mult, col("CC", h), OP.add)
+    cp(a("D1", 33, 54, 5), a("BS", 0, 5))
+    ms(a("D1", 34, 55, 5), 0.0)
+    ms(a("SBP0", 4, 25, 5), 0.0)
+    tt(a("TF", 12, 16), a("TF", 8, 12), a("TF", 20, 24), OP.add)
+    ts(a("TH", 0, 65), a("TH", 0, 65), 0.25, OP.mult, -0.5, OP.add)
+    ts(a("NEG"), a("J"), col("PF", 0), OP.is_equal, -1.0, OP.mult)
+    for w in ("W0", "W1", "H", "ONES"):
+        ms(a(w, Z, WT), 0.0)
+    ms(a("KP", Z, WT), DV)
+    cp(a("GR"), a("TF", 12, 16))
+    for gname in ("G0", "G1"):
+        ms(a(gname, 0, 16), 0.0)
+        ms(a(gname, V + 16, V + 32), 0.0)
+    rest = own_votes("W0", 0)
+    for k in range(6, NP):
+        rest(k)
+    finish("PL", 0, 48, 240, [(0, 6, 0)])
+    send(0, a("SND", 0, 10))
+    iota(a("CI"), [[4097, V]], V * 4097)
+    iota(a("JG"), [[1, 8], [0, 16]])
+    ts(a("BS", 80, 160), v80, -float(V), OP.add)
+    cp(a("BS", 160, 240), v80)
+    ms(a("BS", 240, 320), 0.0)
+    ts(a("BS", 320, 400), v80, float(WT), OP.add)
+    ms(a("BS", 400, 480), 0.0)
+    ms(a("NHT"), 0.0)
+    ms(a("HD"), 80.0)
+    ts(a("HD", 3, 40, 8), a("J", 0, 5), 16.0, OP.mult, 80.0, OP.add)
+    ts(a("HD", 7, 40, 8), a("J", 0, 5), 16.0, OP.mult, 80.0, OP.add)
+
+    def turn(src, slot):
+        tr(a("TL", slot * SL, slot * SL + V), a(src, 16, 16 + V))
+        tr(a("TL", slot * SL + V, (slot + 1) * SL), a(src))
+
+    for e in range(EP):
+        W = "W%d" % e
+        Wt = a(W)
+        ko = 0 if e == 0 else V + WT
+        cp(a("SBP", 0, 25), a("SBP0", 0, 25))
+        cp(a("PEN", 0, 70), a("PEN0", 0, 70))
+        tt(a("E1", 0, 10), a("SND", 160 * e, 160 * e + 10), a("PEN0", 0, 10), OP.add)
+        for i, (lo, hi) in enumerate([(0, 512), (512, 1024), (1024, V)]):
+            act(a("PD%d" % i, 0, hi - lo), a(W, lo, hi), AF.Relu, bias=DV, scale=-DV)
+            tt(a("G0", 16 + lo, 16 + hi), a("WA", ko + lo, ko + hi), a("PD%d" % i, 0, hi - lo), OP.max)
+        if e == 0:
+            act(a("NF", V, 2 * V), a(W, 0, V))
+        turn("G0", 0)
+        if e == 0:
+            ts(a("BO"), a("JG"), col("PF", 2), OP.is_equal, 2.0 ** 19, OP.mult)
+        gh = lambda q: ((rank - q) % NR - 1) * X
+        arrive([a(W, V + gh(q), V + gh(q) + X) for q in src_near], "ad%d" % (8 + e), cnt_near)
+        arrive([a(W, V + gh(q), V + gh(q) + X) for q in src_far], "af%d" % (8 + e), cnt_far)
+        for i, q in enumerate(src_near + src_far):
+            pd = a("PD%d" % ((i + 3) % 5), 0, X)
+            act(pd, a(W, V + gh(q), V + gh(q) + X), AF.Relu, bias=DV, scale=-DV)
+            tt(a("KP", V + gh(q), V + gh(q) + X), a("CI", gh(q), gh(q) + X), pd, OP.max)
+        if e > 0:
+            act(a("NF", V, 2 * V), a(W, 0, V))
+        act(a("KP", 0, V), a("G0", 16, 16 + V))
+
+        for t in range(1, RO + 1):
+            m = RO * e + t - 1
+            n, lo = NX[t - 1], 5 * (160 * e + XO[t - 1])
+            land = lambda k, c=1: a("LAND", lo + k * n, lo + (k + c) * n)
+            nn, nf = len(src_near), len(src_far)
+            arrive([land(0, nn)], "ad%d" % m, cnt_near)
+            arrive([land(nn, nf)], "af%d" % m, cnt_far)
+            e1, e2, e4, us = a("E1", 0, n), a("E2", 0, n), a("E4", 0, n), a("US", 0, n)
+            acc, k = e1, 0
+            if nn >= 3:
+                tt(e2, land(0), land(1), OP.add)
+                tt(e4, e1, land(2), OP.add)
+                tt(e1, e2, e4, OP.add)
+                k = 3
+            while k < nn:
+                nxt = e2 if acc is e1 else e1
+                tt(nxt, acc, land(k), OP.add)
+                acc, k = nxt, k + 1
+            parts = [land(nn + k) for k in range(nf)]
+            if nf == 4:
+                tt(a("E3", 0, 2 * n), land(nn, 2), land(nn + 2, 2), OP.add)
+                parts = [a("E3", 0, n), a("E3", n, 2 * n)]
+            if len(parts) == 2:
+                tt(e4, parts[0], parts[1], OP.add)
+                parts = [e4]
+            u = lambda h: a("US", UP[h], UP[h] + 10)
+            c = lambda h: a("US", CP[h], CP[h] + 10)
+            mmx = lambda j: a("MM", 10 * j, 10 * j + 10)
+            kt = lambda par: a("KT", 32 * par, 32 * par + 5)
+            if t == 1 and len(parts) == 1:
+                an, pn = acc["r"][0][0], parts[0]["r"][0]
+                for par in range(2):
+                    tt(kt(par), a(an, par, 10, 2), a(pn[0], pn[1] + par, pn[1] + 10, 2), OP.add)
+            else:
+                for k, p in enumerate(parts):
+                    nxt = us if k == len(parts) - 1 else (e2 if acc is e1 else e1)
+                    tt(nxt, acc, p, OP.add)
+                    acc = nxt
+                if not parts:
+                    cp(us, acc)
+                if t == 1:
+                    xs = ("US", 0)
+                    cp(mmx(0), u(0))
+                elif t == 2:
+                    tt(mmx(0), u(1), c(0), OP.min)
+                    xs = ("US", 0)
+                elif t == 3:
+                    tt(mmx(1), c(0), c(1), OP.min)
+                    tt(mmx(2), u(0), u(1), OP.max)
+                    tt(mmx(0), u(2), mmx(1), OP.min)
+                    xs = ("MM", 20)
+                else:
+                    tt(mmx(1), c(0), c(1), OP.min)
+                    tt(mmx(3), u(3), c(2), OP.min)
+                    tt(mmx(2), u(0), u(1), OP.max)
+                    tt(mmx(0), mmx(1), mmx(3), OP.min)
+                    tt(mmx(4), mmx(2), u(2), OP.max)
+                    xs = ("MM", 40)
+                for par in range(2):
+                    tt(kt(par), a(xs[0], xs[1] + par, xs[1] + 10, 2), a("MM", par, 10, 2), OP.max)
+            tr(a("T1"), a("KT"))
+            scan(a("S1"), a("M16"), a("T1"), OP.add, OP.max)
+            best = ind(a("S1"), a("BG"))
+            whole(a("BI"), best)
+            tt(a("BJ"), best, a("BI"), OP.subtract)
+            tr(a("C6"), a("BJ"))
+            code = lambda o: ts(o, a("C6", 0, 5), -64.0, OP.mult, -31.5, OP.add)
+            if t == 1:
+                code(a("S2", 0, 5))
+                tt(a("S2", 8, 13), a("S2", 0, 5), a("SBP0", 3, 25, 5), OP.add)
+                cp(a("OFF", 0, 5), a("S2", 8, 13))
+            else:
+                tt(a("GG"), ind(a("C6"), a("GR")), a("TH", 0, 64), OP.is_lt)
+                code(a("D1", 4, 25, 5))
+                scan(a("S2", 0, 55), a("GG", 0, 55), a("D1", 0, 55), OP.mult, OP.add)
+                cp(a("OFF", 0, 11), a("S2", 4, 55, 5))
+            off, offx = a("OFF", 0, 5), a("OFF", 6, 11)
+            tl = a("TL", 0, (2 * t - 1) * SL)
+            bold = a("BB", 0, 80 * t)
+            bt = a("BB", 80 * t, 80 * t + 80)
+            lu = lambda h, c0=0, c1=80: a("LU", 80 + 80 * h + c0, 80 + 80 * h + c1)
+            if t == 1:
+                cp(a("PP"), ind(tl, off))
+                ts(bt, a("PP"), 12, OP.arith_shift_right)
+                ts(bold, a("PP"), 4095, OP.bitwise_and)
+                cp(a("LU", 80, 240), a("BB", 0, 160))
+                llist = lu(0)
+            else:
+                tt(a("PP"), ind(tl, off), a("DM"), OP.max)
+                cp(a("XU", 80 * (t - 2), 80 * (t - 1)), ind(bold, offx))
+                llist = a("LU", 0, 80)
+                if t < RO:
+                    ts(bt, a("PP"), 12, OP.arith_shift_right)
+                    ts(a("LB"), a("PP"), 4095, OP.bitwise_and)
+                    cp(lu(t), bt)
+                else:
+                    ts(a("LB"), a("PP"), 4095, OP.bitwise_and)
+                    ts(bt, a("PP"), 12, OP.arith_shift_right)
+                    cp(llist, a("LB"))
+                tt(a("EQ", 80 * (t - 2), 80 * (t - 1)), ind(bold, offx), v80, OP.is_equal)
+
+            def dropped():
+                cm = c(0) if t == 2 else mmx(1)
+                if t == 4:
+                    cm = a("CM", 0, 10)
+                    tt(cm, mmx(1), c(2), OP.min)
+                ts(a("NHT", 5 - t, 40, 4), cm, 0.0, OP.is_lt)
+
+            if t < RO:
+                so = 160 * e + XO[t]
+                order = [t] + list(range(t))
+                ks = KS[t]
+
+                def gm(i, k0, k1):
+                    tt(a("M", V * i + 128 * k0, V * i + 128 * k1), ind(Wt, lu(order[i], 8 * k0, 8 * k1)),
+                       a("NF", V + 128 * k0, V + 128 * k1), OP.min)
+
+                nch = (ks + 3) // 4
+                chunks = [(ks * i // nch, ks * (i + 1) // nch) for i in range(nch)]
+                for i, (k0, k1) in enumerate(chunks):
+                    mk = a("M", 128 * k0, 128 * k1)
+                    act(mk, ind(Wt, lu(t, 8 * k0, 8 * k1)))
+                    mm(a("PD%d" % i, 0, 128 * (k1 - k0)), [(a("ID"), a(W, 128 * k0, 128 * k1)), (a("NEG"), mk)])
+                for i, (k0, k1) in enumerate(chunks):
+                    for k in range(k0, k1):
+                        act(a("M", 128 * k, 128 * k + 128), a("PD%d" % i, 128 * (k - k0), 128 * (k - k0 + 1)),
+                            AF.Relu, acc=col("QQ", k))
+                rep = a("REP", 0, 5 * t)
+                if t > 1:
+                    cp(ind(bold, offx), a("LB"))
+                    ts(a("DZ"), a("PP"), DV, OP.is_ge, float(Z), OP.mult)
+                    gm(0, ks, NP)
+                    tt(bold, ind(a("DZ"), rep), bold, OP.max)
+                    cp(llist, a("LB"))
+                    cp(a("LU", 80, 80 + 80 * t), bold)
+                    tt(a("NEQ", 0, 80 * t), ind(bt, rep), bold, OP.not_equal)
+                else:
+                    tt(a("NEQ", 0, 80), bt, bold, OP.not_equal)
+                    gm(0, ks, NP)
+                mm(a("PC", 0, 10 * t), [(a("BO"), a("NEQ", b, 80 * t, 8)) for b in range(8)])
+                colsum("M", 128 * ks, NP - ks, "PU", 8 * ks)
+                act(a("G0", 16, 16 + V), ind(a("KP"), lu(t)))
+                for h in range(t):
+                    act(a("SND", so + CP[h], so + CP[h] + 10), a("PC", 10 * h, 10 * h + 10))
+                for i in range(1, t):
+                    gm(i, 0, NP)
+                    colsum("M", V * i, NP, "PU", 80 * i)
+                gm(t, 0, 7)
+                colsum("M", V * t, 7, "PL", 0)
+                gm(t, 7, NP)
+                for k in range(7, NP):
+                    x = a("M", V * t + 128 * k, V * t + 128 * k + 128)
+                    act(x, x, acc=col("SND", so + UP[order[t]] + k))
+                if ks:
+                    tt(a("SND", so + UP[t], so + UP[t] + ks), a("SND", 160 * e, 160 * e + ks), a("QQ", 0, ks), OP.subtract)
+                finish("PU", 8 * ks, 80 * t, 0,
+                       [(so + UP[t] + ks, NP - ks, 8 * ks)] + [(so + UP[order[i]], 10, 80 * i) for i in range(1, t)])
+                finish("PL", 0, 56, 240, [(so + UP[order[t]], 7, 0)])
+                send(m + 1, a("SND", so, so + NX[t]))
+                act(a("G1", 16, 16 + V), ind(a("KP"), llist))
+                if e == 0:
+                    if t == 1:
+                        iota(a("WA", V, V + WT), [[1, WT]], 0, 0, False)
+                        act(a("ONES", 0, Z), a(W, 0, Z), bias=1.0, scale=0.0)
+                        act(a("LT", V, WT), a(W, V, WT), scale=0.0)
+                    elif t == 2:
+                        add("g", [a("AA")], [a("ONES", 0, 2048)],
+                            lambda en: en.affine_select(T.AA[:, 0:2048], T.ONES[:, 0:2048], [[-1000, 16], [-16, 8], [999, 16]],
+                                                        OP.is_equal, 0.0, 0, 1))
+                    else:
+                        iota(a("WB"), [[4096, WT]])
+                if t == 2:
+                    act(a("H", 0, Z), a(W, 0, Z), scale=0.5)
+                ts(a("DM"), a("PP"), DV, OP.is_ge, DV, OP.mult)
+                if t > 1:
+                    tt(a("EQH", 0, 25), a("GG", 1, 26), a("GG", 0, 25), OP.subtract)
+                    dropped()
+                    tt(a("EQL", 0, 25), a("EQH", 0, 25), a("LC", 25 * (t - 1), 25 * t), OP.mult)
+                else:
+                    cp(a("SBP", 3, 25, 5), a("LC", 3, 25, 5))
+                tr(a("TL", 2 * t * SL, 2 * t * SL + V), a("G0", 16, 16 + V))
+                if t > 1:
+                    nh = a("NHT", 5 - t, 40, 4)
+                    ts(a("PEN", UP[t - 1], UP[t - 1] + 10), nh, -BIG, OP.mult, col("CC", t - 1), OP.add)
+                    ts(a("PEN", CP[t - 1], CP[t - 1] + 10), nh, BIG, OP.mult, -2.0 ** 18, OP.add)
+                    tt(a("SBP", 0, 25), a("SBP", 0, 25), a("EQL", 0, 25), OP.max)
+                tr(a("TL", 2 * t * SL + V, (2 * t + 1) * SL), a("G0"))
+                tt(a("E1", 0, NX[t]), a("SND", so, so + NX[t]), a("PEN", 0, NX[t]), OP.add)
+                tt(a("D1", 0, 24), a("SBP", 0, 24), a("SBP", 1, 25), OP.subtract)
+                turn("G1", 2 * t - 1)
+                continue
+
+            ones, lt = a("ONES"), a("LT")
+            act(a("LT", 640, V), ind(ones, a("LU", 40, 80)))
+            cp(a("LT", 0, 640), ind(ones, a("LU", 0, 40)))
+            act(a("M", 2 * V, 3 * V), ind(lt, a("XU", 160, 240)))
+            act(a("M", V + 640, 2 * V), ind(lt, a("XU", 120, 160)))
+            dropped()
+            cp(ind(bold, offx), a("LB"))
+            cp(a("M", 0, V), ind(lt, a("XU", 0, 80)))
+            scan(a("HS"), a("NHT"), a("HD"), OP.mult, OP.add)
+            ts(a("DZB"), a("PP"), DV, OP.is_ge, float(Z), OP.mult)
+            cp(a("FL", 0, 80), a("BB", 0, 80))
+            tt(a("M", 0, 640), ind(lt, a("XU", 80, 120)), a("M", 0, 640), OP.add)
+            pc = a("PC", 0, 80)
+            pick = lambda lo2, hi2: [(a("AA", 128 * i, 128 * i + 128), a("M", lo2 + i, hi2, 16)) for i in range(16)]
+            mm(pc, [(a("NEG"), a("EQ", 80 * j, 80 * j + 80)) for j in range(3)] + [(a("ID"), a("DZB"))], True, False)
+            mm(pc, pick(2 * V, 3 * V), False, False)
+            mm(a("PC", 40, 80), pick(V + 640, 2 * V), False, False)
+            mm(pc, pick(0, V), False, True)
+            ts(a("HT", 0, 5), a("HS", 3, 40, 8), col("PG", 2), OP.mult, pa, OP.add)
+            ts(a("HT", 8, 13), a("HS", 7, 40, 8), phi, OP.mult)
+            tt(a("HT", 16, 21), a("HT", 0, 5), a("HT", 8, 13), OP.add)
+            tt(a("DD", 0, 80), a("BB", 0, 80), a("BS", 80, 160) if e == 0 else a("BS", 320, 400), OP.subtract)
+            cp(a("OFB", 0, 5), a("HT", 16, 21))
+            bsel = ind(a("BB"), a("OFB", 0, 5))
+            cp(a("FL", 80, 160), bsel)
+            cp(a("DD", 80, 160), bsel)
+            fl = lambda j, lo2, hi2: a("FL", 80 * j + lo2 // 16, 80 * j + hi2 // 16)
+            for lo2, hi2 in [(0, 512), (512, V)]:
+                act(a("G0", 16 + lo2, 16 + hi2), ind(Wt, fl(0, lo2, hi2)), bias=-0.25, scale=0.5)
+                tt(a("NF", lo2, hi2), ind(a("H"), fl(1, lo2, hi2)), a("G0", 16 + lo2, 16 + hi2), OP.add)
+
+            def w_list():
+                ts(a("NG", 0, 80), pc, 0.5, OP.is_ge, float(V), OP.mult)
+                tt(a("NG", 80, 160), a("NG", 0, 80), v80, OP.add)
+                cp(a("FL", 320, 400), a("NG", 80, 160))
+
+            def kid_lists():
+                ts(a("GO"), pc, 0.5, OP.is_lt)
+                tt(a("ML"), ind(a("GO"), a("REP", 0, 10)), a("DD"), OP.mult)
+                tt(a("MA"), a("ML"), a("BS", 160 + 160 * e, 320 + 160 * e), OP.add)
+                cp(a("FL", 160, 320), a("MA"))
+
+            def new_w(name, lo2, hi2):
+                whole(a(name, lo2, hi2), ind(a("NF"), fl(4, lo2, hi2)))
+
+            def kid_b(lo2, hi2):
+                act(a("G1", 16 + lo2, 16 + hi2), ind(a("WB"), fl(3, lo2, hi2)))
+
+            def kid_a(out, lo2, hi2):
+                win = a("WA", 0, V + WT) if e == 0 else a("WA", V, 2 * V + WT)
+                tt(out, ind(win, fl(2, lo2, hi2)), a("G1", 16 + lo2, 16 + hi2), OP.add)
+
+            if e < EP - 1:
+                w_list()
+                new_w("W1", 0, X)
+                send(9, a("W1", 0, X))
+                kid_lists()
+                kid_b(0, 640)
+                new_w("W1", X, 768)
+                rest = own_votes("W1", 160)
+                new_w("W1", 768, 1024)
+                rest(6)
+                rest(7)
+                new_w("W1", 1024, V)
+                rest(8)
+                rest(9)
+                kid_b(640, V)
+                finish("PL", 0, 48, 240, [(160, 6, 0)])
+                send(RO, a("SND", 160, 170))
+                for lo2, hi2 in [(0, 640), (640, V)]:
+                    kid_a(a("WA", V + WT + lo2, V + WT + hi2), lo2, hi2)
+            else:
+                kid_lists()
+                ck = [(0, 320), (320, 800), (800, V)]
+                for lo2, hi2 in ck:
+                    kid_b(lo2, hi2)
+                w_list()
+                for i, (lo2, hi2) in enumerate(ck):
+                    kid_a(a("TL", lo2, hi2), lo2, hi2)
+                    dma("y", [], [a("TL", lo2, hi2)], T.yk[:, lo2:hi2], T.TL[:, lo2:hi2], "o%d" % (1 + i))
+                for lo2, hi2, sem in [(0, 768, "o0"), (768, V, "o4")]:
+                    new_w("YW", lo2, hi2)
+                    dma("y", [], [a("YW", lo2, hi2)], T.yw[:, lo2:hi2], T.YW[:, lo2:hi2], sem)
+
+    eng = {"g": g, "v": g.vector, "s": g.scalar, "p": g.tensor, "y": g.sync}
+    hist, known = {}, {q: {} for q in eng}
+    for i, o in enumerate(ops):
+        q = o["q"]
+        o["key"] = ("own", i) if isinstance(o["sem"], tuple) else q
+        deps = set()
+        for kind in ("rd", "wr"):
+            for nm, lo, hi in o[kind]:
+                psum = nm in PS_
+                for (l2, h2, k2, j) in hist.get(nm, []):
+                    hit = (kind == "wr" or k2 == "wr") and lo < h2 and l2 < hi
+                    if psum:
+                        hit = ops[j]["q"] != q or (q != "p" and hit)
+                    if hit and ops[j]["sem"] != "none":
+                        deps.add(j)
+        o["waits"] = []
+        if q != "x":
+            for j in sorted(deps, reverse=True):
+                if known[q].get(ops[j]["key"], -1) >= j:
+                    continue
+                o["waits"].append(j)
+                ops[j]["need"] = True
+                for k2, v2 in ops[j]["snap"].items():
+                    if known[q].get(k2, -1) < v2:
+                        known[q][k2] = v2
+            o["snap"] = dict(known[q])
+        else:
+            o["snap"] = {}
+        o["snap"][o["key"]] = i
+        for kind in ("rd", "wr"):
+            for nm, lo, hi in o[kind]:
+                hist.setdefault(nm, []).append((lo, hi, kind, i))
+    count = {q: 0 for q in eng}
+    for o in ops:
+        q = o["q"]
+        if isinstance(o["sem"], tuple):
+            o["tok"] = o["sem"]
+        elif o.get("need"):
+            count[q] += 1
+            o["tok"] = ("q" + q, count[q])
+        if q == "x":
+            continue
+        for j in o["waits"]:
+            eng[q].wait_ge(T.sem[ops[j]["tok"][0]], ops[j]["tok"][1])
+        ins = o["fn"](eng[q])
+        if isinstance(o["sem"], tuple):
+            ins.then_inc(T.sem[o["sem"][0]], o["sem"][1])
+        elif o.get("need"):
+            ins.then_inc(T.sem["q" + q], 1)
+    for i in range(5):
+        g.sync.wait_ge(T.sem["o%d" % i], 16)
+    g.wait_ge(T.sem.sent, sent[0])

@@ -1,53 +1,55 @@
 from concourse.bass import DstId, RemoteDMATransfer
-from concourse.mybir import AluOpType as OP, ActivationFunctionType as AF
+from concourse.mybir import AluOpType as OP, ActivationFunctionType as AF, AxisListType as AX
 
 V, X, NP, RO, EP = 1280, 256, 10, 4, 2
 Z = 2560
 WT = 2576
 DV = float(Z * 4097)
-SL = 2592
 BIG = float(2 ** 21)
 MAGIC = 12582912.0
 MID = 98304.0
-UP = [0, 10, 30, 50]
-CP = [20, 40, 60]
+C0 = 1280.3125
 NX = [10, 30, 50, 70]
 XO = [0, 10, 40, 90]
-KS = [0, 2, 5, 9]
+KS = [0, 10, 14, 17]
+TAIL = 3
+LEAD = [0, 13, 31, 38]
+GV = 384
 
-F, B16, I32, U16 = "float32", "bfloat16", "int32", "uint16"
+F, B16, I32, U16, H16 = "float32", "bfloat16", "int32", "uint16", "float16"
 SB_ = {
-    "W0": (WT, B16), "W1": (WT, B16), "H": (WT, B16), "ONES": (WT, B16), "LT": (WT, B16), "YW": (V, B16),
-    "KP": (WT, F), "WA": (2 * V + WT, I32), "WB": (WT, F), "CI": (V, F), "TL": (7 * SL, F),
-    "G0": (V + 32, F), "G1": (V + 32, F), "M": (4 * V, B16), "NF": (2 * V, F), "AA": (2048, B16),
+    "W0": (WT + V, B16), "W1": (WT + V, B16), "ONES": (WT, B16), "LT": (WT, B16), "YW": (V, B16), "RT": (V, B16),
+    "KP": (WT, F), "WA": (WT + V, I32), "K2": (V, I32), "WB": (WT, F), "CI": (V, F), "TL": (7 * V, F),
+    "G0": (V, F), "G1": (V, F), "M": (3 * V, B16), "MS": (2 * V, B16), "AA": (2048, B16),
     "SND": (320, F), "LAND": (1600, F), "E1": (72, F), "E2": (72, F), "E3": (144, F), "E4": (72, F), "US": (72, F),
-    "PEN": (72, F), "PEN0": (72, F), "MM": (64, F), "KT": (64, F), "T1": (64, F), "S1": (64, F),
-    "BI": (32, F), "BJ": (32, F), "C6": (32, F), "GG": (64, F), "D1": (64, F), "S2": (64, F), "OFF": (12, U16),
-    "PP": (80, I32), "LB": (80, I32), "BB": (400, I32), "LU": (400, U16), "DM": (80, F), "DZ": (80, F),
-    "DZB": (80, B16), "NEQ": (240, B16), "XU": (240, U16), "EQ": (240, B16), "SC": (320, F), "QQ": (16, F),
-    "SBP": (32, F), "SBP0": (32, F), "LC": (80, F), "EQH": (32, F), "EQL": (32, F),
+    "PEN": (72, F), "PEN0": (72, F), "NU": (24, F), "MM": (64, F), "KT": (64, F), "T1": (64, F), "S1": (64, F),
+    "BI": (64, F), "BJ": (64, F), "C6": (64, F), "GG": (64, F), "D1": (64, F), "S2": (64, F), "OFF": (12, U16),
+    "RL": (160, H16), "TM": (80, F), "DM": (80, H16), "EE": (768, H16), "LB": (80, F), "B0": (400, F), "B1": (400, F),
+    "LU": (400, U16), "LL": (80, U16), "DZ": (80, F), "DZB": (80, B16), "NEQ": (240, B16), "XU": (240, U16),
+    "EQ": (240, B16), "SC": (240, F), "SBP": (32, F), "SBP0": (32, F), "LC": (80, F), "EQH": (32, F), "EQL": (32, F),
     "NHT": (40, F), "HD": (40, F), "HS": (40, F), "HT": (24, F), "OFB": (6, U16), "CM": (16, F),
-    "GO": (80, F), "NG": (160, F), "DD": (160, F), "ML": (160, F), "MA": (160, F), "FL": (400, U16), "BS": (480, F),
-    "PI": (8, I32), "PF": (8, F), "PG": (8, F), "CC": (8, F), "J": (128, F), "JG": (128, F), "TH": (72, F),
-    "ID": (128, B16), "NEG": (128, B16), "BO": (128, B16), "M8": (240, F), "M16": (64, F),
-    "RF": (32, F), "REP": (16, U16), "BG": (2, U16), "GR": (4, U16), "TF": (24, F),
+    "XA": (240, F), "BF": (80, F), "FL": (160, U16), "BS": (160, F),
+    "PI": (8, I32), "PF": (8, F), "PG": (16, F), "CC": (8, F), "J": (128, F), "JG": (128, F), "TH": (72, F),
+    "ID": (128, B16), "NEG": (128, B16), "BO": (128, B16), "CS": (640, B16), "M8": (240, F), "M16": (64, F),
+    "RF": (32, F), "REP": (16, U16), "BG": (4, U16), "GR": (4, U16), "TF": (32, F),
 }
-PS_ = ["PU", "PL", "PC", "PD0", "PD1", "PD2", "PD3", "PD4"]
+PS_ = ["PU", "PC", "PR", "PL", "PD0", "PD1", "PD2", "PD3"]
 SCRATCH = {k: ("sbuf", [128, n], d) for k, (n, d) in SB_.items()}
 SCRATCH.update({k: ("psum", [128, 512], F) for k in PS_})
-SEMAPHORES = (["qv", "qs", "qp", "qg", "lw0", "lw1", "lk", "o0", "o1", "o2", "o3", "o4", "sent"]
+SEMAPHORES = (["qv", "qs", "qp", "qg", "lw0", "lw1", "lk0", "lk1", "lk2", "ck", "o0", "o1", "o2", "o3", "o4", "sent"]
               + ["ad%d" % i for i in range(10)] + ["af%d" % i for i in range(10)] + ["rl%d" % i for i in range(10)])
 
 
 def routes(T, topo):
     cores = list(T.cores)
-    near, help_ = [], []
+    near, help_ = [], ([], [])
     for s, c in enumerate(cores):
         near.append([r for r, d in enumerate(cores) if r != s and topo.may_write(c, d)])
         far = [r for r in range(len(cores)) if r != s and r not in near[s]]
-        hs = [h for h in topo.cores_of(c) if T.rank_of(h) is None and topo.die(h) == topo.die(c)
-              and all(topo.may_write(h, cores[r]) for r in far)][:max(1, min(2, len(far)))]
-        help_.append([(h, far[i::len(hs)]) for i, h in enumerate(hs)] if far else [])
+        able = [h for h in topo.cores_of(c) if T.rank_of(h) is None and all(topo.may_write(h, cores[r]) for r in far)]
+        for kind in range(2):
+            hs = [h for h in able if (topo.die(h) == topo.die(c)) == (kind == 0)][:max(1, min(2, len(far)))]
+            help_[kind].append([(h, far[i::len(hs)]) for i, h in enumerate(hs)] if far else [])
     return near, help_
 
 
@@ -87,14 +89,11 @@ def fan(g, T, topo, src_core, dsts, src, sem):
     return bin(mask).count("1")
 
 
-ORDER = [8, 0, 1, 2, 3, 9, 4, 5, 6, 7]
-
-
-def helper_program(g, core, T, topo, s, fars, near, help_):
+def helper_program(g, core, T, topo, s, fars, near, helpers, messages):
     cores = list(T.cores)
-    cnt = fan_count(topo, cores[s], [h for h, _ in help_[s]])
+    cnt = fan_count(topo, cores[s], [h for h, _ in helpers])
     sent = 0
-    for m in ORDER:
+    for m in messages:
         g.wait_ge(T.sem["rl%d" % m], cnt)
         src = message(T, m, s, s, near)[0]
         sent += fan(g, T, topo, core, [(cores[r], message(T, m, s, r, near)[1]) for r in fars], src, T.sem["af%d" % m])
@@ -105,10 +104,11 @@ def rank_program(g, core, T, topo):
     near, help_ = routes(T, topo)
     rank = T.rank_of(core)
     if rank is None:
-        for s in range(len(help_)):
-            for h, fars in help_[s]:
-                if h == core:
-                    helper_program(g, core, T, topo, s, fars, near, help_)
+        for kind, messages in enumerate([range(8), range(8, 10)]):
+            for s in range(len(near)):
+                for h, fars in help_[kind][s]:
+                    if h == core:
+                        helper_program(g, core, T, topo, s, fars, near, help_[kind][s], messages)
         return
     cores = list(T.cores)
     NR = len(cores)
@@ -117,7 +117,7 @@ def rank_program(g, core, T, topo):
     cnt_near = sum(fan_count(topo, cores[q], [cores[r] for r in near[q]]) for q in src_near)
     cnt_far = 0
     for q in src_far:
-        for h, fars in help_[q]:
+        for h, fars in help_[0][q]:
             if rank in fars:
                 cnt_far += fan_count(topo, h, [cores[r] for r in fars])
 
@@ -172,11 +172,14 @@ def rank_program(g, core, T, topo):
     def scan(o, d0, d1, op0, op1):
         add("v", [o], [d0, d1], lambda e: e.tensor_tensor_scan(o["ap"], d0["ap"], d1["ap"], 0.0, op0, op1))
 
+    def negsum(o, x):
+        add("v", [o], [x], lambda e: e.tensor_reduce(o["ap"], x["ap"], AX.X, OP.add, negate=True))
+
     def act(o, x, f=AF.Identity, bias=0.0, scale=1.0, acc=None):
         if acc is None:
             add("s", [o], [x], lambda e: e.activation(o["ap"], x["ap"], f, bias=bias, scale=scale))
         else:
-            add("s", [o, acc], [x], lambda e: e.activation(o["ap"], x["ap"], f, accum_out=acc["ap"]))
+            add("s", [o, acc], [x], lambda e: e.activation(o["ap"], x["ap"], f, scale=scale, accum_out=acc["ap"]))
 
     def mm(o, pairs, start=True, stop=True):
         def fn(e):
@@ -197,44 +200,62 @@ def rank_program(g, core, T, topo):
 
     sent = [0]
 
-    def send(m, src):
+    def send(m, src, to="hn"):
         def fn(e):
             ap = message(T, m, rank, rank, near)[0]
-            if help_[rank]:
-                sent[0] += fan(e, T, topo, core, [(h, ap) for h, _ in help_[rank]], ap, T.sem["rl%d" % m])
-            if near[rank]:
+            hs = help_[m // 8][rank]
+            if hs and "h" in to:
+                sent[0] += fan(e, T, topo, core, [(h, ap) for h, _ in hs], ap, T.sem["rl%d" % m])
+            if near[rank] and "n" in to:
                 sent[0] += fan(e, T, topo, core, [(cores[r], message(T, m, rank, r, near)[1]) for r in near[rank]],
                                ap, T.sem["ad%d" % m])
         add("g", [], [src], fn, "none")
 
     col = lambda name, j: a(name, j, j + 1)
-    v80 = a("BS", 0, 80)
+    v80, kv80 = a("BS", 0, 80), a("BS", 80, 160)
+    cs = lambda j: a("CS", 128 * j, 128 * j + 128)
+    half, quart, n8k, n24, cdv = [cs(j) for j in range(5)]
+    ee = lambda j: a("EE", 128 * j, 128 * j + 128)
+    thirds = [(0, 512), (512, 1024), (1024, V)]
 
-    def colsum(src, lo, npat, ps, po):
-        mm(a(ps, po, po + 8 * npat), [(a("ID"), a(src, lo + i, lo + 128 * npat, 16)) for i in range(16)])
+    def colsum(src, lo, npat, po, j):
+        mm(a("PU", po, po + 8 * npat), [(a("ID"), a(src, lo + i, lo + 128 * npat, 16)) for i in range(4 * j, 4 * j + 4)],
+           j == 0, j == 3)
 
-    def finish(ps, lo, hi, so, dst):
-        scan(a("SC", so + lo, so + hi), a("M8", 0, hi - lo), a(ps, lo, hi), OP.mult, OP.add)
-        for d, n, p in dst:
-            cp(a("SND", d, d + n), a("SC", so + p + 7, so + p + 8 * n, 8))
+    def finish(npat, dst):
+        scan(a("SC", 0, 8 * npat), a("M8", 0, 8 * npat), a("PU", 0, 8 * npat), OP.mult, OP.add)
+        ts(a("SND", dst, dst + npat), a("SC", 7, 8 * npat, 8), -1.0, OP.mult)
 
-    def own_votes(w, dst):
-        colsum(w, 0, 6, "PL", 0)
+    def absent(ps, w, lo, hi):
+        mm(a(ps, 0, hi - lo), [(cdv, a("ONES", 0, hi - lo)), (n24, a(w, lo, hi))])
 
-        def rest(k):
-            act(a("M", 128 * k, 128 * k + 128), a(w, 128 * k, 128 * k + 128), acc=col("SND", dst + k))
-        return rest
+    def chunks_of(ks):
+        out = []
+        for h0 in range(0, ks, NP):
+            w_ = min(NP, ks - h0)
+            nch = (w_ + 3) // 4
+            out += [(h0 + w_ * i // nch, h0 + w_ * (i + 1) // nch) for i in range(nch)]
+        return out
+
+    def roots(w, i, k0, k1):
+        r0 = 128 * (k0 % NP)
+        mm(a("PD%d" % (i % 4), 0, 128 * (k1 - k0)), [(a("ID"), a(w, r0, r0 + 128 * (k1 - k0)))], True, False)
+
+    def roots_ahead(w, t):
+        for i, (k0, k1) in enumerate(chunks_of(KS[t])[:4]):
+            roots(w, i, k0, k1)
 
     dma("y", [a("W0", 0, X)], [], T.W0[:, 0:X], T.w[:, 0:X], "lw0")
     dma("s", [a("W0", X, V)], [], T.W0[:, X:V], T.w[:, X:V], "lw1")
-    dma("y", [a("WA", 0, V)], [], T.WA[:, 0:V], T.kids[:, 0:V], "lk")
+    for i, (lo, hi) in enumerate(thirds):
+        dma("y", [a("WA", WT + lo, WT + hi)], [], T.WA[:, WT + lo:WT + hi], T.kids[:, lo:hi], "lk%d" % i)
     iota(col("PI", 0), [[0, 1]], 0, 1, False)
     iota(a("J"), [[1, 128]])
     iota(a("TH", 0, 65), [[0, 13], [1, 5]])
-    iota(a("SBP0", 0, 25), [[256, 5], [-(2 * SL - 16), 5]], 3 * (2 * SL - 16) + 63)
-    iota(a("LC", 0, 75), [[2 * SL, 3], [256, 5], [16, 5]], SL + 15)
+    iota(a("SBP0", 0, 25), [[256, 5], [-(2 * V - 16), 5]], 3 * (2 * V - 16) + 63, 16)
+    iota(a("LC", 0, 75), [[2 * V, 3], [256, 5], [16, 5]], V + 15, 16)
     iota(a("RF", 0, 15), [[0, 3], [16, 5]])
-    send(8, a("W0", 0, X))
+    send(8, a("W0", 0, X), "h")
     ms(a("M8"), 1.0)
     ms(a("M16"), 0.0)
     ms(a("KT"), 0.0)
@@ -245,89 +266,125 @@ def rank_program(g, core, T, topo):
     ts(col("PI", 4), p0, 4, OP.arith_shift_right, 1, OP.bitwise_and)
     ts(col("PI", 5), p0, 1, OP.bitwise_and)
     ms(a("M8", 0, 240, 8), 0.0)
-    ms(a("M16", 0, 64, 16), -1e9)
+    ms(a("M16", 0, 64, 16), 1e9)
     cp(a("PF", 0, 6), a("PI", 0, 6))
-    ms(a("D1"), 80.0)
-    ms(a("PEN0"), -2.0 ** 18)
-    pa, phi = col("PF", 1), col("PF", 3)
-    ts(a("ID"), a("J"), col("PF", 0), OP.is_equal)
-    tt(col("PG", 0), col("PF", 4), col("PF", 5), OP.not_equal)
-    ts(col("PG", 1), pa, 16.0, OP.mult)
+    ms(a("D1"), -80.0)
+    ms(a("PEN0"), 2.0 ** 18)
+    pp, pa, pg, phi, hi_, odd = [col("PF", j) for j in range(6)]
+    ts(a("ID"), a("J"), pp, OP.is_equal)
+    ts(col("PG", 0), hi_, -32.0, OP.mult, 16.0, OP.add)
+    ts(col("PG", 1), pg, -256.0, OP.mult)
     ts(col("PG", 2), phi, -1.0, OP.mult, 1.0, OP.add)
-    ts(a("TF", 0, 4), a("J", 0, 4), -16.0, OP.mult, 31.5 - 64 * MID, OP.add)
+    ts(col("PG", 3), hi_, -1.0, OP.mult, 1.0, OP.add)
+    ts(col("PG", 4), phi, 32.0, OP.mult, 15.0, OP.add)
+    ts(a("TF", 0, 4), a("J", 0, 4), 16.0, OP.mult, 64 * MID - 31.5, OP.add)
     ts(v80, a("J", 0, 80), 16.0, OP.mult, pa, OP.add)
-    ts(col("PG", 3), col("PG", 0), 1296.0, OP.mult, col("PG", 1), OP.add)
-    ts(a("CC", 0, 4), a("TF", 0, 4), pa, OP.subtract, 1.0 / 64, OP.mult)
-    ts(a("TF", 4, 6), a("J", 0, 2), 16.0, OP.mult, 15.0, OP.add)
-    ts(col("PG", 4), phi, 32.0, OP.mult)
+    tt(col("PG", 5), col("PG", 0), pp, OP.add)
+    ts(a("CC", 0, 4), a("TF", 0, 4), pa, OP.add, 1.0 / 64, OP.mult)
+    ts(a("TF", 4, 6), a("J", 0, 2), 0.0, OP.mult, odd, OP.add)
+    cp(a("TF", 6, 8), a("J", 0, 2))
     ts(a("TF", 16, 20), a("BS", 0, 4), -2.0, OP.add, 0.2, OP.mult)
-    ts(a("REP", 0, 15), a("RF", 0, 15), pa, OP.add)
-    ts(a("SBP0", 0, 25), a("SBP0", 0, 25), col("PG", 3), OP.add)
+    ts(a("SBP0", 0, 25), a("SBP0", 0, 25), col("PG", 1), OP.add)
+    ts(a("BG"), a("TF", 4, 8), 16.0, OP.mult, col("PG", 4), OP.add)
     whole(a("TF", 20, 24), a("TF", 16, 20))
-    ts(a("LC", 0, 75), a("LC", 0, 75), col("PG", 3), OP.add)
-    ts(a("BG"), a("TF", 4, 6), col("PG", 4), OP.add)
-    ts(a("TF", 8, 12), a("TF", 20, 24), 6.0, OP.is_ge, -6.0, OP.mult)
     for h in range(4):
-        ts(a("PEN0", UP[h], UP[h] + 10), a("J", 0, 10), 0.0, OP.mult, col("CC", h), OP.add)
-    cp(a("D1", 33, 54, 5), a("BS", 0, 5))
-    ms(a("D1", 34, 55, 5), 0.0)
+        ts(a("PEN0", 30 - 10 * h, 40 - 10 * h), a("J", 0, 10), 0.0, OP.mult, col("CC", h), OP.add)
     ms(a("SBP0", 4, 25, 5), 0.0)
-    tt(a("TF", 12, 16), a("TF", 8, 12), a("TF", 20, 24), OP.add)
-    ts(a("TH", 0, 65), a("TH", 0, 65), 0.25, OP.mult, -0.5, OP.add)
-    ts(a("NEG"), a("J"), col("PF", 0), OP.is_equal, -1.0, OP.mult)
-    for w in ("W0", "W1", "H", "ONES"):
-        ms(a(w, Z, WT), 0.0)
-    ms(a("KP", Z, WT), DV)
-    cp(a("GR"), a("TF", 12, 16))
-    for gname in ("G0", "G1"):
-        ms(a(gname, 0, 16), 0.0)
-        ms(a(gname, V + 16, V + 32), 0.0)
-    rest = own_votes("W0", 0)
-    for k in range(6, NP):
-        rest(k)
-    finish("PL", 0, 48, 240, [(0, 6, 0)])
+    ts(a("TF", 8, 12), a("TF", 20, 24), 6.0, OP.is_ge, 26.0, OP.mult)
+    for j, (tgt, msk) in enumerate([(pp, col("PG", 3)), (col("PG", 5), col("PG", 3)), (col("PG", 5), hi_), (pp, hi_)]):
+        ts(ee(j), a("J"), tgt, OP.is_equal, msk, OP.mult)
+    for k in range(NP):
+        own = a("W0", 128 * k, 128 * k + 128)
+        if k in (0, 1, 4, 6, 8):
+            act(a("M", 128 * k, 128 * k + 128), own, scale=-1.0, acc=col("SND", k))
+        else:
+            negsum(col("SND", k), own)
     send(0, a("SND", 0, 10))
-    iota(a("CI"), [[4097, V]], V * 4097)
+    send(8, a("W0", 0, X), "n")
     iota(a("JG"), [[1, 8], [0, 16]])
-    ts(a("BS", 80, 160), v80, -float(V), OP.add)
-    cp(a("BS", 160, 240), v80)
-    ms(a("BS", 240, 320), 0.0)
-    ts(a("BS", 320, 400), v80, float(WT), OP.add)
-    ms(a("BS", 400, 480), 0.0)
-    ms(a("NHT"), 0.0)
-    ms(a("HD"), 80.0)
-    ts(a("HD", 3, 40, 8), a("J", 0, 5), 16.0, OP.mult, 80.0, OP.add)
-    ts(a("HD", 7, 40, 8), a("J", 0, 5), 16.0, OP.mult, 80.0, OP.add)
+    iota(a("CI"), [[4097, V]], V * 4097)
+    ts(ee(4), a("J"), pp, OP.is_equal)
+    ts(ee(5), a("J"), pp, OP.is_equal, 4096.0, OP.mult)
+    ts(a("NEG"), a("ID"), -1.0, OP.mult)
+    ms(a("KP", Z, WT), DV)
+    ms(a("W0", Z, WT), 0.0)
+    for i, (lo, hi) in enumerate(thirds):
+        act(a("PD%d" % i, 0, hi - lo), a("W0", lo, hi), AF.Relu, bias=DV, scale=-DV)
+    act(a("ONES", 0, V), a("W0", 0, V), bias=1.0, scale=0.0)
 
-    def turn(src, slot):
-        tr(a("TL", slot * SL, slot * SL + V), a(src, 16, 16 + V))
-        tr(a("TL", slot * SL + V, (slot + 1) * SL), a(src))
+    def late_constants():
+        tt(a("TF", 12, 16), a("TF", 8, 12), a("TF", 20, 24), OP.add)
+        ts(a("REP", 0, 15), a("RF", 0, 15), pa, OP.add)
+        ts(a("LC", 0, 75), a("LC", 0, 75), col("PG", 1), OP.add)
+        ts(a("TH", 0, 65), a("TH", 0, 65), -0.25, OP.mult, 0.5, OP.add)
+        cp(a("GR"), a("TF", 12, 16))
+        ts(a("TF", 24, 29), a("SBP0", 3, 25, 5), -31.5, OP.add, 1.0 / 64, OP.mult)
+        ms(a("NHT"), 0.0)
+        ts(a("D1", 33, 54, 5), a("BS", 0, 5), 320.0, OP.add)
+        ms(a("D1", 34, 55, 5), 0.0)
+        ts(col("PG", 6), pp, 0.0, OP.is_equal, 4096.0 * Z, OP.mult)
+        ts(col("PG", 7), pp, 1.0, OP.is_equal, float(Z), OP.mult)
+        ts(n24, a("ID"), -2.0 ** 24, OP.mult)
+        tt(col("PG", 8), col("PG", 6), col("PG", 7), OP.add)
+        ts(a("BO"), a("JG"), pg, OP.is_equal, -2.0 ** 19, OP.mult)
+        ts(cdv, a("J"), 0.0, OP.mult, col("PG", 8), OP.add)
+
+    def end_constants():
+        ts(kv80, v80, float(WT), OP.add)
+        ms(a("HD"), -80.0)
+        for w in ("W1", "ONES"):
+            ms(a(w, Z, WT), 0.0)
+        ts(half, a("ID"), 0.5, OP.mult)
+        ts(quart, a("ID"), -0.25, OP.mult)
+        ts(n8k, a("ID"), -8192.0, OP.mult)
+        ts(a("HD", 3, 40, 8), a("J", 0, 5), 16.0, OP.mult, 240.0, OP.add)
+        ts(a("HD", 7, 40, 8), a("J", 0, 5), 16.0, OP.mult, 240.0, OP.add)
+        ms(a("WB", Z, WT), 0.0)
+
+    def dead_term():
+        mm(a("PR", 0, 80), [(ee(5), a("DM"))], True, False)
+        mm(a("PL", 0, 80), [(ee(4), a("DM"))], True, False)
+
+    def swap(ps, lo):
+        for par in range(2):
+            mm(a(ps, par, 80, 2), [(ee(2 * par + q), a("RL", lo + q, lo + 80, 2)) for q in range(2)], False, par == 1)
 
     for e in range(EP):
         W = "W%d" % e
-        Wt = a(W)
-        ko = 0 if e == 0 else V + WT
+        Wt = a(W, 0, WT)
+        kin = "WA" if e == 0 else "K2"
+        ko = WT if e == 0 else 0
         cp(a("SBP", 0, 25), a("SBP0", 0, 25))
         cp(a("PEN", 0, 70), a("PEN0", 0, 70))
-        tt(a("E1", 0, 10), a("SND", 160 * e, 160 * e + 10), a("PEN0", 0, 10), OP.add)
-        for i, (lo, hi) in enumerate([(0, 512), (512, 1024), (1024, V)]):
-            act(a("PD%d" % i, 0, hi - lo), a(W, lo, hi), AF.Relu, bias=DV, scale=-DV)
-            tt(a("G0", 16 + lo, 16 + hi), a("WA", ko + lo, ko + hi), a("PD%d" % i, 0, hi - lo), OP.max)
-        if e == 0:
-            act(a("NF", V, 2 * V), a(W, 0, V))
-        turn("G0", 0)
-        if e == 0:
-            ts(a("BO"), a("JG"), col("PF", 2), OP.is_equal, 2.0 ** 19, OP.mult)
+        ts(a("DM"), a("J", 0, 80), 0.0, OP.mult, 0.3125, OP.add)
+        tt(a("E1", 0, 10), a("SND", 160 * e, 160 * e + 10), a("PEN0", 30, 40), OP.add)
+        if e > 0:
+            for lo, hi in thirds:
+                act(a("G1", lo, hi), ind(a("WB"), a("FL", 80 + lo // 16, 80 + hi // 16)))
+        for i, (lo, hi) in enumerate(thirds):
+            if e > 0:
+                absent("PD%d" % i, W, lo, hi)
+                tt(a("K2", lo, hi), ind(a("WA"), a("FL", lo // 16, hi // 16)), a("G1", lo, hi), OP.add)
+            tt(a("KP", lo, hi), a(kin, ko + lo, ko + hi), a("PD%d" % i, 0, hi - lo), OP.max)
+            act(a("G0", lo, hi), a("KP", lo, hi), bias=-C0, scale=1.0 / 4096)
+            if e == 0 and i == 0:
+                late_constants()
+            if i:
+                tr(a("TL", *thirds[i - 1]), a("G0", *thirds[i - 1]))
+        tr(a("TL", *thirds[2]), a("G0", *thirds[2]))
+        dead_term()
+        roots_ahead(W, 1)
+        if e > 0:
+            dma("y", [a("WA", WT, WT + V)], [a("K2")], T.WA[:, WT:WT + V], T.K2[:, 0:V], "ck")
+        else:
+            act(a("ONES", V, Z), a("W0", 0, V), bias=1.0, scale=0.0)
+            act(a("B0"), a("W0", 0, 400), scale=0.0)
+            act(a("B1"), a("W0", 0, 400), scale=0.0)
+        act(a("RT"), a(W, 0, V))
+        act(a(W, WT, WT + V), a(W, 0, V), scale=2.0)
         gh = lambda q: ((rank - q) % NR - 1) * X
         arrive([a(W, V + gh(q), V + gh(q) + X) for q in src_near], "ad%d" % (8 + e), cnt_near)
         arrive([a(W, V + gh(q), V + gh(q) + X) for q in src_far], "af%d" % (8 + e), cnt_far)
-        for i, q in enumerate(src_near + src_far):
-            pd = a("PD%d" % ((i + 3) % 5), 0, X)
-            act(pd, a(W, V + gh(q), V + gh(q) + X), AF.Relu, bias=DV, scale=-DV)
-            tt(a("KP", V + gh(q), V + gh(q) + X), a("CI", gh(q), gh(q) + X), pd, OP.max)
-        if e > 0:
-            act(a("NF", V, 2 * V), a(W, 0, V))
-        act(a("KP", 0, V), a("G0", 16, 16 + V))
 
         for t in range(1, RO + 1):
             m = RO * e + t - 1
@@ -354,256 +411,307 @@ def rank_program(g, core, T, topo):
             if len(parts) == 2:
                 tt(e4, parts[0], parts[1], OP.add)
                 parts = [e4]
-            u = lambda h: a("US", UP[h], UP[h] + 10)
-            c = lambda h: a("US", CP[h], CP[h] + 10)
+            u = lambda h: a("US", 10 * (t - 1 - h), 10 * (t - h))
+            c = lambda i: a("US", 10 * (t + i), 10 * (t + i + 1))
             mmx = lambda j: a("MM", 10 * j, 10 * j + 10)
             kt = lambda par: a("KT", 32 * par, 32 * par + 5)
-            if t == 1 and len(parts) == 1:
+            first = (acc, parts[0])
+            if t == 1:
                 an, pn = acc["r"][0][0], parts[0]["r"][0]
                 for par in range(2):
                     tt(kt(par), a(an, par, 10, 2), a(pn[0], pn[1] + par, pn[1] + 10, 2), OP.add)
             else:
-                for k, p in enumerate(parts):
-                    nxt = us if k == len(parts) - 1 else (e2 if acc is e1 else e1)
-                    tt(nxt, acc, p, OP.add)
-                    acc = nxt
-                if not parts:
-                    cp(us, acc)
-                if t == 1:
-                    xs = ("US", 0)
-                    cp(mmx(0), u(0))
-                elif t == 2:
-                    tt(mmx(0), u(1), c(0), OP.min)
-                    xs = ("US", 0)
+                tt(us, acc, parts[0], OP.add)
+                if t == 2:
+                    tt(mmx(0), u(1), c(0), OP.max)
+                    xs = ("US", 10)
                 elif t == 3:
-                    tt(mmx(1), c(0), c(1), OP.min)
-                    tt(mmx(2), u(0), u(1), OP.max)
-                    tt(mmx(0), u(2), mmx(1), OP.min)
+                    tt(mmx(1), c(0), c(1), OP.max)
+                    tt(mmx(2), u(0), u(1), OP.min)
+                    tt(mmx(0), u(2), mmx(1), OP.max)
                     xs = ("MM", 20)
                 else:
-                    tt(mmx(1), c(0), c(1), OP.min)
-                    tt(mmx(3), u(3), c(2), OP.min)
-                    tt(mmx(2), u(0), u(1), OP.max)
-                    tt(mmx(0), mmx(1), mmx(3), OP.min)
-                    tt(mmx(4), mmx(2), u(2), OP.max)
+                    tt(mmx(1), c(0), c(1), OP.max)
+                    tt(mmx(3), u(3), c(2), OP.max)
+                    tt(mmx(2), u(0), u(1), OP.min)
+                    tt(mmx(0), mmx(1), mmx(3), OP.max)
+                    tt(mmx(4), mmx(2), u(2), OP.min)
                     xs = ("MM", 40)
                 for par in range(2):
-                    tt(kt(par), a(xs[0], xs[1] + par, xs[1] + 10, 2), a("MM", par, 10, 2), OP.max)
+                    tt(kt(par), a(xs[0], xs[1] + par, xs[1] + 10, 2), a("MM", par, 10, 2), OP.min)
+            def dropped():
+                ts(a("NHT", 5 - t, 40, 4), c(0) if t == 2 else mmx(1) if t == 3 else a("CM", 0, 10), 0.0, OP.is_gt)
+
+            fill = [lambda: tt(a("CM", 0, 10), mmx(1), c(2), OP.max), dropped,
+                    lambda: scan(a("HS"), a("NHT"), a("HD"), OP.mult, OP.add),
+                    lambda: ts(a("HT", 0, 5), a("HS", 3, 40, 8), col("PG", 2), OP.mult, pa, OP.add),
+                    lambda: ts(a("HT", 8, 13), a("HS", 7, 40, 8), phi, OP.mult),
+                    lambda: tt(a("HT", 16, 21), a("HT", 0, 5), a("HT", 8, 13), OP.add),
+                    lambda: cp(a("OFB", 0, 5), a("HT", 16, 21))] if t == RO else []
+
+            def between():
+                if fill:
+                    fill.pop(0)()
+
+            between()
             tr(a("T1"), a("KT"))
-            scan(a("S1"), a("M16"), a("T1"), OP.add, OP.max)
-            best = ind(a("S1"), a("BG"))
-            whole(a("BI"), best)
-            tt(a("BJ"), best, a("BI"), OP.subtract)
-            tr(a("C6"), a("BJ"))
-            code = lambda o: ts(o, a("C6", 0, 5), -64.0, OP.mult, -31.5, OP.add)
+            between()
+            scan(a("S1"), a("M16"), a("T1"), OP.add, OP.min)
+            between()
+            nb = 32 if t == 1 else 64
+            best = ind(a("S1"), a("BG", 0, nb // 16))
+            whole(a("BI", 0, nb), best)
+            between()
+            tt(a("BJ", 0, nb), best, a("BI", 0, nb), OP.subtract)
+            between()
+            tr(a("C6", 0, nb), a("BJ", 0, nb))
+            between()
             if t == 1:
-                code(a("S2", 0, 5))
-                tt(a("S2", 8, 13), a("S2", 0, 5), a("SBP0", 3, 25, 5), OP.add)
-                cp(a("OFF", 0, 5), a("S2", 8, 13))
+                tt(a("S2", 0, 5), a("C6", 0, 5), a("TF", 24, 29), OP.add)
+                ts(a("OFF", 0, 5), a("S2", 0, 5), 64.0, OP.mult)
             else:
-                tt(a("GG"), ind(a("C6"), a("GR")), a("TH", 0, 64), OP.is_lt)
-                code(a("D1", 4, 25, 5))
+                tt(a("GG"), ind(a("C6"), a("GR")), a("TH", 0, 64), OP.is_gt)
+                ts(a("D1", 4, 25, 5), a("C6", 0, 5), 64.0, OP.mult, -31.5, OP.add)
                 scan(a("S2", 0, 55), a("GG", 0, 55), a("D1", 0, 55), OP.mult, OP.add)
+                between()
                 cp(a("OFF", 0, 11), a("S2", 4, 55, 5))
             off, offx = a("OFF", 0, 5), a("OFF", 6, 11)
-            tl = a("TL", 0, (2 * t - 1) * SL)
-            bold = a("BB", 0, 80 * t)
-            bt = a("BB", 80 * t, 80 * t + 80)
-            lu = lambda h, c0=0, c1=80: a("LU", 80 + 80 * h + c0, 80 + 80 * h + c1)
-            if t == 1:
-                cp(a("PP"), ind(tl, off))
-                ts(bt, a("PP"), 12, OP.arith_shift_right)
-                ts(bold, a("PP"), 4095, OP.bitwise_and)
-                cp(a("LU", 80, 240), a("BB", 0, 160))
-                llist = lu(0)
+            tl = a("TL", 0, (2 * t - 1) * V)
+            old, new = ("B1", "B0") if t % 2 == 0 else ("B0", "B1")
+            if t == RO:
+                new = old
+            hp = lambda h: 80 * (RO - h)
+            lu = lambda c0, c1: a("LU", hp(t) + c0, hp(t) + c1)
+            rr, ll = a("RL", 0, 80), a("RL", 80, 160)
+            pr, pl = a("PR", 0, 80), a("PL", 0, 80)
+            src = ind(tl, off)
+            if t < RO:
+                whole(rr, src)
+                swap("PR", 0)
+                tt(ll, src, rr, OP.subtract)
+                swap("PL", 80)
+                ts(lu(0, 80), pr, float(Z), OP.min)
             else:
-                tt(a("PP"), ind(tl, off), a("DM"), OP.max)
-                cp(a("XU", 80 * (t - 2), 80 * (t - 1)), ind(bold, offx))
-                llist = a("LU", 0, 80)
-                if t < RO:
-                    ts(bt, a("PP"), 12, OP.arith_shift_right)
-                    ts(a("LB"), a("PP"), 4095, OP.bitwise_and)
-                    cp(lu(t), bt)
-                else:
-                    ts(a("LB"), a("PP"), 4095, OP.bitwise_and)
-                    ts(bt, a("PP"), 12, OP.arith_shift_right)
-                    cp(llist, a("LB"))
-                tt(a("EQ", 80 * (t - 2), 80 * (t - 1)), ind(bold, offx), v80, OP.is_equal)
+                whole(rr, src)
+                tt(ll, src, rr, OP.subtract)
+                swap("PL", 80)
+                swap("PR", 0)
 
-            def dropped():
-                cm = c(0) if t == 2 else mmx(1)
-                if t == 4:
-                    cm = a("CM", 0, 10)
-                    tt(cm, mmx(1), c(2), OP.min)
-                ts(a("NHT", 5 - t, 40, 4), cm, 0.0, OP.is_lt)
+            def expanded():
+                cp(a("XU", 80 * (t - 2), 80 * (t - 1)), ind(a(old), offx))
+                tt(a("EQ", 80 * (t - 2), 80 * (t - 1)), ind(a(old), offx), v80, OP.is_equal)
 
             if t < RO:
                 so = 160 * e + XO[t]
-                order = [t] + list(range(t))
-                ks = KS[t]
-
-                def gm(i, k0, k1):
-                    tt(a("M", V * i + 128 * k0, V * i + 128 * k1), ind(Wt, lu(order[i], 8 * k0, 8 * k1)),
-                       a("NF", V + 128 * k0, V + 128 * k1), OP.min)
-
-                nch = (ks + 3) // 4
-                chunks = [(ks * i // nch, ks * (i + 1) // nch) for i in range(nch)]
-                for i, (k0, k1) in enumerate(chunks):
-                    mk = a("M", 128 * k0, 128 * k1)
-                    act(mk, ind(Wt, lu(t, 8 * k0, 8 * k1)))
-                    mm(a("PD%d" % i, 0, 128 * (k1 - k0)), [(a("ID"), a(W, 128 * k0, 128 * k1)), (a("NEG"), mk)])
-                for i, (k0, k1) in enumerate(chunks):
-                    for k in range(k0, k1):
-                        act(a("M", 128 * k, 128 * k + 128), a("PD%d" % i, 128 * (k - k0), 128 * (k - k0 + 1)),
-                            AF.Relu, acc=col("QQ", k))
+                nu, ks = 10 * (t + 1), KS[t]
+                bt, bold = a(new, hp(t), hp(t) + 80), a(new, hp(t - 1), 400)
                 rep = a("REP", 0, 5 * t)
-                if t > 1:
-                    cp(ind(bold, offx), a("LB"))
-                    ts(a("DZ"), a("PP"), DV, OP.is_ge, float(Z), OP.mult)
-                    gm(0, ks, NP)
-                    tt(bold, ind(a("DZ"), rep), bold, OP.max)
-                    cp(llist, a("LB"))
-                    cp(a("LU", 80, 80 + 80 * t), bold)
-                    tt(a("NEQ", 0, 80 * t), ind(bt, rep), bold, OP.not_equal)
-                else:
+                if t == 1:
+                    ts(lu(80, 160), pl, 4096.0, OP.mult, float(Z), OP.min)
+                    cp(a(new, hp(1), 400), lu(0, 160))
                     tt(a("NEQ", 0, 80), bt, bold, OP.not_equal)
-                    gm(0, ks, NP)
-                mm(a("PC", 0, 10 * t), [(a("BO"), a("NEQ", b, 80 * t, 8)) for b in range(8)])
-                colsum("M", 128 * ks, NP - ks, "PU", 8 * ks)
-                act(a("G0", 16, 16 + V), ind(a("KP"), lu(t)))
-                for h in range(t):
-                    act(a("SND", so + CP[h], so + CP[h] + 10), a("PC", 10 * h, 10 * h + 10))
-                for i in range(1, t):
-                    gm(i, 0, NP)
-                    colsum("M", V * i, NP, "PU", 80 * i)
-                gm(t, 0, 7)
-                colsum("M", V * t, 7, "PL", 0)
-                gm(t, 7, NP)
-                for k in range(7, NP):
-                    x = a("M", V * t + 128 * k, V * t + 128 * k + 128)
-                    act(x, x, acc=col("SND", so + UP[order[t]] + k))
-                if ks:
-                    tt(a("SND", so + UP[t], so + UP[t] + ks), a("SND", 160 * e, 160 * e + ks), a("QQ", 0, ks), OP.subtract)
-                finish("PU", 8 * ks, 80 * t, 0,
-                       [(so + UP[t] + ks, NP - ks, 8 * ks)] + [(so + UP[order[i]], 10, 80 * i) for i in range(1, t)])
-                finish("PL", 0, 56, 240, [(so + UP[order[t]], 7, 0)])
+                else:
+                    ts(a("LB"), pl, 4096.0, OP.mult, float(Z), OP.min)
+                    ts(a("DZ"), pr, float(Z), OP.is_ge, float(Z), OP.mult)
+                    ts(bt, pr, float(Z), OP.min)
+                    tt(bold, ind(a("DZ"), rep), a(old, hp(t - 1), 400), OP.max)
+                    cp(ind(a(new), offx), a("LB"))
+                    cp(lu(80, 80 + 80 * t), bold)
+                    tt(a("NEQ", 0, 80 * t), ind(bt, rep), bold, OP.not_equal)
+                chunks = chunks_of(ks)
+
+                def short(i):
+                    k0, k1 = chunks[i]
+                    for k in range(k0, k1):
+                        act(a("MS", 128 * k, 128 * k + 128), a("PD%d" % (i % 4), 128 * (k - k0), 128 * (k - k0 + 1)),
+                            AF.Relu, acc=col("SND", so + k))
+
+                def scalar_part(i):
+                    k0, k1 = chunks[i]
+                    mk = a("MS", 128 * k0, 128 * k1)
+                    act(mk, ind(Wt, lu(8 * k0, 8 * k1)))
+                    if i >= 4:
+                        roots(W, i, k0, k1)
+                    mm(a("PD%d" % (i % 4), 0, 128 * (k1 - k0)), [(a("NEG"), mk)], False, True)
+                    if i == 1:
+                        mm(a("PC", 0, 10 * t), [(a("BO"), a("NEQ", b, 80 * t, 8)) for b in range(8)])
+                    if i:
+                        short(i - 1)
+                    if i == len(chunks) - 1:
+                        act(a("SND", so + nu, so + nu + 10 * t), a("PC", 0, 10 * t))
+                        short(i)
+
+                def vector_part(k0, k1):
+                    r0 = 128 * (k0 % NP)
+                    tt(a("M", 128 * (k0 - ks), 128 * (k1 - ks)), ind(Wt, lu(8 * k0, 8 * k1)),
+                       a("RT", r0, r0 + 128 * (k1 - k0)), OP.min)
+
+                mid = (ks + nu - TAIL + 1) // 2 if nu - TAIL - ks >= 14 else ks
+                cuts = sorted(set([ks, mid, nu - TAIL, nu] + [x for x in range(0, nu, NP) if x > ks]))
+                steps = [(4 * k1 + 3 * (chunks[i - 1][0] if i else 0), 0, i) for i, (k0, k1) in enumerate(chunks)]
+                steps += [(LEAD[t] + 4 * (k1 - ks), 1, (k0, k1)) for k0, k1 in zip(cuts, cuts[1:])]
+                for k0, k1 in [(ks, mid), (mid, nu - TAIL)]:
+                    if k1 > k0:
+                        steps += [(LEAD[t] + 4 * (k1 - ks) + 5 * j, 2, (k0, k1, j)) for j in range(4)]
+                for _, kind, x in sorted(steps):
+                    if kind == 2:
+                        colsum("M", 128 * (x[0] - ks), x[1] - x[0], 8 * (x[0] - ks), x[2])
+                    elif kind:
+                        vector_part(*x)
+                    else:
+                        scalar_part(x)
+                for k in range(nu - TAIL, nu):
+                    negsum(col("SND", so + k), a("M", 128 * (k - ks), 128 * (k - ks + 1)))
+                finish(nu - TAIL - ks, so + ks)
+                if t == 1:
+                    for i, (lo2, hi2) in enumerate(thirds):
+                        ps = ["PR", "PL", "PD0"][i]
+                        absent(ps, W, V + lo2, V + hi2)
+                        tt(a("KP", V + lo2, V + hi2), a("CI", lo2, hi2), a(ps, 0, hi2 - lo2), OP.max)
                 send(m + 1, a("SND", so, so + NX[t]))
-                act(a("G1", 16, 16 + V), ind(a("KP"), llist))
+                if t == 1:
+                    llist = lambda c0, c1: lu(80 + c0, 80 + c1)
+                else:
+                    cp(a("LL"), a("LB"))
+                    llist = lambda c0, c1: a("LL", c0, c1)
+                for lo2, hi2 in [(0, 640), (640, V)]:
+                    act(a("G0", lo2, hi2), ind(a("KP"), lu(lo2 // 16, hi2 // 16)), bias=-C0, scale=1.0 / 4096)
+                for lo2, hi2 in [(GV, 896), (896, V)]:
+                    act(a("G1", lo2, hi2), ind(a("KP"), llist(lo2 // 16, hi2 // 16)), bias=-C0, scale=1.0 / 4096)
                 if e == 0:
                     if t == 1:
-                        iota(a("WA", V, V + WT), [[1, WT]], 0, 0, False)
-                        act(a("ONES", 0, Z), a(W, 0, Z), bias=1.0, scale=0.0)
-                        act(a("LT", V, WT), a(W, V, WT), scale=0.0)
+                        iota(a("WA", 0, WT), [[1, WT]], 0, 0, False)
                     elif t == 2:
                         add("g", [a("AA")], [a("ONES", 0, 2048)],
                             lambda en: en.affine_select(T.AA[:, 0:2048], T.ONES[:, 0:2048], [[-1000, 16], [-16, 8], [999, 16]],
                                                         OP.is_equal, 0.0, 0, 1))
                     else:
-                        iota(a("WB"), [[4096, WT]])
-                if t == 2:
-                    act(a("H", 0, Z), a(W, 0, Z), scale=0.5)
-                ts(a("DM"), a("PP"), DV, OP.is_ge, DV, OP.mult)
+                        iota(a("WB", 0, Z), [[4096, Z]])
+                        act(a("LT", V, WT), a(W, V, WT), scale=0.0)
+                ts(a("G1", 0, GV), ind(a("KP"), llist(0, GV // 16)), 1.0 / 4096, OP.mult, -C0, OP.add)
+                ts(a("DM"), bt, float(Z), OP.is_ge, 0.3125, OP.add)
                 if t > 1:
                     tt(a("EQH", 0, 25), a("GG", 1, 26), a("GG", 0, 25), OP.subtract)
                     dropped()
                     tt(a("EQL", 0, 25), a("EQH", 0, 25), a("LC", 25 * (t - 1), 25 * t), OP.mult)
+                    expanded()
                 else:
                     cp(a("SBP", 3, 25, 5), a("LC", 3, 25, 5))
-                tr(a("TL", 2 * t * SL, 2 * t * SL + V), a("G0", 16, 16 + V))
+                    tt(a("US", 0, 10), first[0]["r"] and a(first[0]["r"][0][0], 0, 10), first[1], OP.add)
+                dead_term()
+                if t + 1 < RO:
+                    roots_ahead(W, t + 1)
+                else:
+                    for i in range(4):
+                        mm(a("PD%d" % i, 0, 512), [(quart, a("ONES", 0, 512))], True, False)
+                sl, sr = (2 * t - 1) * V, 2 * t * V
+                tr(a("TL", sl, sl + GV), a("G1", 0, GV))
                 if t > 1:
                     nh = a("NHT", 5 - t, 40, 4)
-                    ts(a("PEN", UP[t - 1], UP[t - 1] + 10), nh, -BIG, OP.mult, col("CC", t - 1), OP.add)
-                    ts(a("PEN", CP[t - 1], CP[t - 1] + 10), nh, BIG, OP.mult, -2.0 ** 18, OP.add)
+                    if t == 3:
+                        cp(a("PEN", 50, 60), a("PEN", 40, 50))
+                    ts(a("PEN", 40 - 10 * t, 50 - 10 * t), nh, BIG, OP.mult, col("CC", t - 1), OP.add)
+                    ts(a("PEN", 40, 50), nh, -BIG, OP.mult, 2.0 ** 18, OP.add)
                     tt(a("SBP", 0, 25), a("SBP", 0, 25), a("EQL", 0, 25), OP.max)
-                tr(a("TL", 2 * t * SL + V, (2 * t + 1) * SL), a("G0"))
-                tt(a("E1", 0, NX[t]), a("SND", so, so + NX[t]), a("PEN", 0, NX[t]), OP.add)
+                else:
+                    for j in range(2):
+                        ts(a("NU", 10 * j, 10 * j + 10), a("US", 0, 10), col("CC", 0), OP.subtract)
+                tr(a("TL", sr, sr + 640), a("G0", 0, 640))
+                tt(a("E1", 0, NX[t]), a("SND", so, so + NX[t]), a("PEN", 30 - 10 * t, 30 - 10 * t + NX[t]), OP.add)
                 tt(a("D1", 0, 24), a("SBP", 0, 24), a("SBP", 1, 25), OP.subtract)
-                turn("G1", 2 * t - 1)
+                tt(a("E1", 0, ks), a("E1", 0, ks), a("NU", 0, ks), OP.add)
+                if e == 0 and t == 2:
+                    end_constants()
+                tr(a("TL", sr + 640, sr + V), a("G0", 640, V))
+                tr(a("TL", sl + GV, sl + 896), a("G1", GV, 896))
+                tr(a("TL", sl + 896, sl + V), a("G1", 896, V))
                 continue
 
-            ones, lt = a("ONES"), a("LT")
-            act(a("LT", 640, V), ind(ones, a("LU", 40, 80)))
-            cp(a("LT", 0, 640), ind(ones, a("LU", 0, 40)))
-            act(a("M", 2 * V, 3 * V), ind(lt, a("XU", 160, 240)))
-            act(a("M", V + 640, 2 * V), ind(lt, a("XU", 120, 160)))
-            dropped()
-            cp(ind(bold, offx), a("LB"))
-            cp(a("M", 0, V), ind(lt, a("XU", 0, 80)))
-            scan(a("HS"), a("NHT"), a("HD"), OP.mult, OP.add)
-            ts(a("DZB"), a("PP"), DV, OP.is_ge, float(Z), OP.mult)
-            cp(a("FL", 0, 80), a("BB", 0, 80))
-            tt(a("M", 0, 640), ind(lt, a("XU", 80, 120)), a("M", 0, 640), OP.add)
+            ones, lt, bb = a("ONES"), a("LT"), a(old)
+            expanded()
+            ts(a("LL"), pl, 4096.0, OP.mult, float(Z), OP.min)
+            act(a("LT", 576, V), ind(ones, a("LL", 36, 80)), scale=8192.0)
+            ts(a("LT", 0, 576), ind(ones, a("LL", 0, 36)), 8192.0, OP.mult)
+            ts(a("LB"), pl, 4096.0, OP.mult, float(Z), OP.min)
+            ts(a(old, 0, 80), pr, float(Z), OP.min)
+            xu = lambda j, lo2, hi2: ind(lt, a("XU", 80 * j + lo2 // 16, 80 * j + hi2 // 16))
+            act(a("M", 640, V), xu(0, 640, V))
+            act(a("M", 0, 640), xu(0, 0, 640))
+            act(a("M", V + 640, 2 * V), xu(2, 640, V))
+            ts(a("DZB"), a("LB"), float(Z), OP.is_ge, 32768.0, OP.mult)
+            cp(a("M", V, V + 640), xu(1, 0, 640))
+            tt(a("M", 640, V), xu(1, 640, V), a("M", 640, V), OP.add)
+            tt(a("M", V, V + 640), xu(2, 0, 640), a("M", V, V + 640), OP.add)
             pc = a("PC", 0, 80)
             pick = lambda lo2, hi2: [(a("AA", 128 * i, 128 * i + 128), a("M", lo2 + i, hi2, 16)) for i in range(16)]
-            mm(pc, [(a("NEG"), a("EQ", 80 * j, 80 * j + 80)) for j in range(3)] + [(a("ID"), a("DZB"))], True, False)
-            mm(pc, pick(2 * V, 3 * V), False, False)
-            mm(a("PC", 40, 80), pick(V + 640, 2 * V), False, False)
-            mm(pc, pick(0, V), False, True)
-            ts(a("HT", 0, 5), a("HS", 3, 40, 8), col("PG", 2), OP.mult, pa, OP.add)
-            ts(a("HT", 8, 13), a("HS", 7, 40, 8), phi, OP.mult)
-            tt(a("HT", 16, 21), a("HT", 0, 5), a("HT", 8, 13), OP.add)
-            tt(a("DD", 0, 80), a("BB", 0, 80), a("BS", 80, 160) if e == 0 else a("BS", 320, 400), OP.subtract)
-            cp(a("OFB", 0, 5), a("HT", 16, 21))
-            bsel = ind(a("BB"), a("OFB", 0, 5))
-            cp(a("FL", 80, 160), bsel)
-            cp(a("DD", 80, 160), bsel)
-            fl = lambda j, lo2, hi2: a("FL", 80 * j + lo2 // 16, 80 * j + hi2 // 16)
-            for lo2, hi2 in [(0, 512), (512, V)]:
-                act(a("G0", 16 + lo2, 16 + hi2), ind(Wt, fl(0, lo2, hi2)), bias=-0.25, scale=0.5)
-                tt(a("NF", lo2, hi2), ind(a("H"), fl(1, lo2, hi2)), a("G0", 16 + lo2, 16 + hi2), OP.add)
+            mm(pc, [(n8k, a("EQ", 80 * j, 80 * j + 80)) for j in range(3)] + [(a("ID"), a("DZB"))], True, False)
+            mm(pc, pick(0, V), False, False)
+            mm(pc, pick(V, 2 * V), False, True)
+            cp(ind(bb, offx), a("LB"))
+            cp(a("BF"), ind(bb, a("OFB", 0, 5)))
+            tt(a("XA", 0, 80), a(old, 320, 400), pc, OP.add)
+            tt(a("XA", 80, 160), a("BF"), pc, OP.add)
+            tt(a("XA", 160, 240), a("XA", 0, 80), kv80, OP.min)
+            ts(a("FL", 80, 160), a("XA", 80, 160), float(Z), OP.min)
+            cp(a("FL", 0, 80), a("XA", 160, 240))
+            fa = lambda lo2, hi2: a("FL", lo2 // 16, hi2 // 16)
+            fb = lambda lo2, hi2: a("FL", 80 + lo2 // 16, 80 + hi2 // 16)
 
-            def w_list():
-                ts(a("NG", 0, 80), pc, 0.5, OP.is_ge, float(V), OP.mult)
-                tt(a("NG", 80, 160), a("NG", 0, 80), v80, OP.add)
-                cp(a("FL", 320, 400), a("NG", 80, 160))
+            def wa(lo2, hi2):
+                act(a("MS", lo2, hi2), ind(a(W), fa(lo2, hi2)))
 
-            def kid_lists():
-                ts(a("GO"), pc, 0.5, OP.is_lt)
-                tt(a("ML"), ind(a("GO"), a("REP", 0, 10)), a("DD"), OP.mult)
-                tt(a("MA"), a("ML"), a("BS", 160 + 160 * e, 320 + 160 * e), OP.add)
-                cp(a("FL", 160, 320), a("MA"))
+            def wb(lo2, hi2, q):
+                if q == "s":
+                    act(a("MS", V + lo2, V + hi2), ind(Wt, fb(lo2, hi2)))
+                else:
+                    cp(a("MS", V + lo2, V + hi2), ind(Wt, fb(lo2, hi2)))
 
-            def new_w(name, lo2, hi2):
-                whole(a(name, lo2, hi2), ind(a("NF"), fl(4, lo2, hi2)))
-
-            def kid_b(lo2, hi2):
-                act(a("G1", 16 + lo2, 16 + hi2), ind(a("WB"), fl(3, lo2, hi2)))
-
-            def kid_a(out, lo2, hi2):
-                win = a("WA", 0, V + WT) if e == 0 else a("WA", V, 2 * V + WT)
-                tt(out, ind(win, fl(2, lo2, hi2)), a("G1", 16 + lo2, 16 + hi2), OP.add)
+            def new_w(name, i, lo2, hi2):
+                pd = a("PD%d" % i, 0, hi2 - lo2)
+                mm(pd, [(half, a("MS", lo2, hi2)), (half, a("MS", V + lo2, V + hi2))], False, True)
+                whole(a(name, lo2, hi2), pd)
 
             if e < EP - 1:
-                w_list()
-                new_w("W1", 0, X)
-                send(9, a("W1", 0, X))
-                kid_lists()
-                kid_b(0, 640)
-                new_w("W1", X, 768)
-                rest = own_votes("W1", 160)
-                new_w("W1", 768, 1024)
-                rest(6)
-                rest(7)
-                new_w("W1", 1024, V)
-                rest(8)
-                rest(9)
-                kid_b(640, V)
-                finish("PL", 0, 48, 240, [(160, 6, 0)])
+                own = lambda k: a("W1", 128 * k, 128 * k + 128)
+                wb(0, X, "v")
+                wa(0, X)
+                wa(X, 768)
+                wb(X, 768, "v")
+                new_w("W1", 0, 0, X)
+                send(9, a("W1", 0, X), "h")
+                wa(768, 1024)
+                wb(768, 896, "v")
+                wb(896, V, "s")
+                wa(1024, V)
+                new_w("W1", 1, X, 768)
+                new_w("W1", 2, 768, 1024)
+                new_w("W1", 3, 1024, V)
+                for k in range(7):
+                    act(a("M", 128 * k, 128 * k + 128), own(k), scale=-1.0, acc=col("SND", 160 + k))
+                for k in range(7, NP):
+                    negsum(col("SND", 160 + k), own(k))
                 send(RO, a("SND", 160, 170))
-                for lo2, hi2 in [(0, 640), (640, V)]:
-                    kid_a(a("WA", V + WT + lo2, V + WT + hi2), lo2, hi2)
+                send(9, a("W1", 0, X), "n")
             else:
-                kid_lists()
-                ck = [(0, 320), (320, 800), (800, V)]
-                for lo2, hi2 in ck:
-                    kid_b(lo2, hi2)
-                w_list()
+                ck = [(0, 256), (256, 768), (768, V)]
+                wb(0, 256, "v")
                 for i, (lo2, hi2) in enumerate(ck):
-                    kid_a(a("TL", lo2, hi2), lo2, hi2)
-                    dma("y", [], [a("TL", lo2, hi2)], T.yk[:, lo2:hi2], T.TL[:, lo2:hi2], "o%d" % (1 + i))
-                for lo2, hi2, sem in [(0, 768, "o0"), (768, V, "o4")]:
-                    new_w("YW", lo2, hi2)
-                    dma("y", [], [a("YW", lo2, hi2)], T.yw[:, lo2:hi2], T.YW[:, lo2:hi2], sem)
+                    act(a("G1", lo2, hi2), ind(a("WB"), fb(lo2, hi2)))
+                    tt(a("G0", lo2, hi2), ind(a("WA"), fa(lo2, hi2)), a("G1", lo2, hi2), OP.add)
+                    dma("y", [], [a("G0", lo2, hi2)], T.yk[:, lo2:hi2], T.G0[:, lo2:hi2], "o%d" % (1 + i))
+                wa(0, 384)
+                wb(256, 768, "v")
+                wa(384, 768)
+                new_w("YW", 0, 0, 384)
+                wb(768, 896, "v")
+                wa(768, 1024)
+                wb(896, V, "s")
+                new_w("YW", 1, 384, 768)
+                dma("y", [], [a("YW", 0, 768)], T.yw[:, 0:768], T.YW[:, 0:768], "o0")
+                wa(1024, V)
+                new_w("YW", 2, 768, 1024)
+                new_w("YW", 3, 1024, V)
+                dma("y", [], [a("YW", 768, V)], T.yw[:, 768:V], T.YW[:, 768:V], "o4")
 
     eng = {"g": g, "v": g.vector, "s": g.scalar, "p": g.tensor, "y": g.sync}
     hist, known = {}, {q: {} for q in eng}

@@ -11,20 +11,27 @@ MID = 98304.0
 C0 = 1280.3125
 NX = [10, 30, 50, 70]
 XO = [0, 10, 40, 90]
-KS = [0, 10, 14, 17]
-TAIL = 3
+STEPS = [[7, 7, 7, 7, 7, 0], [7, 7, 7, 7, 2, 1], [7, 7, 7, 4, 0, 8], [7, 7, 3, 7, 2, 1],
+         [7, 5, 6, 0, 8, 8], [4, 7, 7, 3, 2, 1]]
+LATE = [6, 6, 3, 3]
+EV = [0, 2, 3, 3]
+KS = [0, 10, 16, 20]
+TAIL = 2
 LEAD = [0, 13, 31, 38]
-GV = 384
+TS = [0, 1, 2, 1]
+LAST = 8
+GVS = [0, 512, 128, 128]
 
 F, B16, I32, U16, H16 = "float32", "bfloat16", "int32", "uint16", "float16"
 SB_ = {
-    "W0": (WT + V, B16), "W1": (WT + V, B16), "ONES": (WT, B16), "LT": (WT, B16), "YW": (V, B16), "RT": (V, B16),
+    "W0": (WT + V, B16), "W1": (WT + V, B16), "ONES": (WT, B16), "LT": (WT, B16), "YW": (V, B16), "RT": (2 * V, B16), "NS": (240, B16), "M8B": (240, B16),
     "KP": (WT, F), "WA": (WT + V, I32), "K2": (V, I32), "WB": (WT, F), "CI": (V, F), "TL": (7 * V, F),
     "G0": (V, F), "G1": (V, F), "M": (3 * V, B16), "MS": (2 * V, B16), "AA": (2048, B16),
-    "SND": (320, F), "LAND": (1600, F), "E1": (72, F), "E2": (72, F), "E3": (144, F), "E4": (72, F), "US": (72, F),
+    "SND": (320, F), "LAND": (1760, F), "E1": (96, F), "E2": (72, F), "E3": (72, F), "E4": (72, F), "US": (128, F),
+    "UA": (128, F), "UB": (128, F), "PA": (24, U16), "PB": (24, U16), "BC": (216, F), "SI": (36, F), "TG": (88, F),
     "PEN": (72, F), "PEN0": (72, F), "NU": (24, F), "MM": (64, F), "KT": (64, F), "T1": (64, F), "S1": (64, F),
     "BI": (64, F), "BJ": (64, F), "C6": (64, F), "GG": (64, F), "D1": (64, F), "S2": (64, F), "OFF": (12, U16),
-    "RL": (160, H16), "TM": (80, F), "DM": (80, H16), "EE": (768, H16), "LB": (80, F), "B0": (400, F), "B1": (400, F),
+    "RL": (160, H16), "TM": (80, F), "DM": (80, H16), "EE": (896, H16), "AB": (768, H16), "LB": (80, F), "B0": (400, F), "B1": (400, F),
     "LU": (400, U16), "LL": (80, U16), "DZ": (80, F), "DZB": (80, B16), "NEQ": (240, B16), "XU": (240, U16),
     "EQ": (240, B16), "SC": (240, F), "SBP": (32, F), "SBP0": (32, F), "LC": (80, F), "EQH": (32, F), "EQL": (32, F),
     "NHT": (40, F), "HD": (40, F), "HS": (40, F), "HT": (24, F), "OFB": (6, U16), "CM": (16, F),
@@ -37,7 +44,25 @@ PS_ = ["PU", "PC", "PR", "PL", "PD0", "PD1", "PD2", "PD3"]
 SCRATCH = {k: ("sbuf", [128, n], d) for k, (n, d) in SB_.items()}
 SCRATCH.update({k: ("psum", [128, 512], F) for k in PS_})
 SEMAPHORES = (["qv", "qs", "qp", "qg", "lw0", "lw1", "lk0", "lk1", "lk2", "ck", "o0", "o1", "o2", "o3", "o4", "sent"]
-              + ["ad%d" % i for i in range(10)] + ["af%d" % i for i in range(10)] + ["rl%d" % i for i in range(10)])
+              + ["%s%d" % (nm, i) for nm in ("n0m", "n1m", "n2m", "n3m", "af", "ag", "rl") for i in range(10)])
+
+
+def side(s, near):
+    peers = sorted(near[s] + [s])
+    return 2 * peers.index(s) // len(peers)
+
+
+def near_parts(r, near):
+    return sorted(near[r], key=lambda q: near[q].index(r))
+
+
+def near_sem(s, near, m):
+    return "n%dm%d" % (sorted(near[s] + [s]).index(s), m)
+
+
+def far_parts(r, near):
+    far = [q for q in range(len(near)) if q != r and r not in near[q]]
+    return [[q for q in far if side(q, near) == side(r, near) ^ j] for j in range(2)]
 
 
 def routes(T, topo):
@@ -45,11 +70,13 @@ def routes(T, topo):
     near, help_ = [], ([], [])
     for s, c in enumerate(cores):
         near.append([r for r, d in enumerate(cores) if r != s and topo.may_write(c, d)])
-        far = [r for r in range(len(cores)) if r != s and r not in near[s]]
+        near[s] = [r for r in near[s] if r > s] + [r for r in near[s] if r < s]
+    for s, c in enumerate(cores):
+        far = [r for r in range(len(cores)) if r != s and r not in near[s]][::-1 if side(s, near) else 1]
         able = [h for h in topo.cores_of(c) if T.rank_of(h) is None and all(topo.may_write(h, cores[r]) for r in far)]
         for kind in range(2):
-            hs = [h for h in able if (topo.die(h) == topo.die(c)) == (kind == 0)][:max(1, min(2, len(far)))]
-            help_[kind].append([(h, far[i::len(hs)]) for i, h in enumerate(hs)] if far else [])
+            hs = [h for h in able if (topo.die(h) == topo.die(c)) == (kind == 0)][:2]
+            help_[kind].append([(h, far[i::len(hs)]) for i, h in enumerate(hs)])
     return near, help_
 
 
@@ -61,9 +88,15 @@ def message(T, m, s, r, near):
         return w[:, 0:X], w[:, V + (d - 1) * X:V + d * X]
     e, t = divmod(m, RO)
     o, n = 160 * e + XO[t], NX[t]
-    order = [q for q in range(n_ranks) if r in near[q]] + [q for q in range(n_ranks) if q != r and r not in near[q]]
+    order = near_parts(r, near) + sum(far_parts(r, near), [])
     k = order.index(s) if s != r else 0
-    return T.SND[:, o:o + n], T.LAND[:, 5 * o + k * n:5 * o + (k + 1) * n]
+    at = land_at(m, k)
+    return T.SND[:, o:o + n], T.LAND[:, at:at + n]
+
+
+def land_at(m, k):
+    wide = [(n + 7) // 8 * 8 for n in NX]
+    return 5 * (sum(wide) * (m // RO) + sum(wide[:m % RO])) + k * wide[m % RO]
 
 
 def fan_mask(topo, src_core, dst_cores):
@@ -89,37 +122,37 @@ def fan(g, T, topo, src_core, dsts, src, sem):
     return bin(mask).count("1")
 
 
-def helper_program(g, core, T, topo, s, fars, near, helpers, messages):
+def helper_program(g, core, T, topo, s, near, help_):
     cores = list(T.cores)
-    cnt = fan_count(topo, cores[s], [h for h, _ in helpers])
     sent = 0
-    for m in messages:
-        g.wait_ge(T.sem["rl%d" % m], cnt)
-        src = message(T, m, s, s, near)[0]
-        sent += fan(g, T, topo, core, [(cores[r], message(T, m, s, r, near)[1]) for r in fars], src, T.sem["af%d" % m])
-    g.wait_ge(T.sem.sent, sent)
+    for m in [0, 8, 1, 2, 3, 4, 9, 5, 6, 7]:
+        helpers = help_[m // 8][s]
+        for h, fars in helpers:
+            if h == core:
+                g.wait_ge(T.sem["rl%d" % m], fan_count(topo, cores[s], [x for x, _ in helpers]))
+                src = message(T, m, s, s, near)[0]
+                sent += fan(g, T, topo, core, [(cores[r], message(T, m, s, r, near)[1]) for r in fars], src,
+                            T.sem["a%s%d" % ("fg"[side(s, near)], m)])
+    if sent:
+        g.wait_ge(T.sem.sent, sent)
 
 
 def rank_program(g, core, T, topo):
     near, help_ = routes(T, topo)
     rank = T.rank_of(core)
     if rank is None:
-        for kind, messages in enumerate([range(8), range(8, 10)]):
-            for s in range(len(near)):
-                for h, fars in help_[kind][s]:
-                    if h == core:
-                        helper_program(g, core, T, topo, s, fars, near, help_[kind][s], messages)
+        for s, c in enumerate(T.cores):
+            if core in topo.cores_of(c):
+                helper_program(g, core, T, topo, s, near, help_)
         return
     cores = list(T.cores)
     NR = len(cores)
-    src_near = [q for q in range(NR) if rank in near[q]]
-    src_far = [q for q in range(NR) if q != rank and q not in src_near]
-    cnt_near = sum(fan_count(topo, cores[q], [cores[r] for r in near[q]]) for q in src_near)
-    cnt_far = 0
-    for q in src_far:
-        for h, fars in help_[0][q]:
-            if rank in fars:
-                cnt_far += fan_count(topo, h, [cores[r] for r in fars])
+    src_near = near_parts(rank, near)
+    src_far = far_parts(rank, near)
+    cnt_near = [fan_count(topo, cores[q], [cores[r] for r in near[q]]) for q in src_near]
+    cnt_far = [sum(fan_count(topo, h, [cores[r] for r in fars]) for q in part for h, fars in help_[0][q] if rank in fars)
+               for part in src_far]
+    sem_far = ["a" + "fg"[side(rank, near) ^ j] for j in range(2)]
 
     ops = []
 
@@ -208,7 +241,7 @@ def rank_program(g, core, T, topo):
                 sent[0] += fan(e, T, topo, core, [(h, ap) for h, _ in hs], ap, T.sem["rl%d" % m])
             if near[rank] and "n" in to:
                 sent[0] += fan(e, T, topo, core, [(cores[r], message(T, m, rank, r, near)[1]) for r in near[rank]],
-                               ap, T.sem["ad%d" % m])
+                               ap, T.sem[near_sem(rank, near, m)])
         add("g", [], [src], fn, "none")
 
     col = lambda name, j: a(name, j, j + 1)
@@ -217,6 +250,7 @@ def rank_program(g, core, T, topo):
     half, quart, n8k, n24, cdv = [cs(j) for j in range(5)]
     ee = lambda j: a("EE", 128 * j, 128 * j + 128)
     thirds = [(0, 512), (512, 1024), (1024, V)]
+    banks = ["PD0", "PD1", "PD2", "PD3", "PU"]
 
     def colsum(src, lo, npat, po, j):
         mm(a("PU", po, po + 8 * npat), [(a("ID"), a(src, lo + i, lo + 128 * npat, 16)) for i in range(4 * j, 4 * j + 4)],
@@ -229,20 +263,16 @@ def rank_program(g, core, T, topo):
     def absent(ps, w, lo, hi):
         mm(a(ps, 0, hi - lo), [(cdv, a("ONES", 0, hi - lo)), (n24, a(w, lo, hi))])
 
-    def chunks_of(ks):
-        out = []
-        for h0 in range(0, ks, NP):
-            w_ = min(NP, ks - h0)
-            nch = (w_ + 3) // 4
-            out += [(h0 + w_ * i // nch, h0 + w_ * (i + 1) // nch) for i in range(nch)]
-        return out
+    def chunks_of(t):
+        n = KS[t] - EV[t]
+        nch = max(min(4, (n + 2) // 3), (n + 3) // 4)
+        return [(EV[t] + n * i // nch, EV[t] + n * (i + 1) // nch) for i in range(nch)]
 
     def roots(w, i, k0, k1):
-        r0 = 128 * (k0 % NP)
-        mm(a("PD%d" % (i % 4), 0, 128 * (k1 - k0)), [(a("ID"), a(w, r0, r0 + 128 * (k1 - k0)))], True, False)
+        mm(a("PD%d" % (i % 4), 0, 128 * (k1 - k0)), [(a("ID"), a(w if k1 <= NP else "RT", 128 * k0, 128 * k1))], True, False)
 
     def roots_ahead(w, t):
-        for i, (k0, k1) in enumerate(chunks_of(KS[t])[:4]):
+        for i, (k0, k1) in enumerate(chunks_of(t)[:4]):
             roots(w, i, k0, k1)
 
     dma("y", [a("W0", 0, X)], [], T.W0[:, 0:X], T.w[:, 0:X], "lw0")
@@ -290,7 +320,8 @@ def rank_program(g, core, T, topo):
     for h in range(4):
         ts(a("PEN0", 30 - 10 * h, 40 - 10 * h), a("J", 0, 10), 0.0, OP.mult, col("CC", h), OP.add)
     ms(a("SBP0", 4, 25, 5), 0.0)
-    ts(a("TF", 8, 12), a("TF", 20, 24), 6.0, OP.is_ge, 26.0, OP.mult)
+    ts(a("TF", 8, 12), a("TF", 20, 24), 6.0, OP.is_ge, -4.0, OP.mult)
+    ts(a("TF", 16, 20), a("TF", 20, 24), 6.0, OP.mult, 5.0, OP.add)
     for j, (tgt, msk) in enumerate([(pp, col("PG", 3)), (col("PG", 5), col("PG", 3)), (col("PG", 5), hi_), (pp, hi_)]):
         ts(ee(j), a("J"), tgt, OP.is_equal, msk, OP.mult)
     for k in range(NP):
@@ -310,14 +341,13 @@ def rank_program(g, core, T, topo):
     ms(a("W0", Z, WT), 0.0)
     for i, (lo, hi) in enumerate(thirds):
         act(a("PD%d" % i, 0, hi - lo), a("W0", lo, hi), AF.Relu, bias=DV, scale=-DV)
-    act(a("ONES", 0, V), a("W0", 0, V), bias=1.0, scale=0.0)
 
     def late_constants():
-        tt(a("TF", 12, 16), a("TF", 8, 12), a("TF", 20, 24), OP.add)
+        tt(a("TF", 12, 16), a("TF", 8, 12), a("TF", 16, 20), OP.add)
         ts(a("REP", 0, 15), a("RF", 0, 15), pa, OP.add)
         ts(a("LC", 0, 75), a("LC", 0, 75), col("PG", 1), OP.add)
         ts(a("TH", 0, 65), a("TH", 0, 65), -0.25, OP.mult, 0.5, OP.add)
-        cp(a("GR"), a("TF", 12, 16))
+        ts(a("GR"), a("TF", 12, 16), 63.0, OP.min)
         ts(a("TF", 24, 29), a("SBP0", 3, 25, 5), -31.5, OP.add, 1.0 / 64, OP.mult)
         ms(a("NHT"), 0.0)
         ts(a("D1", 33, 54, 5), a("BS", 0, 5), 320.0, OP.add)
@@ -335,11 +365,48 @@ def rank_program(g, core, T, topo):
         for w in ("W1", "ONES"):
             ms(a(w, Z, WT), 0.0)
         ts(half, a("ID"), 0.5, OP.mult)
+        ts(ee(6), a("ID"), 0.5, OP.mult)
         ts(quart, a("ID"), -0.25, OP.mult)
         ts(n8k, a("ID"), -8192.0, OP.mult)
         ts(a("HD", 3, 40, 8), a("J", 0, 5), 16.0, OP.mult, 240.0, OP.add)
         ts(a("HD", 7, 40, 8), a("J", 0, 5), 16.0, OP.mult, 240.0, OP.add)
         ms(a("WB", Z, WT), 0.0)
+
+    def step_lists():
+        bc = a("BC", 0, 36)
+        ms(bc, 70.0)
+        ms(a("BC", 36, 72), 1.0)
+        ts(a("TG", 0, 2), a("BS", 0, 2), -2.5, OP.add, 1.0 / 6, OP.mult)
+        ms(a("E1", 70, 80), 1e9)
+        ms(a("E1", 80, 96), -1e9)
+        ms(a("E1", 10, 70), 0.0)
+        whole(a("TG", 2, 4), a("TG", 0, 2))
+        ms(a("BC", 36, 72, 6), 0.0)
+        marks = [(6 * i + s_, blk) for i, row in enumerate(STEPS) for s_, blk in enumerate(row) if blk != 7]
+
+        def mark(k):
+            for x, blk in marks[:k]:
+                ms(col("BC", x), 10.0 * blk)
+            del marks[:k]
+
+        mark(2)
+        ts(a("TG", 4, 6), a("TG", 2, 4), -6.0, OP.mult)
+        ts(a("TG", 8, 10), a("TG", 2, 4), 2.0, OP.mult)
+        ts(a("TG", 10, 12), a("TG", 2, 4), 2.0, OP.mult, 1.0, OP.add)
+        mark(2)
+        tt(a("TG", 6, 8), a("TG", 4, 6), a("BS", 0, 2), OP.add)
+        mark(4)
+        hot = lambda ph: a("BC", 72 + 36 * ph, 108 + 36 * ph)
+        for ph in range(2):
+            ts(hot(ph), a("SI"), col("TG", 6 + ph), OP.is_equal)
+        mark(len(marks))
+        rest = [lambda ph=ph: tt(hot(ph), hot(ph), bc, OP.mult) for ph in range(2)]
+        rest += [lambda ph=ph: scan(hot(ph + 2), a("BC", 36, 72), hot(ph), OP.mult, OP.add) for ph in range(2)]
+        rest += [lambda ph=ph, par=par: ts(a("TG", 16 + 2 * par + ph, 40, 4), a("BC", 149 + 36 * ph, 180 + 36 * ph, 6),
+                                           col("TG", 8 + 2 * par + ph), OP.add) for ph in range(2) for par in range(2)]
+        rest += [lambda: ts(a("TG", 40, 64), a("TG", 16, 40), 70.0, OP.is_lt), lambda: cp(a("PA"), a("TG", 16, 40)),
+                 lambda: tt(a("TG", 64, 88), a("TG", 40, 64), a("TG", 16, 40), OP.mult), lambda: cp(a("PB"), a("TG", 64, 88))]
+        later.extend(rest)
 
     def dead_term():
         mm(a("PR", 0, 80), [(ee(5), a("DM"))], True, False)
@@ -348,6 +415,15 @@ def rank_program(g, core, T, topo):
     def swap(ps, lo):
         for par in range(2):
             mm(a(ps, par, 80, 2), [(ee(2 * par + q), a("RL", lo + q, lo + 80, 2)) for q in range(2)], False, par == 1)
+
+    later = []
+
+    def turn_last(src, at, lo, k):
+        cut = V - 128 * k
+        if cut > lo:
+            tr(a("TL", at + lo, at + cut), a(src, lo, cut))
+        for x in range(cut, V, 128):
+            later.append(lambda x=x: tr(a("TL", at + x, at + x + 128), a(src, x, x + 128)))
 
     for e in range(EP):
         W = "W%d" % e
@@ -359,69 +435,83 @@ def rank_program(g, core, T, topo):
         ts(a("DM"), a("J", 0, 80), 0.0, OP.mult, 0.3125, OP.add)
         tt(a("E1", 0, 10), a("SND", 160 * e, 160 * e + 10), a("PEN0", 30, 40), OP.add)
         if e > 0:
+            thirds = [(0, 256), (256, 768), (768, V)]
             for lo, hi in thirds:
                 act(a("G1", lo, hi), ind(a("WB"), a("FL", 80 + lo // 16, 80 + hi // 16)))
+        kids2 = lambda lo, hi: tt(a("K2", lo, hi), ind(a("WA"), a("FL", lo // 16, hi // 16)), a("G1", lo, hi), OP.add)
         for i, (lo, hi) in enumerate(thirds):
             if e > 0:
                 absent("PD%d" % i, W, lo, hi)
-                tt(a("K2", lo, hi), ind(a("WA"), a("FL", lo // 16, hi // 16)), a("G1", lo, hi), OP.add)
+                if i == 0:
+                    kids2(lo, hi)
+                if i < 2:
+                    kids2(*thirds[i + 1])
             tt(a("KP", lo, hi), a(kin, ko + lo, ko + hi), a("PD%d" % i, 0, hi - lo), OP.max)
             act(a("G0", lo, hi), a("KP", lo, hi), bias=-C0, scale=1.0 / 4096)
             if e == 0 and i == 0:
                 late_constants()
-            if i:
-                tr(a("TL", *thirds[i - 1]), a("G0", *thirds[i - 1]))
-        tr(a("TL", *thirds[2]), a("G0", *thirds[2]))
+            if i == 1:
+                tr(a("TL", *thirds[0]), a("G0", *thirds[0]))
+        turn_last("G0", 0, thirds[0][1], LATE[0] * e)
         dead_term()
         roots_ahead(W, 1)
+        act(a("RT", 0, V), a(W, 0, V))
+        act(a("RT", V, 2 * V), a(W, 0, V))
         if e > 0:
             dma("y", [a("WA", WT, WT + V)], [a("K2")], T.WA[:, WT:WT + V], T.K2[:, 0:V], "ck")
         else:
-            act(a("ONES", V, Z), a("W0", 0, V), bias=1.0, scale=0.0)
+            end_constants()
+            act(a("ONES", 0, 512), a("W0", 0, 512), bias=1.0, scale=0.0)
             act(a("B0"), a("W0", 0, 400), scale=0.0)
             act(a("B1"), a("W0", 0, 400), scale=0.0)
-        act(a("RT"), a(W, 0, V))
-        act(a(W, WT, WT + V), a(W, 0, V), scale=2.0)
         gh = lambda q: ((rank - q) % NR - 1) * X
-        arrive([a(W, V + gh(q), V + gh(q) + X) for q in src_near], "ad%d" % (8 + e), cnt_near)
-        arrive([a(W, V + gh(q), V + gh(q) + X) for q in src_far], "af%d" % (8 + e), cnt_far)
+        for q, cnt in zip(src_near, cnt_near):
+            arrive([a(W, V + gh(q), V + gh(q) + X)], near_sem(q, near, 8 + e), cnt)
+        for j in range(2):
+            arrive([a(W, V + gh(q), V + gh(q) + X) for q in src_far[j]], "%s%d" % (sem_far[j], 8 + e), cnt_far[j])
 
         for t in range(1, RO + 1):
             m = RO * e + t - 1
-            n, lo = NX[t - 1], 5 * (160 * e + XO[t - 1])
-            land = lambda k, c=1: a("LAND", lo + k * n, lo + (k + c) * n)
-            nn, nf = len(src_near), len(src_far)
-            arrive([land(0, nn)], "ad%d" % m, cnt_near)
-            arrive([land(nn, nf)], "af%d" % m, cnt_far)
-            e1, e2, e4, us = a("E1", 0, n), a("E2", 0, n), a("E4", 0, n), a("US", 0, n)
-            acc, k = e1, 0
-            if nn >= 3:
-                tt(e2, land(0), land(1), OP.add)
-                tt(e4, e1, land(2), OP.add)
-                tt(e1, e2, e4, OP.add)
-                k = 3
-            while k < nn:
-                nxt = e2 if acc is e1 else e1
-                tt(nxt, acc, land(k), OP.add)
-                acc, k = nxt, k + 1
-            parts = [land(nn + k) for k in range(nf)]
-            if nf == 4:
-                tt(a("E3", 0, 2 * n), land(nn, 2), land(nn + 2, 2), OP.add)
-                parts = [a("E3", 0, n), a("E3", n, 2 * n)]
-            if len(parts) == 2:
-                tt(e4, parts[0], parts[1], OP.add)
-                parts = [e4]
+            n = NX[t - 1]
+            land = lambda k: a("LAND", land_at(m, k), land_at(m, k) + n)
+            nn, nf = len(src_near), len(src_far[0])
+            for k in range(nn):
+                arrive([land(k)], near_sem(src_near[k], near, m), cnt_near[k])
+            for j in range(2):
+                arrive([land(nn + j * nf + k) for k in range(nf)], "%s%d" % (sem_far[j], m), cnt_far[j])
+
+            def turns(k):
+                for _ in range(min(k, len(later))):
+                    later.pop(0)()
+
+            e1, e2, e3, e4 = a("E1", 0, n), a("E2", 0, n), a("E3", 0, n), a("E4", 0, n)
+            if nn == 3:
+                tt(e1, e1, land(0), OP.add)
+                turns(1)
+                tt(e1, e1, land(1), OP.add)
+                turns(1)
+                mid_, last = (land(2), land(3)), land(4)
+            else:
+                tt(e1, e1, land(0), OP.add)
+                turns(1)
+                mid_, last = (land(1), land(2)), e4
+            tt(e3, mid_[0], mid_[1], OP.add)
+            turns(1)
+            tt(e2, e1, e3, OP.add)
+            if nn != 3:
+                tt(e4, land(3), land(4), OP.add)
+            turns(1)
             u = lambda h: a("US", 10 * (t - 1 - h), 10 * (t - h))
             c = lambda i: a("US", 10 * (t + i), 10 * (t + i + 1))
             mmx = lambda j: a("MM", 10 * j, 10 * j + 10)
-            kt = lambda par: a("KT", 32 * par, 32 * par + 5)
-            first = (acc, parts[0])
+            kt = lambda par: a("KT", 32 * par + 5, 32 * par + 30, 6)
             if t == 1:
-                an, pn = acc["r"][0][0], parts[0]["r"][0]
+                pn = last["r"][0]
                 for par in range(2):
-                    tt(kt(par), a(an, par, 10, 2), a(pn[0], pn[1] + par, pn[1] + 10, 2), OP.add)
+                    tt(kt(par), a("E2", par, 10, 2), a(pn[0], pn[1] + par, pn[1] + 10, 2), OP.add)
             else:
-                tt(us, acc, parts[0], OP.add)
+                tt(a("US", 0, n), e2, last, OP.add)
+                turns(1)
                 if t == 2:
                     tt(mmx(0), u(1), c(0), OP.max)
                     xs = ("US", 10)
@@ -439,6 +529,7 @@ def rank_program(g, core, T, topo):
                     xs = ("MM", 40)
                 for par in range(2):
                     tt(kt(par), a(xs[0], xs[1] + par, xs[1] + 10, 2), a("MM", par, 10, 2), OP.min)
+
             def dropped():
                 ts(a("NHT", 5 - t, 40, 4), c(0) if t == 2 else mmx(1) if t == 3 else a("CM", 0, 10), 0.0, OP.is_gt)
 
@@ -452,6 +543,7 @@ def rank_program(g, core, T, topo):
             def between():
                 if fill:
                     fill.pop(0)()
+                turns(1)
 
             between()
             tr(a("T1"), a("KT"))
@@ -467,14 +559,15 @@ def rank_program(g, core, T, topo):
             tr(a("C6", 0, nb), a("BJ", 0, nb))
             between()
             if t == 1:
-                tt(a("S2", 0, 5), a("C6", 0, 5), a("TF", 24, 29), OP.add)
+                tt(a("S2", 0, 5), a("C6", 5, 30, 6), a("TF", 24, 29), OP.add)
                 ts(a("OFF", 0, 5), a("S2", 0, 5), 64.0, OP.mult)
             else:
                 tt(a("GG"), ind(a("C6"), a("GR")), a("TH", 0, 64), OP.is_gt)
-                ts(a("D1", 4, 25, 5), a("C6", 0, 5), 64.0, OP.mult, -31.5, OP.add)
+                ts(a("D1", 4, 25, 5), a("C6", 5, 30, 6), 64.0, OP.mult, -31.5, OP.add)
                 scan(a("S2", 0, 55), a("GG", 0, 55), a("D1", 0, 55), OP.mult, OP.add)
                 between()
                 cp(a("OFF", 0, 11), a("S2", 4, 55, 5))
+            turns(len(later))
             off, offx = a("OFF", 0, 5), a("OFF", 6, 11)
             tl = a("TL", 0, (2 * t - 1) * V)
             old, new = ("B1", "B0") if t % 2 == 0 else ("B0", "B1")
@@ -506,19 +599,33 @@ def rank_program(g, core, T, topo):
                 nu, ks = 10 * (t + 1), KS[t]
                 bt, bold = a(new, hp(t), hp(t) + 80), a(new, hp(t - 1), 400)
                 rep = a("REP", 0, 5 * t)
+                ev = EV[t]
+                mo = lambda k: k if k < ev else k - ks + ev
+
+                def vector_part(k0, k1):
+                    r0 = 128 * (k0 % NP)
+                    tt(a("M", 128 * mo(k0), 128 * (mo(k0) + k1 - k0)), ind(Wt, lu(8 * k0, 8 * k1)),
+                       a("RT", r0, r0 + 128 * (k1 - k0)), OP.min)
+
                 if t == 1:
+                    ts(bt, pr, float(Z), OP.min)
+                    vector_part(0, 1)
                     ts(lu(80, 160), pl, 4096.0, OP.mult, float(Z), OP.min)
-                    cp(a(new, hp(1), 400), lu(0, 160))
+                    ts(bold, pl, 4096.0, OP.mult, float(Z), OP.min)
+                    vector_part(1, ev)
                     tt(a("NEQ", 0, 80), bt, bold, OP.not_equal)
                 else:
-                    ts(a("LB"), pl, 4096.0, OP.mult, float(Z), OP.min)
                     ts(a("DZ"), pr, float(Z), OP.is_ge, float(Z), OP.mult)
                     ts(bt, pr, float(Z), OP.min)
+                    vector_part(0, 1)
+                    ts(a("LB"), pl, 4096.0, OP.mult, float(Z), OP.min)
                     tt(bold, ind(a("DZ"), rep), a(old, hp(t - 1), 400), OP.max)
+                    vector_part(1, 2)
                     cp(ind(a(new), offx), a("LB"))
+                    vector_part(2, ev)
                     cp(lu(80, 80 + 80 * t), bold)
                     tt(a("NEQ", 0, 80 * t), ind(bt, rep), bold, OP.not_equal)
-                chunks = chunks_of(ks)
+                chunks = chunks_of(t)
 
                 def short(i):
                     k0, k1 = chunks[i]
@@ -541,32 +648,39 @@ def rank_program(g, core, T, topo):
                         act(a("SND", so + nu, so + nu + 10 * t), a("PC", 0, 10 * t))
                         short(i)
 
-                def vector_part(k0, k1):
-                    r0 = 128 * (k0 % NP)
-                    tt(a("M", 128 * (k0 - ks), 128 * (k1 - ks)), ind(Wt, lu(8 * k0, 8 * k1)),
-                       a("RT", r0, r0 + 128 * (k1 - k0)), OP.min)
-
-                mid = (ks + nu - TAIL + 1) // 2 if nu - TAIL - ks >= 14 else ks
-                cuts = sorted(set([ks, mid, nu - TAIL, nu] + [x for x in range(0, nu, NP) if x > ks]))
-                steps = [(4 * k1 + 3 * (chunks[i - 1][0] if i else 0), 0, i) for i, (k0, k1) in enumerate(chunks)]
+                pe = nu - TAIL - TS[t]
+                mid = pe - LAST if mo(pe) > LAST + 4 else ks
+                cuts = sorted(set([ks, mid, pe, nu - TAIL, nu]))
+                for k0, k1 in list(zip(cuts, cuts[1:])):
+                    if k0 % NP + k1 - k0 > 2 * NP:
+                        cuts = sorted(cuts + [k0 - k0 % NP + 2 * NP])
+                steps = [(4 * (k1 - ev) + 3 * (chunks[i - 1][0] - ev if i else 0), 0, i) for i, (k0, k1) in enumerate(chunks)]
                 steps += [(LEAD[t] + 4 * (k1 - ks), 1, (k0, k1)) for k0, k1 in zip(cuts, cuts[1:])]
-                for k0, k1 in [(ks, mid), (mid, nu - TAIL)]:
-                    if k1 > k0:
-                        steps += [(LEAD[t] + 4 * (k1 - ks) + 5 * j, 2, (k0, k1, j)) for j in range(4)]
+                for m0, k1 in ([(0, mid), (mo(mid), pe)] if mid > ks else [(0, pe)]):
+                    steps += [(LEAD[t] + 4 * (k1 - ks) + 5 * j, 2, (m0, mo(k1), j)) for j in range(4)]
                 for _, kind, x in sorted(steps):
                     if kind == 2:
-                        colsum("M", 128 * (x[0] - ks), x[1] - x[0], 8 * (x[0] - ks), x[2])
+                        colsum("M", 128 * x[0], x[1] - x[0], 8 * x[0], x[2])
                     elif kind:
                         vector_part(*x)
                     else:
                         scalar_part(x)
+                unit = lambda k: a("M", 128 * mo(k), 128 * mo(k) + 128)
+                for k in range(pe, nu - TAIL):
+                    act(unit(k), unit(k), scale=-1.0, acc=col("SND", so + k))
+                w8 = 8 * mo(pe)
+                scan(a("SC", 0, w8), a("M8", 0, w8), a("PU", 0, w8), OP.mult, OP.add)
                 for k in range(nu - TAIL, nu):
-                    negsum(col("SND", so + k), a("M", 128 * (k - ks), 128 * (k - ks + 1)))
-                finish(nu - TAIL - ks, so + ks)
+                    negsum(col("SND", so + k), unit(k))
+                ts(a("SND", so, so + ev), a("SC", 7, 8 * ev, 8), -1.0, OP.mult)
+                ts(a("SND", so + ks, so + pe), a("SC", 8 * ev + 7, w8, 8), -1.0, OP.mult)
                 if t == 1:
-                    for i, (lo2, hi2) in enumerate(thirds):
-                        ps = ["PR", "PL", "PD0"][i]
-                        absent(ps, W, V + lo2, V + hi2)
+                    for i, (lo2, hi2) in enumerate([(0, 256), (256, 768), (768, V)]):
+                        ps = ["PD3", "PL", "PR"][i]
+                        if i < 2:
+                            act(a(ps, 0, hi2 - lo2), a(W, V + lo2, V + hi2), AF.Relu, bias=DV, scale=-DV)
+                        else:
+                            absent(ps, W, V + lo2, V + hi2)
                         tt(a("KP", V + lo2, V + hi2), a("CI", lo2, hi2), a(ps, 0, hi2 - lo2), OP.max)
                 send(m + 1, a("SND", so, so + NX[t]))
                 if t == 1:
@@ -576,11 +690,15 @@ def rank_program(g, core, T, topo):
                     llist = lambda c0, c1: a("LL", c0, c1)
                 for lo2, hi2 in [(0, 640), (640, V)]:
                     act(a("G0", lo2, hi2), ind(a("KP"), lu(lo2 // 16, hi2 // 16)), bias=-C0, scale=1.0 / 4096)
+                GV = GVS[t]
                 for lo2, hi2 in [(GV, 896), (896, V)]:
                     act(a("G1", lo2, hi2), ind(a("KP"), llist(lo2 // 16, hi2 // 16)), bias=-C0, scale=1.0 / 4096)
+                if t == 2:
+                    act(a(W, WT, WT + V), a(W, 0, V), scale=2.0)
                 if e == 0:
                     if t == 1:
                         iota(a("WA", 0, WT), [[1, WT]], 0, 0, False)
+                        act(a("ONES", 512, Z), a(W, 512, Z), bias=1.0, scale=0.0)
                     elif t == 2:
                         add("g", [a("AA")], [a("ONES", 0, 2048)],
                             lambda en: en.affine_select(T.AA[:, 0:2048], T.ONES[:, 0:2048], [[-1000, 16], [-16, 8], [999, 16]],
@@ -597,13 +715,13 @@ def rank_program(g, core, T, topo):
                     expanded()
                 else:
                     cp(a("SBP", 3, 25, 5), a("LC", 3, 25, 5))
-                    tt(a("US", 0, 10), first[0]["r"] and a(first[0]["r"][0][0], 0, 10), first[1], OP.add)
+                    tt(a("US", 0, 10), e2, last, OP.add)
                 dead_term()
                 if t + 1 < RO:
                     roots_ahead(W, t + 1)
                 else:
-                    for i in range(4):
-                        mm(a("PD%d" % i, 0, 512), [(quart, a("ONES", 0, 512))], True, False)
+                    for ps in banks[:5 - e]:
+                        mm(a(ps, 0, 384), [(quart, a("ONES", 0, 384))], True, False)
                 sl, sr = (2 * t - 1) * V, 2 * t * V
                 tr(a("TL", sl, sl + GV), a("G1", 0, GV))
                 if t > 1:
@@ -619,34 +737,35 @@ def rank_program(g, core, T, topo):
                 tr(a("TL", sr, sr + 640), a("G0", 0, 640))
                 tt(a("E1", 0, NX[t]), a("SND", so, so + NX[t]), a("PEN", 30 - 10 * t, 30 - 10 * t + NX[t]), OP.add)
                 tt(a("D1", 0, 24), a("SBP", 0, 24), a("SBP", 1, 25), OP.subtract)
-                tt(a("E1", 0, ks), a("E1", 0, ks), a("NU", 0, ks), OP.add)
-                if e == 0 and t == 2:
-                    end_constants()
+                tt(a("E1", ev, ks), a("E1", ev, ks), a("NU", ev, ks), OP.add)
                 tr(a("TL", sr + 640, sr + V), a("G0", 640, V))
-                tr(a("TL", sl + GV, sl + 896), a("G1", GV, 896))
-                tr(a("TL", sl + 896, sl + V), a("G1", 896, V))
+                turn_last("G1", sl, GV, LATE[t])
                 continue
 
             ones, lt, bb = a("ONES"), a("LT"), a(old)
             expanded()
             ts(a("LL"), pl, 4096.0, OP.mult, float(Z), OP.min)
-            act(a("LT", 576, V), ind(ones, a("LL", 36, 80)), scale=8192.0)
-            ts(a("LT", 0, 576), ind(ones, a("LL", 0, 36)), 8192.0, OP.mult)
+            act(a("LT", 640, V), ind(ones, a("LL", 40, 80)), scale=8192.0)
             ts(a("LB"), pl, 4096.0, OP.mult, float(Z), OP.min)
             ts(a(old, 0, 80), pr, float(Z), OP.min)
+            ts(a("LT", 0, 640), ind(ones, a("LL", 0, 40)), 8192.0, OP.mult)
             xu = lambda j, lo2, hi2: ind(lt, a("XU", 80 * j + lo2 // 16, 80 * j + hi2 // 16))
-            act(a("M", 640, V), xu(0, 640, V))
-            act(a("M", 0, 640), xu(0, 0, 640))
-            act(a("M", V + 640, 2 * V), xu(2, 640, V))
+            for j in range(3):
+                act(a("M", V * (2 - j) + 640, V * (3 - j)), xu(j, 640, V))
             ts(a("DZB"), a("LB"), float(Z), OP.is_ge, 32768.0, OP.mult)
-            cp(a("M", V, V + 640), xu(1, 0, 640))
-            tt(a("M", 640, V), xu(1, 640, V), a("M", 640, V), OP.add)
-            tt(a("M", V, V + 640), xu(2, 0, 640), a("M", V, V + 640), OP.add)
+            for j in range(3):
+                for lo2 in (0, 320):
+                    mj = a("M", lo2, lo2 + 320)
+                    if j:
+                        tt(mj, xu(j, lo2, lo2 + 320), mj, OP.add)
+                    else:
+                        cp(mj, xu(j, lo2, lo2 + 320))
             pc = a("PC", 0, 80)
             pick = lambda lo2, hi2: [(a("AA", 128 * i, 128 * i + 128), a("M", lo2 + i, hi2, 16)) for i in range(16)]
             mm(pc, [(n8k, a("EQ", 80 * j, 80 * j + 80)) for j in range(3)] + [(a("ID"), a("DZB"))], True, False)
-            mm(pc, pick(0, V), False, False)
-            mm(pc, pick(V, 2 * V), False, True)
+            for j in (2, 1):
+                mm(a("PC", 40, 80), pick(V * j + 640, V * j + V), False, False)
+            mm(pc, pick(0, V), False, True)
             cp(ind(bb, offx), a("LB"))
             cp(a("BF"), ind(bb, a("OFB", 0, 5)))
             tt(a("XA", 0, 80), a(old, 320, 400), pc, OP.add)
@@ -666,49 +785,56 @@ def rank_program(g, core, T, topo):
                 else:
                     cp(a("MS", V + lo2, V + hi2), ind(Wt, fb(lo2, hi2)))
 
-            def new_w(name, i, lo2, hi2):
-                pd = a("PD%d" % i, 0, hi2 - lo2)
-                mm(pd, [(half, a("MS", lo2, hi2)), (half, a("MS", V + lo2, V + hi2))], False, True)
+            def wab(i, lo2, hi2):
+                tt(a("AB", lo2, hi2), ind(Wt, fb(lo2, hi2)), a("MS", lo2, hi2), OP.add)
+                mm(a(banks[i], 0, hi2 - lo2), [(ee(6), a("AB", lo2, hi2))], False, True)
+
+            def new_w(name, i, lo2, hi2, summed=False):
+                pd = a(banks[i], 0, hi2 - lo2)
+                if not summed:
+                    mm(pd, [(half, a("MS", lo2, hi2)), (half, a("MS", V + lo2, V + hi2))], False, True)
                 whole(a(name, lo2, hi2), pd)
 
             if e < EP - 1:
                 own = lambda k: a("W1", 128 * k, 128 * k + 128)
-                wb(0, X, "v")
-                wa(0, X)
-                wa(X, 768)
-                wb(X, 768, "v")
-                new_w("W1", 0, 0, X)
+                wb(768, 1152, "v")
+                for i in range(3):
+                    wa(X * i, X * i + X)
+                wab(0, 0, X)
+                wab(1, X, 2 * X)
+                new_w("W1", 0, 0, X, True)
                 send(9, a("W1", 0, X), "h")
+                wab(2, 2 * X, 3 * X)
                 wa(768, 1024)
-                wb(768, 896, "v")
-                wb(896, V, "s")
+                wb(1152, V, "s")
                 wa(1024, V)
-                new_w("W1", 1, X, 768)
-                new_w("W1", 2, 768, 1024)
-                new_w("W1", 3, 1024, V)
-                for k in range(7):
+                new_w("W1", 1, X, 2 * X, True)
+                new_w("W1", 2, 2 * X, 3 * X, True)
+                new_w("W1", 3, 768, 1024)
+                new_w("W1", 4, 1024, V)
+                for k in range(8):
                     act(a("M", 128 * k, 128 * k + 128), own(k), scale=-1.0, acc=col("SND", 160 + k))
-                for k in range(7, NP):
+                for k in range(8, NP):
                     negsum(col("SND", 160 + k), own(k))
                 send(RO, a("SND", 160, 170))
                 send(9, a("W1", 0, X), "n")
             else:
                 ck = [(0, 256), (256, 768), (768, V)]
-                wb(0, 256, "v")
+                wb(768, 1024, "v")
                 for i, (lo2, hi2) in enumerate(ck):
                     act(a("G1", lo2, hi2), ind(a("WB"), fb(lo2, hi2)))
                     tt(a("G0", lo2, hi2), ind(a("WA"), fa(lo2, hi2)), a("G1", lo2, hi2), OP.add)
                     dma("y", [], [a("G0", lo2, hi2)], T.yk[:, lo2:hi2], T.G0[:, lo2:hi2], "o%d" % (1 + i))
                 wa(0, 384)
-                wb(256, 768, "v")
                 wa(384, 768)
-                new_w("YW", 0, 0, 384)
-                wb(768, 896, "v")
+                wab(0, 0, 384)
+                wab(1, 384, 768)
+                new_w("YW", 0, 0, 384, True)
                 wa(768, 1024)
-                wb(896, V, "s")
-                new_w("YW", 1, 384, 768)
-                dma("y", [], [a("YW", 0, 768)], T.yw[:, 0:768], T.YW[:, 0:768], "o0")
+                wb(1024, V, "s")
                 wa(1024, V)
+                new_w("YW", 1, 384, 768, True)
+                dma("y", [], [a("YW", 0, 768)], T.yw[:, 0:768], T.YW[:, 0:768], "o0")
                 new_w("YW", 2, 768, 1024)
                 new_w("YW", 3, 1024, V)
                 dma("y", [], [a("YW", 768, V)], T.yw[:, 768:V], T.YW[:, 768:V], "o4")

@@ -11,39 +11,51 @@ MID = 98304.0
 C0 = 1280.3125
 NX = [10, 30, 50, 70]
 XO = [0, 10, 40, 90]
-STEPS = [[7, 7, 7, 7, 7, 0], [7, 7, 7, 7, 2, 1], [7, 7, 7, 4, 0, 8], [7, 7, 3, 7, 2, 1],
-         [7, 5, 6, 0, 8, 8], [4, 7, 7, 3, 2, 1]]
-LATE = [6, 6, 3, 3]
 EV = [0, 2, 3, 3]
-KS = [0, 10, 16, 20]
+KS = [0, 10, 15, 20]
+SP = [0, 1, 2, 3]
+LV = 512
+XV = 512
+GV = [0, 512, 512, 512]
+NQ = [0, 2, 2, 2]
+WS = 1024
+GA = 1.6
+GF = [0.5, 0.0]
+GN = [0.5, 0.5]
+PF = 0.01
 TAIL = 2
-LEAD = [0, 13, 31, 38]
-TS = [0, 1, 2, 1]
 LAST = 8
-GVS = [0, 512, 128, 128]
+PIECE = 10
+FINE = 768
+
+CY = 1.0e-3
+SEM = 0.14
+SWEEPS = 0
+NEAR = 1.6
+STEP = 0.5
+FAR = 2.5
 
 F, B16, I32, U16, H16 = "float32", "bfloat16", "int32", "uint16", "float16"
 SB_ = {
-    "W0": (WT + V, B16), "W1": (WT + V, B16), "ONES": (WT, B16), "LT": (WT, B16), "YW": (V, B16), "RT": (2 * V, B16), "NS": (240, B16), "M8B": (240, B16),
+    "W0": (WT + V, B16), "W1": (WT + V, B16), "ONES": (WT, B16), "LT": (WT, B16), "YW": (V, B16), "RT": (V, B16),
     "KP": (WT, F), "WA": (WT + V, I32), "K2": (V, I32), "WB": (WT, F), "CI": (V, F), "TL": (7 * V, F),
-    "G0": (V, F), "G1": (V, F), "M": (3 * V, B16), "MS": (2 * V, B16), "AA": (2048, B16),
-    "SND": (320, F), "LAND": (1760, F), "E1": (96, F), "E2": (72, F), "E3": (72, F), "E4": (72, F), "US": (128, F),
-    "UA": (128, F), "UB": (128, F), "PA": (24, U16), "PB": (24, U16), "BC": (216, F), "SI": (36, F), "TG": (88, F),
-    "PEN": (72, F), "PEN0": (72, F), "NU": (24, F), "MM": (64, F), "KT": (64, F), "T1": (64, F), "S1": (64, F),
+    "G0": (V, F), "G1": (V, F), "GB": (V, F), "M": (5 * V, B16), "MS": (3 * V, B16), "XS": (3 * V, B16), "AA": (2048, B16),
+    "SND": (320, F), "LAND": (1760, F), "US": (128, F), "SGN": (32, F), "ID32": (128, F),
+    "PEN": (72, F), "PEN0": (72, F), "NU": (32, F), "MM": (64, F), "KT": (64, F), "T1": (64, F), "S1": (64, F),
     "BI": (64, F), "BJ": (64, F), "C6": (64, F), "GG": (64, F), "D1": (64, F), "S2": (64, F), "OFF": (12, U16),
-    "RL": (160, H16), "TM": (80, F), "DM": (80, H16), "EE": (896, H16), "AB": (768, H16), "LB": (80, F), "B0": (400, F), "B1": (400, F),
-    "LU": (400, U16), "LL": (80, U16), "DZ": (80, F), "DZB": (80, B16), "NEQ": (240, B16), "XU": (240, U16),
-    "EQ": (240, B16), "SC": (240, F), "SBP": (32, F), "SBP0": (32, F), "LC": (80, F), "EQH": (32, F), "EQL": (32, F),
+    "RL": (160, H16), "DM": (80, B16), "EE": (640, H16), "AB": (V, H16), "LB": (80, F), "B0": (400, F), "B1": (400, F),
+    "LU": (400, U16), "LL": (80, U16), "DZB": (80, B16), "NEQ": (240, B16), "XU": (240, U16),
+    "EQ": (240, B16), "SC": (512, F), "SD": (128, F), "SBP": (32, F), "SBP0": (32, F), "LC": (80, F), "EQH": (32, F), "EQL": (32, F),
     "NHT": (40, F), "HD": (40, F), "HS": (40, F), "HT": (24, F), "OFB": (6, U16), "CM": (16, F),
-    "XA": (240, F), "BF": (80, F), "FL": (160, U16), "BS": (160, F),
-    "PI": (8, I32), "PF": (8, F), "PG": (16, F), "CC": (8, F), "J": (128, F), "JG": (128, F), "TH": (72, F),
-    "ID": (128, B16), "NEG": (128, B16), "BO": (128, B16), "CS": (640, B16), "M8": (240, F), "M16": (64, F),
-    "RF": (32, F), "REP": (16, U16), "BG": (4, U16), "GR": (4, U16), "TF": (32, F),
+    "XA": (160, F), "BH": (80, H16), "AM": (80, F), "FL": (160, U16), "BS": (160, F),
+    "PI": (8, I32), "PF": (8, F), "PG": (16, F), "CC": (8, F), "J": (128, F), "JG": (128, F), "TH": (168, F), "LI": (160, U16),
+    "ID": (128, B16), "NEG": (128, B16), "BO": (256, B16), "CS": (1024, B16), "M8": (512, F), "M16": (64, F),
+    "BG": (4, U16), "GR": (4, U16), "TF": (32, F),
 }
 PS_ = ["PU", "PC", "PR", "PL", "PD0", "PD1", "PD2", "PD3"]
 SCRATCH = {k: ("sbuf", [128, n], d) for k, (n, d) in SB_.items()}
 SCRATCH.update({k: ("psum", [128, 512], F) for k in PS_})
-SEMAPHORES = (["qv", "qs", "qp", "qg", "lw0", "lw1", "lk0", "lk1", "lk2", "ck", "o0", "o1", "o2", "o3", "o4", "sent"]
+SEMAPHORES = (["qv", "qs", "qp", "qg", "lw0", "lw1", "lk0", "lk1", "lk2", "ck", "o0", "o1", "o2", "o3", "o4", "o5", "sent"]
               + ["%s%d" % (nm, i) for nm in ("n0m", "n1m", "n2m", "n3m", "af", "ag", "rl") for i in range(10)])
 
 
@@ -110,8 +122,22 @@ def fan_count(topo, src_core, dst_cores):
     return bin(fan_mask(topo, src_core, dst_cores)).count("1")
 
 
-def fan(g, T, topo, src_core, dsts, src, sem):
-    mask = fan_mask(topo, src_core, [d for d, _ in dsts])
+def relay_mask(T, topo, m, s, near, help_):
+    cores = list(T.cores)
+    every = fan_mask(topo, cores[s], [h for h, _ in help_[m // 8][s]])
+    out = fan_mask(topo, cores[s], [cores[r] for r in near[s]])
+    return every & ~out if m == 8 else out if m == 0 else every
+
+
+def near_by(m, s, near, help_):
+    free = [h for h, fars in help_[1][s] if len(fars) < 2] if m >= 8 else []
+    by = {h: [r] for h, r in zip(free, near[s][1:])}
+    by[None] = near[s][:len(near[s]) - len(by)] if not by else near[s][:1] + near[s][1 + len(by):]
+    return by
+
+
+def fan(g, T, topo, src_core, dsts, src, sem, mask=-1):
+    mask &= fan_mask(topo, src_core, [d for d, _ in dsts])
     ad = [topo.addr(d, src_core) for d, _ in dsts]
     if len(dsts) == 1:
         g.remote_dma(dsts[0][1], src, sem, T.sem.sent, ad[0][1], ad[0][0], mask)
@@ -129,12 +155,78 @@ def helper_program(g, core, T, topo, s, near, help_):
         helpers = help_[m // 8][s]
         for h, fars in helpers:
             if h == core:
-                g.wait_ge(T.sem["rl%d" % m], fan_count(topo, cores[s], [x for x, _ in helpers]))
+                g.wait_ge(T.sem["rl%d" % m], bin(relay_mask(T, topo, m, s, near, help_)).count("1"))
                 src = message(T, m, s, s, near)[0]
                 sent += fan(g, T, topo, core, [(cores[r], message(T, m, s, r, near)[1]) for r in fars], src,
                             T.sem["a%s%d" % ("fg"[side(s, near)], m)])
+                for r in near_by(m, s, near, help_).get(h, []):
+                    sent += fan(g, T, topo, core, [(cores[r], message(T, m, s, r, near)[1])], src, T.sem[near_sem(s, near, m)])
     if sent:
         g.wait_ge(T.sem.sent, sent)
+
+
+def depends(ops):
+    hist = {}
+    for i, o in enumerate(ops):
+        hard, soft = set(), set()
+        for kind in ("rd", "wr"):
+            for nm, lo, hi in o[kind]:
+                for l2, h2, k2, j in hist.get(nm, []):
+                    hit = (kind == "wr" or k2 == "wr") and lo < h2 and l2 < hi
+                    if nm in PS_ and ops[j]["q"] != o["q"]:
+                        hard.add(j)
+                    elif nm in PS_ and o["q"] == "p":
+                        if o["grp"] is None or o["grp"] != ops[j]["grp"]:
+                            soft.add(j)
+                    elif hit and ops[j]["sem"] != "none":
+                        hard.add(j)
+        o["hard"], o["soft"] = hard, soft - hard
+        for kind in ("rd", "wr"):
+            for nm, lo, hi in o[kind]:
+                hist.setdefault(nm, []).append((lo, hi, kind, i))
+
+
+def put_in_order(ops):
+    edges = []
+    for o in ops:
+        edges.append([(j, ops[j]["cost"] + ops[j]["lat"] + SEM) for j in o["hard"]] + [(j, ops[j]["cost"]) for j in o["soft"]]
+                     + [(j, ops[j]["cost"] + d) for j, d in o["after"]])
+    ahead = [o["cost"] + o["lat"] for o in ops]
+    for i in range(len(ops) - 1, -1, -1):
+        for j, d in edges[i]:
+            ahead[j] = max(ahead[j], d + ahead[i])
+    back = [[] for _ in ops]
+    for i, o in enumerate(ops):
+        for j, d in edges[i]:
+            back[j].append((i, d + o["cost"] - ops[j]["cost"]))
+
+    def place(order, before, least):
+        start, busy = {}, {}
+        for i in order:
+            t = max([start[j] + d for j, d in before[i]] + [least[i]])
+            if ops[i]["q"] != "x":
+                line = busy.setdefault(ops[i]["q"], [])
+                k = 0
+                while k < len(line) and line[k][1] <= t:
+                    k += 1
+                while k < len(line) and line[k][0] < t + ops[i]["cost"] - 1e-9:
+                    t = max(t, line[k][1])
+                    k += 1
+                line.insert(k, (t, t + ops[i]["cost"]))
+            start[i] = t
+        return start
+
+    every = range(len(ops))
+    zero, lats = [0.0] * len(ops), [o["lat"] for o in ops]
+    end = lambda st, i: st[i] + ops[i]["cost"]
+    start = best = place(sorted(every, key=lambda i: (-ahead[i], i)), edges, zero)
+    span = lambda st: max(end(st, i) + lats[i] for i in every)
+    for _ in range(SWEEPS):
+        rev = place(sorted(every, key=lambda i: (-end(start, i) - lats[i], -i)), back, lats)
+        start = place(sorted(every, key=lambda i: (-end(rev, i), i)), edges, zero)
+        if span(start) < span(best):
+            best = start
+    return sorted(every, key=lambda i: (best[i], i))
 
 
 def rank_program(g, core, T, topo):
@@ -160,15 +252,17 @@ def rank_program(g, core, T, topo):
         if hi is None:
             hi = SB_[name][0]
         ap = T[name][:, lo:hi] if st == 1 else T[name][:, lo:hi:st]
-        return {"ap": ap, "r": [(name, lo, hi)]}
+        return {"ap": ap, "r": [(name, lo, hi)], "n": len(range(lo, hi, st)), "ps": name in PS_,
+                "two": name not in PS_ and SB_[name][1] in (B16, H16, U16)}
 
     def ind(win, off):
-        return {"ap": win["ap"].indirect(off["ap"]), "r": win["r"] + off["r"], "w": win["r"], "o": off["r"]}
+        return {"ap": win["ap"].indirect(off["ap"]), "r": win["r"] + off["r"], "w": win["r"], "o": off["r"],
+                "n": 16 * off["n"], "ps": False, "two": False}
 
     def val(x):
         return x["ap"] if isinstance(x, dict) else x
 
-    def add(q, outs, ins, fn, sem=None):
+    def add(q, outs, ins, fn, cost, sem=None, lat=0.0, after=(), grp=None):
         rd, wr = [], []
         for x in ins:
             if isinstance(x, dict):
@@ -176,116 +270,153 @@ def rank_program(g, core, T, topo):
         for x in outs:
             wr += x.get("w", x["r"])
             rd += x.get("o", [])
-        ops.append({"q": q, "rd": rd, "wr": wr, "fn": fn, "sem": sem})
+        ops.append({"q": q, "rd": rd, "wr": wr, "fn": fn, "sem": sem, "cost": cost, "lat": lat, "after": list(after), "grp": grp})
+        return len(ops) - 1
 
-    def arrive(outs, sem, n):
-        add("x", outs, [], None, (sem, n))
+    rows = {}
+
+    def in_row(name):
+        if name in rows:
+            ops[-1]["after"].append((rows[name], 0.0))
+        rows[name] = len(ops) - 1
+
+    def vcost(o, x, rate=None):
+        if "o" in o:
+            return 0.05 + 3 * CY * x["n"]
+        if "o" in x:
+            return 0.05 + GA * CY * x["n"]
+        if rate is None:
+            rate = 0.5 if o["two"] and x["two"] else 1
+        return CY * max(64, rate * x["n"])
+
+    def arrive(outs, sem, n, after):
+        add("x", outs, [], None, 0.01, (sem, n), after=[after])
 
     def tt(o, x, y, op):
-        add("v", [o], [x, y], lambda e: e.tensor_tensor(o["ap"], x["ap"], y["ap"], op))
+        add("v", [o], [x, y], lambda e: e.tensor_tensor(o["ap"], x["ap"], y["ap"], op), vcost(o, x, 1 if x["ps"] or y["ps"] else 2))
 
     def ts(o, x, s1, op0, s2=None, op1=None):
         if op1 is None:
-            add("v", [o], [x, s1], lambda e: e.tensor_scalar(o["ap"], x["ap"], val(s1), None, op0))
+            add("v", [o], [x, s1], lambda e: e.tensor_scalar(o["ap"], x["ap"], val(s1), None, op0), vcost(o, x))
         else:
-            add("v", [o], [x, s1, s2], lambda e: e.tensor_scalar(o["ap"], x["ap"], val(s1), val(s2), op0, op1))
+            add("v", [o], [x, s1, s2], lambda e: e.tensor_scalar(o["ap"], x["ap"], val(s1), val(s2), op0, op1), vcost(o, x))
 
     def whole(o, x):
         ts(o, x, MAGIC, OP.add, MAGIC, OP.subtract)
 
     def cp(o, x):
-        add("v", [o], [x], lambda e: e.tensor_copy(o["ap"], x["ap"]))
+        add("v", [o], [x], lambda e: e.tensor_copy(o["ap"], x["ap"]), vcost(o, x))
 
     def ms(o, c):
-        add("v", [o], [], lambda e: e.memset(o["ap"], c))
+        add("v", [o], [], lambda e: e.memset(o["ap"], c), vcost(o, o))
 
     def tr(o, x):
-        add("v", [o], [x], lambda e: e.transpose(o["ap"], x["ap"]))
+        add("v", [o], [x], lambda e: e.transpose(o["ap"], x["ap"]), vcost(o, x))
 
     def scan(o, d0, d1, op0, op1):
-        add("v", [o], [d0, d1], lambda e: e.tensor_tensor_scan(o["ap"], d0["ap"], d1["ap"], 0.0, op0, op1))
+        add("v", [o], [d0, d1], lambda e: e.tensor_tensor_scan(o["ap"], d0["ap"], d1["ap"], 0.0, op0, op1), vcost(o, d1))
 
-    def negsum(o, x):
-        add("v", [o], [x], lambda e: e.tensor_reduce(o["ap"], x["ap"], AX.X, OP.add, negate=True))
+    def rowsum(o, x, negate=True):
+        add("v", [o], [x], lambda e: e.tensor_reduce(o["ap"], x["ap"], AX.X, OP.add, negate=negate), vcost(o, x, 1))
 
     def act(o, x, f=AF.Identity, bias=0.0, scale=1.0, acc=None):
+        cost = 0.065 + GA * CY * x["n"] if "o" in x else 0.09 + CY * x["n"]
         if acc is None:
-            add("s", [o], [x], lambda e: e.activation(o["ap"], x["ap"], f, bias=bias, scale=scale))
+            add("s", [o], [x, bias], lambda e: e.activation(o["ap"], x["ap"], f, bias=val(bias), scale=scale), cost)
         else:
-            add("s", [o, acc], [x], lambda e: e.activation(o["ap"], x["ap"], f, scale=scale, accum_out=acc["ap"]))
+            add("s", [o, acc], [x], lambda e: e.activation(o["ap"], x["ap"], f, scale=scale, accum_out=acc["ap"]), cost + 0.02)
 
-    def mm(o, pairs, start=True, stop=True):
-        def fn(e):
+    def mm(o, pairs, start=True, stop=True, grp=None):
+        def fn(e, first=start, final=stop):
             last = None
             for i, (l, r) in enumerate(pairs):
-                last = e.matmul(o["ap"], l["ap"], r["ap"], start and i == 0, stop and i == len(pairs) - 1)
+                last = e.matmul(o["ap"], l["ap"], r["ap"], first and i == 0, final and i == len(pairs) - 1)
             return last
-        add("p", [o], [x for p in pairs for x in p], fn)
+        cost = sum(PF + 0.5 * CY * max(64, r["n"]) * (1 if r["two"] else 4) for l, r in pairs)
+        add("p", [o], [x for p in pairs for x in p], fn, cost, grp=grp)
 
     def iota(o, pat, base=0, cm=0, fl=True):
+        cost = 0.13 + 2 * CY * o["n"]
         if fl:
-            add("g", [o], [], lambda e: e.iota(o["ap"], pat, base, cm, allow_small_or_imprecise_dtypes=True))
+            add("g", [o], [], lambda e: e.iota(o["ap"], pat, base, cm, allow_small_or_imprecise_dtypes=True), cost)
         else:
-            add("g", [o], [], lambda e: e.iota(o["ap"], pat, base, cm))
+            add("g", [o], [], lambda e: e.iota(o["ap"], pat, base, cm), cost)
 
-    def dma(q, outs, ins, o, i, sem):
-        add(q, outs, ins, lambda e: e.dma_start(o, i), (sem, 16))
+    def dma(q, outs, ins, o, i, sem, lat):
+        add(q, outs, ins, lambda e: e.dma_start(o, i), 0.1, (sem, 16), lat=lat)
 
-    sent = [0]
+    sent, sends = [0], []
 
-    def send(m, src, to="hn"):
+    def send(m, src, to="hn", cost=0.3):
         def fn(e):
             ap = message(T, m, rank, rank, near)[0]
             hs = help_[m // 8][rank]
             if hs and "h" in to:
-                sent[0] += fan(e, T, topo, core, [(h, ap) for h, _ in hs], ap, T.sem["rl%d" % m])
+                sent[0] += fan(e, T, topo, core, [(h, ap) for h, _ in hs], ap, T.sem["rl%d" % m],
+                               relay_mask(T, topo, m, rank, near, help_))
             if near[rank] and "n" in to:
-                sent[0] += fan(e, T, topo, core, [(cores[r], message(T, m, rank, r, near)[1]) for r in near[rank]],
+                sent[0] += fan(e, T, topo, core, [(cores[r], message(T, m, rank, r, near)[1]) for r in near_by(m, rank, near, help_)[None]],
                                ap, T.sem[near_sem(rank, near, m)])
-        add("g", [], [src], fn, "none")
+        sends.append(add("g", [], [src], fn, cost * len(to), "none", after=[(j, 0.0) for j in sends[-1:]]))
+        return sends[-1]
 
     col = lambda name, j: a(name, j, j + 1)
     v80, kv80 = a("BS", 0, 80), a("BS", 80, 160)
     cs = lambda j: a("CS", 128 * j, 128 * j + 128)
-    half, quart, n8k, n24, cdv = [cs(j) for j in range(5)]
+    n8k, n24, cdv, i4k, mid_r, mid_l, half, quart = [cs(j) for j in range(8)]
     ee = lambda j: a("EE", 128 * j, 128 * j + 128)
     thirds = [(0, 512), (512, 1024), (1024, V)]
-    banks = ["PD0", "PD1", "PD2", "PD3", "PU"]
+    pieces = lambda lo, hi, n: [(x, min(x + n, hi)) for x in range(lo, hi, n)]
 
-    def colsum(src, lo, npat, po, j):
-        mm(a("PU", po, po + 8 * npat), [(a("ID"), a(src, lo + i, lo + 128 * npat, 16)) for i in range(4 * j, 4 * j + 4)],
-           j == 0, j == 3)
+    def colsum(ps, at, src, u0, u1, grp, one=None):
+        for j in range(4):
+            mm(a(ps, at, at + 8 * (u1 - u0)), [(one or a("ID"), a(src, 128 * u0 + i, 128 * u1, 16)) for i in range(4 * j, 4 * j + 4)], grp=grp)
+            in_row("p")
 
-    def finish(npat, dst):
-        scan(a("SC", 0, 8 * npat), a("M8", 0, 8 * npat), a("PU", 0, 8 * npat), OP.mult, OP.add)
-        ts(a("SND", dst, dst + npat), a("SC", 7, 8 * npat, 8), -1.0, OP.mult)
-
-    def absent(ps, w, lo, hi):
-        mm(a(ps, 0, hi - lo), [(cdv, a("ONES", 0, hi - lo)), (n24, a(w, lo, hi))])
+    def absent(ps, at, w, lo, hi):
+        mm(a(ps, at, at + hi - lo), [(cdv, a("ONES", 0, hi - lo)), (n24, a(w, lo, hi))])
 
     def chunks_of(t):
         n = KS[t] - EV[t]
         nch = max(min(4, (n + 2) // 3), (n + 3) // 4)
         return [(EV[t] + n * i // nch, EV[t] + n * (i + 1) // nch) for i in range(nch)]
 
+    def unwrapped(k0, k1):
+        cuts = [k0] + [k for k in range(k0 + 1, k1) if k % NP == 0] + [k1]
+        return list(zip(cuts, cuts[1:]))
+
     def roots(w, i, k0, k1):
-        mm(a("PD%d" % (i % 4), 0, 128 * (k1 - k0)), [(a("ID"), a(w if k1 <= NP else "RT", 128 * k0, 128 * k1))], True, False)
+        for n, (x0, x1) in enumerate(unwrapped(k0, k1)):
+            mm(a("PD%d" % (i % 4), 128 * (x0 - k0), 128 * (x1 - k0)),
+               [(a("ID"), a(w, 128 * (x0 % NP), 128 * (x0 % NP + x1 - x0)))], n == 0, False)
 
     def roots_ahead(w, t):
         for i, (k0, k1) in enumerate(chunks_of(t)[:4]):
             roots(w, i, k0, k1)
 
-    dma("y", [a("W0", 0, X)], [], T.W0[:, 0:X], T.w[:, 0:X], "lw0")
-    dma("s", [a("W0", X, V)], [], T.W0[:, X:V], T.w[:, X:V], "lw1")
+    def dead_term(t):
+        for ps, mid_, big in (("PR", mid_r, i4k), ("PL", mid_l, a("ID"))):
+            mm(a(ps, 0, 80), [(mid_, a("ONES", 0, 80))] + ([(big, a("DM"))] if t > 1 else []), True, False)
+
+    def swap(ps, lo):
+        for par in range(2):
+            mm(a(ps, par, 80, 2), [(ee(2 * par + q), a("RL", lo + q, lo + 80, 2)) for q in range(2)], False, par == 1)
+
+    def turn(src, at, lo, hi=V):
+        for x0, x1 in pieces(lo, max(lo, min(hi, V - FINE)), 256) + pieces(max(lo, V - FINE), hi, 128):
+            tr(a("TL", at + x0, at + x1), a(src, x0, x1))
+
+    dma("y", [a("W0", 0, X)], [], T.W0[:, 0:X], T.w[:, 0:X], "lw0", 2.2)
+    dma("s", [a("W0", X, V)], [], T.W0[:, X:V], T.w[:, X:V], "lw1", 2.8)
     for i, (lo, hi) in enumerate(thirds):
-        dma("y", [a("WA", WT + lo, WT + hi)], [], T.WA[:, WT + lo:WT + hi], T.kids[:, lo:hi], "lk%d" % i)
+        dma("y", [a("WA", WT + lo, WT + hi)], [], T.WA[:, WT + lo:WT + hi], T.kids[:, lo:hi], "lk%d" % i, 3.5 + i)
+        in_row("y")
     iota(col("PI", 0), [[0, 1]], 0, 1, False)
     iota(a("J"), [[1, 128]])
     iota(a("TH", 0, 65), [[0, 13], [1, 5]])
     iota(a("SBP0", 0, 25), [[256, 5], [-(2 * V - 16), 5]], 3 * (2 * V - 16) + 63, 16)
     iota(a("LC", 0, 75), [[2 * V, 3], [256, 5], [16, 5]], V + 15, 16)
-    iota(a("RF", 0, 15), [[0, 3], [16, 5]])
-    send(8, a("W0", 0, X), "h")
+    ghosts = [send(8, a("W0", 0, X), "h", 3.0)]
     ms(a("M8"), 1.0)
     ms(a("M16"), 0.0)
     ms(a("KT"), 0.0)
@@ -295,21 +426,27 @@ def rank_program(g, core, T, topo):
     ts(col("PI", 3), p0, 3, OP.arith_shift_right, 1, OP.bitwise_and)
     ts(col("PI", 4), p0, 4, OP.arith_shift_right, 1, OP.bitwise_and)
     ts(col("PI", 5), p0, 1, OP.bitwise_and)
-    ms(a("M8", 0, 240, 8), 0.0)
+    ts(col("PI", 6), p0, 31, OP.bitwise_and)
+    ms(a("M8", 0, 512, 8), 0.0)
     ms(a("M16", 0, 64, 16), 1e9)
-    cp(a("PF", 0, 6), a("PI", 0, 6))
+    cp(a("PF", 0, 7), a("PI", 0, 7))
     ms(a("D1"), -80.0)
     ms(a("PEN0"), 2.0 ** 18)
-    pp, pa, pg, phi, hi_, odd = [col("PF", j) for j in range(6)]
+    pp, pa, pg, phi, hi_, odd, p32 = [col("PF", j) for j in range(7)]
     ts(a("ID"), a("J"), pp, OP.is_equal)
+    ts(a("ID32"), a("J"), pp, OP.is_equal)
     ts(col("PG", 0), hi_, -32.0, OP.mult, 16.0, OP.add)
     ts(col("PG", 1), pg, -256.0, OP.mult)
     ts(col("PG", 2), phi, -1.0, OP.mult, 1.0, OP.add)
     ts(col("PG", 3), hi_, -1.0, OP.mult, 1.0, OP.add)
     ts(col("PG", 4), phi, 32.0, OP.mult, 15.0, OP.add)
+    ts(col("PG", 9), p32, -5.0, OP.add, 1.0 / 6, OP.mult)
+    ts(col("PG", 12), pa, 16.0, OP.mult, 31.5, OP.add)
     ts(a("TF", 0, 4), a("J", 0, 4), 16.0, OP.mult, 64 * MID - 31.5, OP.add)
     ts(v80, a("J", 0, 80), 16.0, OP.mult, pa, OP.add)
     tt(col("PG", 5), col("PG", 0), pp, OP.add)
+    whole(col("PG", 10), col("PG", 9))
+    ts(col("PG", 11), col("PG", 10), 4.0, OP.mult, MAGIC, OP.add)
     ts(a("CC", 0, 4), a("TF", 0, 4), pa, OP.add, 1.0 / 64, OP.mult)
     ts(a("TF", 4, 6), a("J", 0, 2), 0.0, OP.mult, odd, OP.add)
     cp(a("TF", 6, 8), a("J", 0, 2))
@@ -317,11 +454,11 @@ def rank_program(g, core, T, topo):
     ts(a("SBP0", 0, 25), a("SBP0", 0, 25), col("PG", 1), OP.add)
     ts(a("BG"), a("TF", 4, 8), 16.0, OP.mult, col("PG", 4), OP.add)
     whole(a("TF", 20, 24), a("TF", 16, 20))
-    for h in range(4):
+    for h in (0, 2, 3):
         ts(a("PEN0", 30 - 10 * h, 40 - 10 * h), a("J", 0, 10), 0.0, OP.mult, col("CC", h), OP.add)
     ms(a("SBP0", 4, 25, 5), 0.0)
     ts(a("TF", 8, 12), a("TF", 20, 24), 6.0, OP.is_ge, -4.0, OP.mult)
-    ts(a("TF", 16, 20), a("TF", 20, 24), 6.0, OP.mult, 5.0, OP.add)
+    ts(a("TF", 24, 28), a("TF", 20, 24), 6.0, OP.mult, 5.0, OP.add)
     for j, (tgt, msk) in enumerate([(pp, col("PG", 3)), (col("PG", 5), col("PG", 3)), (col("PG", 5), hi_), (pp, hi_)]):
         ts(ee(j), a("J"), tgt, OP.is_equal, msk, OP.mult)
     for k in range(NP):
@@ -329,146 +466,111 @@ def rank_program(g, core, T, topo):
         if k in (0, 1, 4, 6, 8):
             act(a("M", 128 * k, 128 * k + 128), own, scale=-1.0, acc=col("SND", k))
         else:
-            negsum(col("SND", k), own)
-    send(0, a("SND", 0, 10))
-    send(8, a("W0", 0, X), "n")
+            rowsum(col("SND", k), own)
+    sums = send(0, a("SND", 0, 10))
+    ghosts.append(send(8, a("W0", 0, X), "n"))
     iota(a("JG"), [[1, 8], [0, 16]])
     iota(a("CI"), [[4097, V]], V * 4097)
+    ops[-1]["after"].append((sends[-1], 0.0))
     ts(ee(4), a("J"), pp, OP.is_equal)
-    ts(ee(5), a("J"), pp, OP.is_equal, 4096.0, OP.mult)
     ts(a("NEG"), a("ID"), -1.0, OP.mult)
     ms(a("KP", Z, WT), DV)
     ms(a("W0", Z, WT), 0.0)
     for i, (lo, hi) in enumerate(thirds):
         act(a("PD%d" % i, 0, hi - lo), a("W0", lo, hi), AF.Relu, bias=DV, scale=-DV)
+    act(a("ONES", 0, 512), a("W0", 0, 512), bias=1.0, scale=0.0)
+    tt(a("TF", 12, 16), a("TF", 8, 12), a("TF", 24, 28), OP.add)
+    ts(a("LC", 0, 75), a("LC", 0, 75), col("PG", 1), OP.add)
+    ts(a("TH", 0, 65), a("TH", 0, 65), -0.25, OP.mult, 0.5, OP.add)
+    iota(a("TH", 72, 162), [[0, 3], [8, 6], [0, 5]], 21)
+    ts(a("TH", 75, 162, 5), a("TH", 75, 162, 5), -1.125, OP.add)
+    ts(a("TH", 76, 162, 5), a("TH", 76, 162, 5), -2.0, OP.add)
+    ts(col("PG", 13), col("PG", 10), 8.0, OP.mult, MAGIC + V / 64, OP.add)
+    ts(col("PG", 15), odd, -16.0, OP.mult, 31.5, OP.add)
+    ts(col("PG", 14), pa, 32.0, OP.mult, col("PG", 15), OP.add)
+    for nm, s_, x in (("SBP0", 2, V + 47.5), ("LC", 3, V + 31.5)):
+        ts(a("TF", 0, 5), a("J", 0, 5), 512.0, OP.mult, x, OP.add)
+        ts(a(nm, s_, 25, 5), a("TF", 0, 5), col("PG", 14), OP.add)
+    ts(a("PEN0", 20, 30), a("PEN0", 30, 40), 0.5, OP.add)
+    ts(a("GR"), a("TF", 12, 16), 63.0, OP.min)
+    ms(a("NHT"), 0.0)
+    ts(a("D1", 33, 54, 5), a("BS", 0, 5), 320.0, OP.add)
+    ms(a("D1", 34, 55, 5), 0.0)
+    ts(col("PG", 6), pp, 0.0, OP.is_equal, 4096.0 * Z, OP.mult)
+    ts(col("PG", 7), pp, 1.0, OP.is_equal, float(Z), OP.mult)
+    ts(n24, a("ID"), -2.0 ** 24, OP.mult)
+    tt(col("PG", 8), col("PG", 6), col("PG", 7), OP.add)
+    for j, x in enumerate((-2.0 ** 19, 2.0 ** 19)):
+        ts(a("BO", 128 * j, 128 * j + 128), a("JG"), pg, OP.is_equal, x, OP.mult)
+    ts(cdv, a("J"), 0.0, OP.mult, col("PG", 8), OP.add)
+    for c_, x in ((n8k, -8192.0), (i4k, 4096.0), (mid_r, 1280.0), (mid_l, 0.3125), (half, 0.5), (quart, -0.25)):
+        ts(c_, a("ID"), x, OP.mult)
+    ms(a("SGN"), 1.0)
+    ts(kv80, v80, float(WT), OP.add)
+    ms(a("HD"), -80.0)
+    for w in ("W1", "ONES", "WB"):
+        ms(a(w, Z, WT), 0.0)
+    ts(a("HD", 3, 40, 8), a("J", 0, 5), 16.0, OP.mult, 240.0, OP.add)
+    ts(a("HD", 7, 40, 8), a("J", 0, 5), 16.0, OP.mult, 240.0, OP.add)
+    act(a("B0"), a("W0", 0, 400), scale=0.0)
+    act(a("B1"), a("W0", 0, 400), scale=0.0)
+    for lo, hi in pieces(512, Z, 512):
+        act(a("ONES", lo, hi), a("W0", (lo - 512) // 2, (lo - 512) // 2 + hi - lo), bias=1.0, scale=0.0)
+    for lo, hi in pieces(V, WT, 432):
+        act(a("LT", lo, hi), a("W0", 0, hi - lo), scale=0.0)
 
-    def late_constants():
-        tt(a("TF", 12, 16), a("TF", 8, 12), a("TF", 16, 20), OP.add)
-        ts(a("REP", 0, 15), a("RF", 0, 15), pa, OP.add)
-        ts(a("LC", 0, 75), a("LC", 0, 75), col("PG", 1), OP.add)
-        ts(a("TH", 0, 65), a("TH", 0, 65), -0.25, OP.mult, 0.5, OP.add)
-        ts(a("GR"), a("TF", 12, 16), 63.0, OP.min)
-        ts(a("TF", 24, 29), a("SBP0", 3, 25, 5), -31.5, OP.add, 1.0 / 64, OP.mult)
-        ms(a("NHT"), 0.0)
-        ts(a("D1", 33, 54, 5), a("BS", 0, 5), 320.0, OP.add)
-        ms(a("D1", 34, 55, 5), 0.0)
-        ts(col("PG", 6), pp, 0.0, OP.is_equal, 4096.0 * Z, OP.mult)
-        ts(col("PG", 7), pp, 1.0, OP.is_equal, float(Z), OP.mult)
-        ts(n24, a("ID"), -2.0 ** 24, OP.mult)
-        tt(col("PG", 8), col("PG", 6), col("PG", 7), OP.add)
-        ts(a("BO"), a("JG"), pg, OP.is_equal, -2.0 ** 19, OP.mult)
-        ts(cdv, a("J"), 0.0, OP.mult, col("PG", 8), OP.add)
-
-    def end_constants():
-        ts(kv80, v80, float(WT), OP.add)
-        ms(a("HD"), -80.0)
-        for w in ("W1", "ONES"):
-            ms(a(w, Z, WT), 0.0)
-        ts(half, a("ID"), 0.5, OP.mult)
-        ts(ee(6), a("ID"), 0.5, OP.mult)
-        ts(quart, a("ID"), -0.25, OP.mult)
-        ts(n8k, a("ID"), -8192.0, OP.mult)
-        ts(a("HD", 3, 40, 8), a("J", 0, 5), 16.0, OP.mult, 240.0, OP.add)
-        ts(a("HD", 7, 40, 8), a("J", 0, 5), 16.0, OP.mult, 240.0, OP.add)
-        ms(a("WB", Z, WT), 0.0)
-
-    def step_lists():
-        bc = a("BC", 0, 36)
-        ms(bc, 70.0)
-        ms(a("BC", 36, 72), 1.0)
-        ts(a("TG", 0, 2), a("BS", 0, 2), -2.5, OP.add, 1.0 / 6, OP.mult)
-        ms(a("E1", 70, 80), 1e9)
-        ms(a("E1", 80, 96), -1e9)
-        ms(a("E1", 10, 70), 0.0)
-        whole(a("TG", 2, 4), a("TG", 0, 2))
-        ms(a("BC", 36, 72, 6), 0.0)
-        marks = [(6 * i + s_, blk) for i, row in enumerate(STEPS) for s_, blk in enumerate(row) if blk != 7]
-
-        def mark(k):
-            for x, blk in marks[:k]:
-                ms(col("BC", x), 10.0 * blk)
-            del marks[:k]
-
-        mark(2)
-        ts(a("TG", 4, 6), a("TG", 2, 4), -6.0, OP.mult)
-        ts(a("TG", 8, 10), a("TG", 2, 4), 2.0, OP.mult)
-        ts(a("TG", 10, 12), a("TG", 2, 4), 2.0, OP.mult, 1.0, OP.add)
-        mark(2)
-        tt(a("TG", 6, 8), a("TG", 4, 6), a("BS", 0, 2), OP.add)
-        mark(4)
-        hot = lambda ph: a("BC", 72 + 36 * ph, 108 + 36 * ph)
-        for ph in range(2):
-            ts(hot(ph), a("SI"), col("TG", 6 + ph), OP.is_equal)
-        mark(len(marks))
-        rest = [lambda ph=ph: tt(hot(ph), hot(ph), bc, OP.mult) for ph in range(2)]
-        rest += [lambda ph=ph: scan(hot(ph + 2), a("BC", 36, 72), hot(ph), OP.mult, OP.add) for ph in range(2)]
-        rest += [lambda ph=ph, par=par: ts(a("TG", 16 + 2 * par + ph, 40, 4), a("BC", 149 + 36 * ph, 180 + 36 * ph, 6),
-                                           col("TG", 8 + 2 * par + ph), OP.add) for ph in range(2) for par in range(2)]
-        rest += [lambda: ts(a("TG", 40, 64), a("TG", 16, 40), 70.0, OP.is_lt), lambda: cp(a("PA"), a("TG", 16, 40)),
-                 lambda: tt(a("TG", 64, 88), a("TG", 40, 64), a("TG", 16, 40), OP.mult), lambda: cp(a("PB"), a("TG", 64, 88))]
-        later.extend(rest)
-
-    def dead_term():
-        mm(a("PR", 0, 80), [(ee(5), a("DM"))], True, False)
-        mm(a("PL", 0, 80), [(ee(4), a("DM"))], True, False)
-
-    def swap(ps, lo):
-        for par in range(2):
-            mm(a(ps, par, 80, 2), [(ee(2 * par + q), a("RL", lo + q, lo + 80, 2)) for q in range(2)], False, par == 1)
-
-    later = []
-
-    def turn_last(src, at, lo, k):
-        cut = V - 128 * k
-        if cut > lo:
-            tr(a("TL", at + lo, at + cut), a(src, lo, cut))
-        for x in range(cut, V, 128):
-            later.append(lambda x=x: tr(a("TL", at + x, at + x + 128), a(src, x, x + 128)))
+    def end_table(t):
+        if t == 1:
+            iota(a("WA", 0, WT), [[1, WT]], 0, 0, False)
+        elif t == 2:
+            iota(a("WB", 0, Z), [[4096, Z]])
+        else:
+            add("g", [a("AA")], [a("ONES", 0, 2048)],
+                lambda en: en.affine_select(T.AA[:, 0:2048], T.ONES[:, 0:2048], [[-1000, 16], [-16, 8], [999, 16]],
+                                            OP.is_equal, 0.0, 0, 1), 3.9)
+        ops[-1]["after"].append((sends[-1], 0.0))
 
     for e in range(EP):
         W = "W%d" % e
         Wt = a(W, 0, WT)
         kin = "WA" if e == 0 else "K2"
         ko = WT if e == 0 else 0
+        late = 3.0 * (1 - e)
         cp(a("SBP", 0, 25), a("SBP0", 0, 25))
         cp(a("PEN", 0, 70), a("PEN0", 0, 70))
-        ts(a("DM"), a("J", 0, 80), 0.0, OP.mult, 0.3125, OP.add)
-        tt(a("E1", 0, 10), a("SND", 160 * e, 160 * e + 10), a("PEN0", 30, 40), OP.add)
-        if e > 0:
-            thirds = [(0, 256), (256, 768), (768, V)]
-            for lo, hi in thirds:
-                act(a("G1", lo, hi), ind(a("WB"), a("FL", 80 + lo // 16, 80 + hi // 16)))
-        kids2 = lambda lo, hi: tt(a("K2", lo, hi), ind(a("WA"), a("FL", lo // 16, hi // 16)), a("G1", lo, hi), OP.add)
+        part = lambda x, lo=0: mm(a("PU", lo, lo + x["n"]), [(a("ID32"), x)], grp="sum%d" % len(sends))
+        part(a("SND", 160 * e, 160 * e + 10))
+        part(a("PEN0", 30, 40))
         for i, (lo, hi) in enumerate(thirds):
             if e > 0:
-                absent("PD%d" % i, W, lo, hi)
-                if i == 0:
-                    kids2(lo, hi)
-                if i < 2:
-                    kids2(*thirds[i + 1])
-            tt(a("KP", lo, hi), a(kin, ko + lo, ko + hi), a("PD%d" % i, 0, hi - lo), OP.max)
-            act(a("G0", lo, hi), a("KP", lo, hi), bias=-C0, scale=1.0 / 4096)
-            if e == 0 and i == 0:
-                late_constants()
-            if i == 1:
-                tr(a("TL", *thirds[0]), a("G0", *thirds[0]))
-        turn_last("G0", 0, thirds[0][1], LATE[0] * e)
-        dead_term()
+                absent("PD%d" % i, 0, W, lo, hi)
+            for x0, x1 in pieces(lo, hi, 256):
+                if e > 0:
+                    act(a("G1", x0, x1), ind(a("WB"), a("FL", 80 + x0 // 16, 80 + x1 // 16)))
+                    tt(a("K2", x0, x1), ind(a("WA"), a("FL", x0 // 16, x1 // 16)), a("G1", x0, x1), OP.add)
+                tt(a("KP", x0, x1), a(kin, ko + x0, ko + x1), a("PD%d" % i, x0 - lo, x1 - lo), OP.max)
+                act(a("G0", x0, x1), a("KP", x0, x1), bias=-C0, scale=1.0 / 4096)
+        turn("G0", 0, 0)
+        dead_term(1)
         roots_ahead(W, 1)
-        act(a("RT", 0, V), a(W, 0, V))
-        act(a("RT", V, 2 * V), a(W, 0, V))
-        if e > 0:
-            dma("y", [a("WA", WT, WT + V)], [a("K2")], T.WA[:, WT:WT + V], T.K2[:, 0:V], "ck")
-        else:
-            end_constants()
-            act(a("ONES", 0, 512), a("W0", 0, 512), bias=1.0, scale=0.0)
-            act(a("B0"), a("W0", 0, 400), scale=0.0)
-            act(a("B1"), a("W0", 0, 400), scale=0.0)
-        gh = lambda q: ((rank - q) % NR - 1) * X
-        for q, cnt in zip(src_near, cnt_near):
-            arrive([a(W, V + gh(q), V + gh(q) + X)], near_sem(q, near, 8 + e), cnt)
+        for lo, hi in pieces(0, V, 320):
+            act(a("RT", lo, hi), a(W, lo, hi))
+        gh = lambda q: V + ((rank - q) % NR - 1) * X
         for j in range(2):
-            arrive([a(W, V + gh(q), V + gh(q) + X) for q in src_far[j]], "%s%d" % (sem_far[j], 8 + e), cnt_far[j])
+            arrive([a(W, gh(q), gh(q) + X) for q in src_far[j]], "%s%d" % (sem_far[j], 8 + e), cnt_far[j],
+                   (sums, FAR + late + GF[e] + STEP * j))
+        for k, q in enumerate(src_near):
+            arrive([a(W, gh(q), gh(q) + X)], near_sem(q, near, 8 + e), cnt_near[k], (sums, FAR + late + GN[e] + STEP * k))
+        kinds = [src_near, src_far[0] + src_far[1]][::-1 if e else 1]
+        for ps, two in zip(("PC", "PD3", "PD3"), [kind[i:i + 2] for kind in kinds for i in range(0, len(kind), 2)]):
+            for i, q in enumerate(two):
+                absent(ps, X * i, W, gh(q), gh(q) + X)
+            for i, q in enumerate(two):
+                for x0 in (0, 128):
+                    tt(a("KP", gh(q) + x0, gh(q) + x0 + 128), a("CI", gh(q) - V + x0, gh(q) - V + x0 + 128),
+                       a(ps, X * i + x0, X * i + x0 + 128), OP.max)
+        for lo, hi in pieces(0, V, 320):
+            act(a(W, WT + lo, WT + hi), a(W, lo, hi), scale=2.0)
 
         for t in range(1, RO + 1):
             m = RO * e + t - 1
@@ -476,42 +578,23 @@ def rank_program(g, core, T, topo):
             land = lambda k: a("LAND", land_at(m, k), land_at(m, k) + n)
             nn, nf = len(src_near), len(src_far[0])
             for k in range(nn):
-                arrive([land(k)], near_sem(src_near[k], near, m), cnt_near[k])
+                arrive([land(k)], near_sem(src_near[k], near, m), cnt_near[k], (sums, NEAR + STEP * k))
             for j in range(2):
-                arrive([land(nn + j * nf + k) for k in range(nf)], "%s%d" % (sem_far[j], m), cnt_far[j])
-
-            def turns(k):
-                for _ in range(min(k, len(later))):
-                    later.pop(0)()
-
-            e1, e2, e3, e4 = a("E1", 0, n), a("E2", 0, n), a("E3", 0, n), a("E4", 0, n)
-            if nn == 3:
-                tt(e1, e1, land(0), OP.add)
-                turns(1)
-                tt(e1, e1, land(1), OP.add)
-                turns(1)
-                mid_, last = (land(2), land(3)), land(4)
-            else:
-                tt(e1, e1, land(0), OP.add)
-                turns(1)
-                mid_, last = (land(1), land(2)), e4
-            tt(e3, mid_[0], mid_[1], OP.add)
-            turns(1)
-            tt(e2, e1, e3, OP.add)
-            if nn != 3:
-                tt(e4, land(3), land(4), OP.add)
-            turns(1)
+                arrive([land(nn + j * nf + k) for k in range(nf)], "%s%d" % (sem_far[j], m), cnt_far[j],
+                       (sums, FAR + STEP * j + (late if t == 1 else 0)))
+            for k in range(NR - 2):
+                part(land(k))
+            last, at = land(NR - 2), land_at(m, NR - 2)
             u = lambda h: a("US", 10 * (t - 1 - h), 10 * (t - h))
             c = lambda i: a("US", 10 * (t + i), 10 * (t + i + 1))
             mmx = lambda j: a("MM", 10 * j, 10 * j + 10)
             kt = lambda par: a("KT", 32 * par + 5, 32 * par + 30, 6)
             if t == 1:
-                pn = last["r"][0]
                 for par in range(2):
-                    tt(kt(par), a("E2", par, 10, 2), a(pn[0], pn[1] + par, pn[1] + 10, 2), OP.add)
+                    tt(kt(par), a("PU", par, 10, 2), a("LAND", at + par, at + 10, 2), OP.add)
+                tt(a("US", 0, n), a("PU", 0, n), last, OP.add)
             else:
-                tt(a("US", 0, n), e2, last, OP.add)
-                turns(1)
+                tt(a("US", 0, n), a("PU", 0, n), last, OP.add)
                 if t == 2:
                     tt(mmx(0), u(1), c(0), OP.max)
                     xs = ("US", 10)
@@ -533,41 +616,24 @@ def rank_program(g, core, T, topo):
             def dropped():
                 ts(a("NHT", 5 - t, 40, 4), c(0) if t == 2 else mmx(1) if t == 3 else a("CM", 0, 10), 0.0, OP.is_gt)
 
-            fill = [lambda: tt(a("CM", 0, 10), mmx(1), c(2), OP.max), dropped,
-                    lambda: scan(a("HS"), a("NHT"), a("HD"), OP.mult, OP.add),
-                    lambda: ts(a("HT", 0, 5), a("HS", 3, 40, 8), col("PG", 2), OP.mult, pa, OP.add),
-                    lambda: ts(a("HT", 8, 13), a("HS", 7, 40, 8), phi, OP.mult),
-                    lambda: tt(a("HT", 16, 21), a("HT", 0, 5), a("HT", 8, 13), OP.add),
-                    lambda: cp(a("OFB", 0, 5), a("HT", 16, 21))] if t == RO else []
-
-            def between():
-                if fill:
-                    fill.pop(0)()
-                turns(1)
-
-            between()
             tr(a("T1"), a("KT"))
-            between()
             scan(a("S1"), a("M16"), a("T1"), OP.add, OP.min)
-            between()
             nb = 32 if t == 1 else 64
             best = ind(a("S1"), a("BG", 0, nb // 16))
-            whole(a("BI", 0, nb), best)
-            between()
+            ts(a("BI", 0, nb), best, MAGIC, OP.add, col("PG", 9 + 2 * t) if t < 3 else MAGIC, OP.subtract)
             tt(a("BJ", 0, nb), best, a("BI", 0, nb), OP.subtract)
-            between()
             tr(a("C6", 0, nb), a("BJ", 0, nb))
-            between()
-            if t == 1:
-                tt(a("S2", 0, 5), a("C6", 5, 30, 6), a("TF", 24, 29), OP.add)
-                ts(a("OFF", 0, 5), a("S2", 0, 5), 64.0, OP.mult)
-            else:
-                tt(a("GG"), ind(a("C6"), a("GR")), a("TH", 0, 64), OP.is_gt)
-                ts(a("D1", 4, 25, 5), a("C6", 5, 30, 6), 64.0, OP.mult, -31.5, OP.add)
-                scan(a("S2", 0, 55), a("GG", 0, 55), a("D1", 0, 55), OP.mult, OP.add)
-                between()
-                cp(a("OFF", 0, 11), a("S2", 4, 55, 5))
-            turns(len(later))
+            if t < 3:
+                ts(a("OFF", 0, 5), a("C6", 5, 30, 6), 64.0, OP.mult, col("PG", 10 + 2 * t), OP.add)
+            if t > 1:
+                lo = 30 if t == 2 else 0
+                tt(a("GG"), ind(a("C6"), a("GR")), a("TH", 72 * (t == 2), 72 * (t == 2) + 64), OP.is_gt)
+                if t > 2:
+                    act(a("D1", 4, 25, 5), a("C6", 5, 30, 6), bias=-31.5, scale=64.0)
+                scan(a("S2", lo, 55), a("GG", lo, 55), a("D1", lo, 55), OP.mult, OP.add)
+                cp(a("OFF", lo // 5, 11), a("S2", lo + 4, 55, 5))
+            if e > 0 and t == 2:
+                dma("y", [a("WA", WT, WT + V)], [a("K2"), a("OFF")], T.WA[:, WT:WT + V], T.K2[:, 0:V], "ck", 4.0)
             off, offx = a("OFF", 0, 5), a("OFF", 6, 11)
             tl = a("TL", 0, (2 * t - 1) * V)
             old, new = ("B1", "B0") if t % 2 == 0 else ("B0", "B1")
@@ -578,17 +644,10 @@ def rank_program(g, core, T, topo):
             rr, ll = a("RL", 0, 80), a("RL", 80, 160)
             pr, pl = a("PR", 0, 80), a("PL", 0, 80)
             src = ind(tl, off)
-            if t < RO:
-                whole(rr, src)
-                swap("PR", 0)
-                tt(ll, src, rr, OP.subtract)
-                swap("PL", 80)
-                ts(lu(0, 80), pr, float(Z), OP.min)
-            else:
-                whole(rr, src)
-                tt(ll, src, rr, OP.subtract)
-                swap("PL", 80)
-                swap("PR", 0)
+            whole(rr, src)
+            swap("PR", 0)
+            tt(ll, src, rr, OP.subtract)
+            swap("PL", 80)
 
             def expanded():
                 cp(a("XU", 80 * (t - 2), 80 * (t - 1)), ind(a(old), offx))
@@ -596,135 +655,115 @@ def rank_program(g, core, T, topo):
 
             if t < RO:
                 so = 160 * e + XO[t]
-                nu, ks = 10 * (t + 1), KS[t]
+                nu, ks, ev = 10 * (t + 1), KS[t], EV[t]
                 bt, bold = a(new, hp(t), hp(t) + 80), a(new, hp(t - 1), 400)
-                rep = a("REP", 0, 5 * t)
-                ev = EV[t]
-                mo = lambda k: k if k < ev else k - ks + ev
-
-                def vector_part(k0, k1):
-                    r0 = 128 * (k0 % NP)
-                    tt(a("M", 128 * mo(k0), 128 * (mo(k0) + k1 - k0)), ind(Wt, lu(8 * k0, 8 * k1)),
-                       a("RT", r0, r0 + 128 * (k1 - k0)), OP.min)
-
+                blk = lambda nm, i: a(nm, hp(t - 1 - i), hp(t - 1 - i) + 80)
+                ts(lu(0, 80), pr, float(Z), OP.min)
                 if t == 1:
-                    ts(bt, pr, float(Z), OP.min)
-                    vector_part(0, 1)
                     ts(lu(80, 160), pl, 4096.0, OP.mult, float(Z), OP.min)
                     ts(bold, pl, 4096.0, OP.mult, float(Z), OP.min)
-                    vector_part(1, ev)
-                    tt(a("NEQ", 0, 80), bt, bold, OP.not_equal)
-                else:
-                    ts(a("DZ"), pr, float(Z), OP.is_ge, float(Z), OP.mult)
                     ts(bt, pr, float(Z), OP.min)
-                    vector_part(0, 1)
+                else:
+                    dz = a("PR", 80, 160)
+                    ts(dz, pr, float(Z), OP.is_ge, float(Z), OP.mult)
+                    ts(bt, pr, float(Z), OP.min)
                     ts(a("LB"), pl, 4096.0, OP.mult, float(Z), OP.min)
-                    tt(bold, ind(a("DZ"), rep), a(old, hp(t - 1), 400), OP.max)
-                    vector_part(1, 2)
+                    for i in range(t):
+                        tt(blk(new, i), blk(old, i), dz, OP.max)
                     cp(ind(a(new), offx), a("LB"))
-                    vector_part(2, ev)
                     cp(lu(80, 80 + 80 * t), bold)
-                    tt(a("NEQ", 0, 80 * t), ind(bt, rep), bold, OP.not_equal)
                 chunks = chunks_of(t)
+                sp = chunks[SP[t] - 1][1] if SP[t] else ev
+                pe = ks + TAIL
+                mid = min(pe + LAST, nu)
+                mo = lambda k: k if k < ks else k - mid + sp if k >= mid else k - ks + 36
+                votes = "votes%d" % m
+
+                def counts():
+                    for i in range(t):
+                        tt(a("NEQ", 80 * i, 80 * i + 80), blk(new, i), pr, OP.not_equal)
+                        in_row("v")
+                    for i in range(t if t > 1 else 0):
+                        mm(a("PC", 10 * i, 10 * i + 10), [(a("BO", 128, 256), a("DM", b, 80, 8)) for b in range(8)], i == 0, False)
+                    mm(a("PC", 0, 10 * t), [(a("BO", 0, 128), a("NEQ", b, 80 * t, 8)) for b in range(8)], t == 1, True)
+                    act(a("SND", so + nu, so + nu + 10 * t), a("PC", 0, 10 * t))
+
+                unit = lambda k0, k1: a("M", 128 * mo(k0), 128 * (mo(k0) + k1 - k0))
 
                 def short(i):
                     k0, k1 = chunks[i]
-                    for k in range(k0, k1):
-                        act(a("MS", 128 * k, 128 * k + 128), a("PD%d" % (i % 4), 128 * (k - k0), 128 * (k - k0 + 1)),
-                            AF.Relu, acc=col("SND", so + k))
+                    pd = "PD%d" % (i % 4)
+                    if i < SP[t]:
+                        act(unit(k0, k1), a(pd, 0, 128 * (k1 - k0)), AF.Relu)
+                        in_row("s")
+                    else:
+                        for k in range(k0, k1):
+                            act(a("MS", 128 * k, 128 * k + 128), a(pd, 128 * (k - k0), 128 * (k - k0 + 1)), AF.Relu,
+                                acc=col("SND", so + k))
+                            in_row("s")
 
-                def scalar_part(i):
-                    k0, k1 = chunks[i]
+                for i, (k0, k1) in enumerate(chunks):
                     mk = a("MS", 128 * k0, 128 * k1)
                     act(mk, ind(Wt, lu(8 * k0, 8 * k1)))
+                    in_row("s")
                     if i >= 4:
                         roots(W, i, k0, k1)
                     mm(a("PD%d" % (i % 4), 0, 128 * (k1 - k0)), [(a("NEG"), mk)], False, True)
-                    if i == 1:
-                        mm(a("PC", 0, 10 * t), [(a("BO"), a("NEQ", b, 80 * t, 8)) for b in range(8)])
                     if i:
                         short(i - 1)
-                    if i == len(chunks) - 1:
-                        act(a("SND", so + nu, so + nu + 10 * t), a("PC", 0, 10 * t))
-                        short(i)
-
-                pe = nu - TAIL - TS[t]
-                mid = pe - LAST if mo(pe) > LAST + 4 else ks
-                cuts = sorted(set([ks, mid, pe, nu - TAIL, nu]))
-                for k0, k1 in list(zip(cuts, cuts[1:])):
-                    if k0 % NP + k1 - k0 > 2 * NP:
-                        cuts = sorted(cuts + [k0 - k0 % NP + 2 * NP])
-                steps = [(4 * (k1 - ev) + 3 * (chunks[i - 1][0] - ev if i else 0), 0, i) for i, (k0, k1) in enumerate(chunks)]
-                steps += [(LEAD[t] + 4 * (k1 - ks), 1, (k0, k1)) for k0, k1 in zip(cuts, cuts[1:])]
-                for m0, k1 in ([(0, mid), (mo(mid), pe)] if mid > ks else [(0, pe)]):
-                    steps += [(LEAD[t] + 4 * (k1 - ks) + 5 * j, 2, (m0, mo(k1), j)) for j in range(4)]
-                for _, kind, x in sorted(steps):
-                    if kind == 2:
-                        colsum("M", 128 * x[0], x[1] - x[0], 8 * x[0], x[2])
-                    elif kind:
-                        vector_part(*x)
-                    else:
-                        scalar_part(x)
-                unit = lambda k: a("M", 128 * mo(k), 128 * mo(k) + 128)
-                for k in range(pe, nu - TAIL):
-                    act(unit(k), unit(k), scale=-1.0, acc=col("SND", so + k))
-                w8 = 8 * mo(pe)
+                short(len(chunks) - 1)
+                runs = [(0, 1), (1, ev)][:ev] + pieces(mid, nu, PIECE) + pieces(pe, mid, PIECE) + [(ks, pe)]
+                for i, (k0, k1) in enumerate(sum([unwrapped(*r) for r in runs], [])):
+                    if i == NQ[t]:
+                        counts()
+                    r0 = 128 * (k0 % NP)
+                    tt(unit(k0, k1), ind(Wt, lu(8 * k0, 8 * k1)), a("RT", r0, r0 + 128 * (k1 - k0)), OP.min)
+                    in_row("v")
+                for u0, u1 in ([(sp, mo(nu)), (0, sp)] if SP[t] else [(0, mo(nu))]):
+                    if u1 > u0:
+                        colsum("PU", 8 * u0, "M", u0, u1, votes)
+                w8 = 8 * mo(nu)
                 scan(a("SC", 0, w8), a("M8", 0, w8), a("PU", 0, w8), OP.mult, OP.add)
-                for k in range(nu - TAIL, nu):
-                    negsum(col("SND", so + k), unit(k))
-                ts(a("SND", so, so + ev), a("SC", 7, 8 * ev, 8), -1.0, OP.mult)
-                ts(a("SND", so + ks, so + pe), a("SC", 8 * ev + 7, w8, 8), -1.0, OP.mult)
+                if sp > ev:
+                    ms(a("SGN", 0, ev), -1.0)
+                    tt(a("SND", so, so + sp), a("SC", 7, 8 * sp, 8), a("SGN", 0, sp), OP.mult)
+                else:
+                    ts(a("SND", so, so + ev), a("SC", 7, 8 * ev, 8), -1.0, OP.mult)
+                if mid < nu:
+                    ts(a("SND", so + mid, so + nu), a("SC", 8 * sp + 7, w8, 8), -1.0, OP.mult)
+                w8 = 8 * (mid - pe)
+                colsum("PL", 128, "M", mo(pe), mo(pe) + mid - pe, "last%d" % m)
+                scan(a("SD", 0, w8), a("M8", 0, w8), a("PL", 128, 128 + w8), OP.mult, OP.add)
+                for k in range(ks, pe):
+                    rowsum(col("SND", so + k), unit(k, k + 1))
+                ts(a("SND", so + pe, so + mid), a("SD", 7, w8, 8), -1.0, OP.mult)
+                sums = send(m + 1, a("SND", so, so + NX[t]))
+                if t == RO - 1:
+                    ms(a("SGN", 0, ev), 1.0)
+                if e == 0:
+                    end_table(t)
                 if t == 1:
-                    for i, (lo2, hi2) in enumerate([(0, 256), (256, 768), (768, V)]):
-                        ps = ["PD3", "PL", "PR"][i]
-                        if i < 2:
-                            act(a(ps, 0, hi2 - lo2), a(W, V + lo2, V + hi2), AF.Relu, bias=DV, scale=-DV)
-                        else:
-                            absent(ps, W, V + lo2, V + hi2)
-                        tt(a("KP", V + lo2, V + hi2), a("CI", lo2, hi2), a(ps, 0, hi2 - lo2), OP.max)
-                send(m + 1, a("SND", so, so + NX[t]))
-                if t == 1:
-                    llist = lambda c0, c1: lu(80 + c0, 80 + c1)
+                    for i in range(4):
+                        cp(a("LI", i, 160, 4), a("LU", hp(i // 2) + i % 2, hp(i // 2) + 80, 2))
+                    lists = [lambda c0, c1, x=x: a("LI", x + c0, x + c1) for x in (80, 0)]
                 else:
                     cp(a("LL"), a("LB"))
-                    llist = lambda c0, c1: a("LL", c0, c1)
-                for lo2, hi2 in [(0, 640), (640, V)]:
-                    act(a("G0", lo2, hi2), ind(a("KP"), lu(lo2 // 16, hi2 // 16)), bias=-C0, scale=1.0 / 4096)
-                GV = GVS[t]
-                for lo2, hi2 in [(GV, 896), (896, V)]:
-                    act(a("G1", lo2, hi2), ind(a("KP"), llist(lo2 // 16, hi2 // 16)), bias=-C0, scale=1.0 / 4096)
-                if t == 2:
-                    act(a(W, WT, WT + V), a(W, 0, V), scale=2.0)
-                if e == 0:
-                    if t == 1:
-                        iota(a("WA", 0, WT), [[1, WT]], 0, 0, False)
-                        act(a("ONES", 512, Z), a(W, 512, Z), bias=1.0, scale=0.0)
-                    elif t == 2:
-                        add("g", [a("AA")], [a("ONES", 0, 2048)],
-                            lambda en: en.affine_select(T.AA[:, 0:2048], T.ONES[:, 0:2048], [[-1000, 16], [-16, 8], [999, 16]],
-                                                        OP.is_equal, 0.0, 0, 1))
-                    else:
-                        iota(a("WB", 0, Z), [[4096, Z]])
-                        act(a("LT", V, WT), a(W, V, WT), scale=0.0)
-                ts(a("G1", 0, GV), ind(a("KP"), llist(0, GV // 16)), 1.0 / 4096, OP.mult, -C0, OP.add)
-                ts(a("DM"), bt, float(Z), OP.is_ge, 0.3125, OP.add)
+                    lists = [lu, lambda c0, c1: a("LL", c0, c1)]
+                sl, sr = (2 * t - 1) * V, 2 * t * V
+                for gx, lst, slot in (("G0", lists[0], sr), ("G1", lists[1], sl)):
+                    for lo, hi in pieces(0, V, 256):
+                        if gx == "G1" and lo < GV[t]:
+                            ts(a(gx, lo, hi), ind(a("KP"), lst(lo // 16, hi // 16)), 1.0 / 4096, OP.mult, -C0, OP.add)
+                        else:
+                            act(a(gx, lo, hi), ind(a("KP"), lst(lo // 16, hi // 16)), bias=-C0, scale=1.0 / 4096)
+                            in_row("s")
+                    turn(gx, slot, 0)
+                ts(a("DM"), bt, float(Z), OP.is_ge)
                 if t > 1:
                     tt(a("EQH", 0, 25), a("GG", 1, 26), a("GG", 0, 25), OP.subtract)
                     dropped()
                     tt(a("EQL", 0, 25), a("EQH", 0, 25), a("LC", 25 * (t - 1), 25 * t), OP.mult)
                     expanded()
-                else:
-                    cp(a("SBP", 3, 25, 5), a("LC", 3, 25, 5))
-                    tt(a("US", 0, 10), e2, last, OP.add)
-                dead_term()
-                if t + 1 < RO:
-                    roots_ahead(W, t + 1)
-                else:
-                    for ps in banks[:5 - e]:
-                        mm(a(ps, 0, 384), [(quart, a("ONES", 0, 384))], True, False)
-                sl, sr = (2 * t - 1) * V, 2 * t * V
-                tr(a("TL", sl, sl + GV), a("G1", 0, GV))
-                if t > 1:
                     nh = a("NHT", 5 - t, 40, 4)
                     if t == 3:
                         cp(a("PEN", 50, 60), a("PEN", 40, 50))
@@ -732,132 +771,131 @@ def rank_program(g, core, T, topo):
                     ts(a("PEN", 40, 50), nh, -BIG, OP.mult, 2.0 ** 18, OP.add)
                     tt(a("SBP", 0, 25), a("SBP", 0, 25), a("EQL", 0, 25), OP.max)
                 else:
-                    for j in range(2):
+                    cp(a("SBP", 3, 25, 5), a("LC", 3, 25, 5))
+                    for j in range((max(KS) + 9) // 10):
                         ts(a("NU", 10 * j, 10 * j + 10), a("US", 0, 10), col("CC", 0), OP.subtract)
-                tr(a("TL", sr, sr + 640), a("G0", 0, 640))
-                tt(a("E1", 0, NX[t]), a("SND", so, so + NX[t]), a("PEN", 30 - 10 * t, 30 - 10 * t + NX[t]), OP.add)
-                tt(a("D1", 0, 24), a("SBP", 0, 24), a("SBP", 1, 25), OP.subtract)
-                tt(a("E1", ev, ks), a("E1", ev, ks), a("NU", ev, ks), OP.add)
-                tr(a("TL", sr + 640, sr + V), a("G0", 640, V))
-                turn_last("G1", sl, GV, LATE[t])
+                if t > 1:
+                    tt(a("D1", 0, 24), a("SBP", 0, 24), a("SBP", 1, 25), OP.subtract)
+                dead_term(t + 1)
+                if t + 1 < RO:
+                    roots_ahead(W, t + 1)
+                part(a("SND", so, so + NX[t]))
+                part(a("PEN", 30 - 10 * t, 30 - 10 * t + NX[t]))
+                part(a("NU", ev, ks), ev)
                 continue
 
+            tt(a("CM", 0, 10), mmx(1), c(2), OP.max)
+            dropped()
+            scan(a("HS"), a("NHT"), a("HD"), OP.mult, OP.add)
+            ts(a("HT", 0, 5), a("HS", 3, 40, 8), col("PG", 2), OP.mult, pa, OP.add)
+            ts(a("HT", 8, 13), a("HS", 7, 40, 8), phi, OP.mult)
+            tt(a("HT", 16, 21), a("HT", 0, 5), a("HT", 8, 13), OP.add)
+            cp(a("OFB", 0, 5), a("HT", 16, 21))
             ones, lt, bb = a("ONES"), a("LT"), a(old)
             expanded()
-            ts(a("LL"), pl, 4096.0, OP.mult, float(Z), OP.min)
-            act(a("LT", 640, V), ind(ones, a("LL", 40, 80)), scale=8192.0)
+            ts(a("LL"), pr, float(Z), OP.min)
+            act(a("LT", LV, V), ind(ones, a("LL", LV // 16, 80)), scale=8192.0)
+            ts(a("LT", 0, LV), ind(ones, a("LL", 0, LV // 16)), 8192.0, OP.mult)
             ts(a("LB"), pl, 4096.0, OP.mult, float(Z), OP.min)
             ts(a(old, 0, 80), pr, float(Z), OP.min)
-            ts(a("LT", 0, 640), ind(ones, a("LL", 0, 40)), 8192.0, OP.mult)
+            ts(a("DZB"), pr, float(Z), OP.is_ge, 32768.0, OP.mult)
+            cp(ind(bb, offx), a("LB"))
+            ts(a("BH"), ind(bb, a("OFB", 0, 5)), -1280.0, OP.add)
+            tt(a("AM"), a(old, 320, 400), a("BH"), OP.subtract)
             xu = lambda j, lo2, hi2: ind(lt, a("XU", 80 * j + lo2 // 16, 80 * j + hi2 // 16))
             for j in range(3):
-                act(a("M", V * (2 - j) + 640, V * (3 - j)), xu(j, 640, V))
-            ts(a("DZB"), a("LB"), float(Z), OP.is_ge, 32768.0, OP.mult)
+                act(a("XS", V * (2 - j) + XV, V * (3 - j)), xu(j, XV, V))
+                in_row("s")
             for j in range(3):
-                for lo2 in (0, 320):
-                    mj = a("M", lo2, lo2 + 320)
+                for lo2, hi2 in pieces(0, XV, XV // 64 * 32):
+                    mj = a("XS", lo2, hi2)
                     if j:
-                        tt(mj, xu(j, lo2, lo2 + 320), mj, OP.add)
+                        tt(mj, xu(j, lo2, hi2), mj, OP.add)
                     else:
-                        cp(mj, xu(j, lo2, lo2 + 320))
+                        cp(mj, xu(j, lo2, hi2))
+                    in_row("v")
             pc = a("PC", 0, 80)
-            pick = lambda lo2, hi2: [(a("AA", 128 * i, 128 * i + 128), a("M", lo2 + i, hi2, 16)) for i in range(16)]
+            pick = lambda lo2, hi2: [(a("AA", 128 * i, 128 * i + 128), a("XS", lo2 + i, hi2, 16)) for i in range(16)]
             mm(pc, [(n8k, a("EQ", 80 * j, 80 * j + 80)) for j in range(3)] + [(a("ID"), a("DZB"))], True, False)
+            mm(pc, [(ee(4), a("BH"))], False, False)
             for j in (2, 1):
-                mm(a("PC", 40, 80), pick(V * j + 640, V * j + V), False, False)
+                mm(a("PC", XV // 16, 80), pick(V * j + XV, V * j + V), False, False)
             mm(pc, pick(0, V), False, True)
-            cp(ind(bb, offx), a("LB"))
-            cp(a("BF"), ind(bb, a("OFB", 0, 5)))
-            tt(a("XA", 0, 80), a(old, 320, 400), pc, OP.add)
-            tt(a("XA", 80, 160), a("BF"), pc, OP.add)
-            tt(a("XA", 160, 240), a("XA", 0, 80), kv80, OP.min)
-            ts(a("FL", 80, 160), a("XA", 80, 160), float(Z), OP.min)
-            cp(a("FL", 0, 80), a("XA", 160, 240))
+            ts(a("FL", 80, 160), pc, 1280.0, OP.add, float(Z), OP.min)
+            tt(a("XA", 0, 80), a("AM"), pc, OP.add)
+            tt(a("XA", 80, 160), a("XA", 0, 80), kv80, OP.min)
+            cp(a("FL", 0, 80), a("XA", 80, 160))
             fa = lambda lo2, hi2: a("FL", lo2 // 16, hi2 // 16)
             fb = lambda lo2, hi2: a("FL", 80 + lo2 // 16, 80 + hi2 // 16)
 
-            def wa(lo2, hi2):
-                act(a("MS", lo2, hi2), ind(a(W), fa(lo2, hi2)))
+            def both_w(lo2, hi2):
+                act(a("GB", lo2, hi2), ind(Wt, fb(lo2, hi2)), bias=2047.5)
+                in_row("s")
+                tt(a("AB", lo2, hi2), ind(a(W), fa(lo2, hi2)), a("GB", lo2, hi2), OP.add)
+                in_row("v")
 
-            def wb(lo2, hi2, q):
-                if q == "s":
-                    act(a("MS", V + lo2, V + hi2), ind(Wt, fb(lo2, hi2)))
-                else:
-                    cp(a("MS", V + lo2, V + hi2), ind(Wt, fb(lo2, hi2)))
-
-            def wab(i, lo2, hi2):
-                tt(a("AB", lo2, hi2), ind(Wt, fb(lo2, hi2)), a("MS", lo2, hi2), OP.add)
-                mm(a(banks[i], 0, hi2 - lo2), [(ee(6), a("AB", lo2, hi2))], False, True)
-
-            def new_w(name, i, lo2, hi2, summed=False):
-                pd = a(banks[i], 0, hi2 - lo2)
-                if not summed:
-                    mm(pd, [(half, a("MS", lo2, hi2)), (half, a("MS", V + lo2, V + hi2))], False, True)
-                whole(a(name, lo2, hi2), pd)
+            def new_w(name, lo2, hi2):
+                ts(a(name, lo2, hi2), a("AB", lo2, hi2), 0.5, OP.mult, -1024.0, OP.add)
 
             if e < EP - 1:
-                own = lambda k: a("W1", 128 * k, 128 * k + 128)
-                wb(768, 1152, "v")
-                for i in range(3):
-                    wa(X * i, X * i + X)
-                wab(0, 0, X)
-                wab(1, X, 2 * X)
-                new_w("W1", 0, 0, X, True)
-                send(9, a("W1", 0, X), "h")
-                wab(2, 2 * X, 3 * X)
-                wa(768, 1024)
-                wb(1152, V, "s")
-                wa(1024, V)
-                new_w("W1", 1, X, 2 * X, True)
-                new_w("W1", 2, 2 * X, 3 * X, True)
-                new_w("W1", 3, 768, 1024)
-                new_w("W1", 4, 1024, V)
-                for k in range(8):
-                    act(a("M", 128 * k, 128 * k + 128), own(k), scale=-1.0, acc=col("SND", 160 + k))
+                for i, (lo2, hi2) in enumerate([(0, 128), (128, X)] + pieces(X, V, X)):
+                    both_w(lo2, hi2)
+                    if i == 2:
+                        new_w("W1", 0, X)
+                        in_row("v")
+                for lo2, hi2 in pieces(X, V, X):
+                    new_w("W1", lo2, hi2)
+                ghosts = [send(9, a("W1", 0, X), "h")]
+                colsum("PU", 0, "AB", 0, 8, "ends", ee(4))
+                scan(a("SC", 0, 64), a("M8", 0, 64), a("PU", 0, 64), OP.mult, OP.add)
                 for k in range(8, NP):
-                    negsum(col("SND", 160 + k), own(k))
-                send(RO, a("SND", 160, 170))
-                send(9, a("W1", 0, X), "n")
+                    rowsum(col("SC", 8 * k + 7), a("AB", 128 * k, 128 * k + 128), False)
+                ts(a("SND", 160, 170), a("SC", 7, 80, 8), -0.5, OP.mult, 128 * 1024.0, OP.add)
+                sums = send(RO, a("SND", 160, 170))
+                ghosts.append(send(9, a("W1", 0, X), "n"))
             else:
-                ck = [(0, 256), (256, 768), (768, V)]
-                wb(768, 1024, "v")
-                for i, (lo2, hi2) in enumerate(ck):
-                    act(a("G1", lo2, hi2), ind(a("WB"), fb(lo2, hi2)))
-                    tt(a("G0", lo2, hi2), ind(a("WA"), fa(lo2, hi2)), a("G1", lo2, hi2), OP.add)
-                    dma("y", [], [a("G0", lo2, hi2)], T.yk[:, lo2:hi2], T.G0[:, lo2:hi2], "o%d" % (1 + i))
-                wa(0, 384)
-                wa(384, 768)
-                wab(0, 0, 384)
-                wab(1, 384, 768)
-                new_w("YW", 0, 0, 384, True)
-                wa(768, 1024)
-                wb(1024, V, "s")
-                wa(1024, V)
-                new_w("YW", 1, 384, 768, True)
-                dma("y", [], [a("YW", 0, 768)], T.yw[:, 0:768], T.YW[:, 0:768], "o0")
-                new_w("YW", 2, 768, 1024)
-                new_w("YW", 3, 1024, V)
-                dma("y", [], [a("YW", 768, V)], T.yw[:, 768:V], T.YW[:, 768:V], "o4")
+                def new_kids(i, lo2, hi2, n):
+                    for x0, x1 in pieces(lo2, hi2, n):
+                        act(a("G1", x0, x1), ind(a("WB"), fb(x0, x1)))
+                        in_row("s")
+                        tt(a("G0", x0, x1), ind(a("WA"), fa(x0, x1)), a("G1", x0, x1), OP.add)
+                        in_row("v")
+                    dma("y", [], [a("G0", lo2, hi2)], T.yk[:, lo2:hi2], T.G0[:, lo2:hi2], "o%d" % i, 2.0 + (hi2 - lo2) / 512)
 
+                def store_w(i, lo2, hi2):
+                    new_w("YW", lo2, hi2)
+                    in_row("v")
+                    dma("y", [], [a("YW", lo2, hi2)], T.yw[:, lo2:hi2], T.YW[:, lo2:hi2], "o%d" % i, 2.0 + (hi2 - lo2) / 1024)
+
+                new_kids(0, 0, X, 128)
+                new_kids(1, X, 768, X)
+                new_kids(2, 768, V, X)
+                both_w(0, 384)
+                both_w(384, 640)
+                store_w(3, 0, 384)
+                both_w(640, WS)
+                store_w(4, 384, WS)
+                for i, x in enumerate((ind(Wt, fb(WS, V)), ind(a(W), fa(WS, V)))):
+                    act(a("MS", V * i + WS, V * i + V), x)
+                    in_row("s")
+                mm(a("PD0", 0, V - WS), [(quart, a("ONES", 0, V - WS)), (half, a("MS", WS, V)), (half, a("MS", V + WS, 2 * V))])
+                whole(a("YW", WS, V), a("PD0", 0, V - WS))
+                dma("y", [], [a("YW", WS, V)], T.yw[:, WS:V], T.YW[:, WS:V], "o5", 2.2)
+
+    depends(ops)
+    order = put_in_order(ops)
+    place = {i: n for n, i in enumerate(order)}
     eng = {"g": g, "v": g.vector, "s": g.scalar, "p": g.tensor, "y": g.sync}
-    hist, known = {}, {q: {} for q in eng}
-    for i, o in enumerate(ops):
+    known = {q: {} for q in eng}
+    first, final = {}, {}
+    for i in order:
+        o = ops[i]
         q = o["q"]
         o["key"] = ("own", i) if isinstance(o["sem"], tuple) else q
-        deps = set()
-        for kind in ("rd", "wr"):
-            for nm, lo, hi in o[kind]:
-                psum = nm in PS_
-                for (l2, h2, k2, j) in hist.get(nm, []):
-                    hit = (kind == "wr" or k2 == "wr") and lo < h2 and l2 < hi
-                    if psum:
-                        hit = ops[j]["q"] != q or (q != "p" and hit)
-                    if hit and ops[j]["sem"] != "none":
-                        deps.add(j)
         o["waits"] = []
         if q != "x":
-            for j in sorted(deps, reverse=True):
-                if known[q].get(ops[j]["key"], -1) >= j:
+            for j in sorted(o["hard"], key=lambda j: -place[j]):
+                if known[q].get(ops[j]["key"], -1) >= place[j]:
                     continue
                 o["waits"].append(j)
                 ops[j]["need"] = True
@@ -867,12 +905,12 @@ def rank_program(g, core, T, topo):
             o["snap"] = dict(known[q])
         else:
             o["snap"] = {}
-        o["snap"][o["key"]] = i
-        for kind in ("rd", "wr"):
-            for nm, lo, hi in o[kind]:
-                hist.setdefault(nm, []).append((lo, hi, kind, i))
+        o["snap"][o["key"]] = place[i]
+        first.setdefault(o["grp"], i)
+        final[o["grp"]] = i
     count = {q: 0 for q in eng}
-    for o in ops:
+    for i in order:
+        o = ops[i]
         q = o["q"]
         if isinstance(o["sem"], tuple):
             o["tok"] = o["sem"]
@@ -883,11 +921,11 @@ def rank_program(g, core, T, topo):
             continue
         for j in o["waits"]:
             eng[q].wait_ge(T.sem[ops[j]["tok"][0]], ops[j]["tok"][1])
-        ins = o["fn"](eng[q])
+        ins = o["fn"](eng[q], first[o["grp"]] == i, final[o["grp"]] == i) if o["grp"] else o["fn"](eng[q])
         if isinstance(o["sem"], tuple):
             ins.then_inc(T.sem[o["sem"][0]], o["sem"][1])
         elif o.get("need"):
             ins.then_inc(T.sem["q" + q], 1)
-    for i in range(5):
+    for i in range(6):
         g.sync.wait_ge(T.sem["o%d" % i], 16)
     g.wait_ge(T.sem.sent, sent[0])

@@ -9,54 +9,72 @@ BIG = float(2 ** 21)
 MAGIC = 12582912.0
 MID = 98304.0
 C0 = 1280.3125
-NX = [10, 30, 50, 70]
-XO = [0, 10, 40, 90]
+NX = [10, 20, 30, 40]
+XO = [0, 10, 30, 60]
+CO = [0, 100, 110, 130]
 EV = [0, 2, 3, 3]
 KS = [0, 10, 15, 20]
 SP = [0, 1, 2, 3]
 LV = 512
 XV = 512
 GV = [0, 512, 512, 512]
-NQ = [0, 2, 2, 2]
-WS = 1024
+NQ = [0, 1, 2, 2]
+WS = 960
+CL = [0, 1.0, 1.0, 1.0]
+CA = [0, 1, 2, 3]
+RP = [0, -1, -2, -3]
+SPLIT = 2
+PS2 = 0
+GZ = 2
+L0 = 2.0
+GO = -1
+EROW = 0
+SROW = (3,)
+LP = [0, 0, 2, 1]
+ES = 0
+TS = [0, 0, 0, 0]
+LATE = [1.0, 0.3, 0.0, 0.0]
+KROW = 2
 GA = 1.6
-GF = [0.5, 0.0]
-GN = [0.5, 0.5]
+GF = [0.5, 0.3]
+GN = [0.0, 0.8]
 PF = 0.01
 TAIL = 2
 LAST = 8
 PIECE = 10
-FINE = 768
+FINE = 512
 
 CY = 1.0e-3
 SEM = 0.14
 SWEEPS = 0
+ROOM = 2
 NEAR = 1.6
 STEP = 0.5
-FAR = 2.5
+FAR = 2.2
 
 F, B16, I32, U16, H16 = "float32", "bfloat16", "int32", "uint16", "float16"
 SB_ = {
-    "W0": (WT + V, B16), "W1": (WT + V, B16), "ONES": (WT, B16), "LT": (WT, B16), "YW": (V, B16), "RT": (V, B16),
+    "W0": (WT + V, B16), "W1": (WT + V, B16), "ONES": (512, B16), "LT": (WT, B16), "YW": (V, B16), "RT": (V, B16),
     "KP": (WT, F), "WA": (WT + V, I32), "K2": (V, I32), "WB": (WT, F), "CI": (V, F), "TL": (7 * V, F),
     "G0": (V, F), "G1": (V, F), "GB": (V, F), "M": (5 * V, B16), "MS": (3 * V, B16), "XS": (3 * V, B16), "AA": (2048, B16),
-    "SND": (320, F), "LAND": (1760, F), "US": (128, F), "SGN": (32, F), "ID32": (128, F),
+    "SND": (320, F), "LAND": (1840, F), "US": (40, F), "E4": (40, F), "SGN": (128, F), "ID32": (128, F),
     "PEN": (72, F), "PEN0": (72, F), "NU": (32, F), "MM": (64, F), "KT": (64, F), "T1": (64, F), "S1": (64, F),
     "BI": (64, F), "BJ": (64, F), "C6": (64, F), "GG": (64, F), "D1": (64, F), "S2": (64, F), "OFF": (12, U16),
-    "RL": (160, H16), "DM": (80, B16), "EE": (640, H16), "AB": (V, H16), "LB": (80, F), "B0": (400, F), "B1": (400, F),
+    "RL": (160, H16), "RM": (80, F), "DMM": (80, H16), "LY": (V, B16), "DM": (80, B16), "EE": (640, H16), "AB": (V, H16), "LB": (80, F), "B0": (400, F), "B1": (400, F),
     "LU": (400, U16), "LL": (80, U16), "DZB": (80, B16), "NEQ": (240, B16), "XU": (240, U16),
     "EQ": (240, B16), "SC": (512, F), "SD": (128, F), "SBP": (32, F), "SBP0": (32, F), "LC": (80, F), "EQH": (32, F), "EQL": (32, F),
     "NHT": (40, F), "HD": (40, F), "HS": (40, F), "HT": (24, F), "OFB": (6, U16), "CM": (16, F),
     "XA": (160, F), "BH": (80, H16), "AM": (80, F), "FL": (160, U16), "BS": (160, F),
     "PI": (8, I32), "PF": (8, F), "PG": (16, F), "CC": (8, F), "J": (128, F), "JG": (128, F), "TH": (168, F), "LI": (160, U16),
-    "ID": (128, B16), "NEG": (128, B16), "BO": (256, B16), "CS": (1024, B16), "M8": (512, F), "M16": (64, F),
+    "ID": (128, B16), "NEG": (128, B16), "BO": (256, B16), "CS": (1152, B16), "RC": (32, B16), "M8": (256, F), "M16": (64, F),
     "BG": (4, U16), "GR": (4, U16), "TF": (32, F),
 }
 PS_ = ["PU", "PC", "PR", "PL", "PD0", "PD1", "PD2", "PD3"]
 SCRATCH = {k: ("sbuf", [128, n], d) for k, (n, d) in SB_.items()}
 SCRATCH.update({k: ("psum", [128, 512], F) for k in PS_})
 SEMAPHORES = (["qv", "qs", "qp", "qg", "lw0", "lw1", "lk0", "lk1", "lk2", "ck", "o0", "o1", "o2", "o3", "o4", "o5", "sent"]
-              + ["%s%d" % (nm, i) for nm in ("n0m", "n1m", "n2m", "n3m", "af", "ag", "rl") for i in range(10)])
+              + ["%s%d" % (nm, i) for nm in ("n0m", "n1m", "n2m", "n3m", "af", "ag", "rl") for i in range(16)])
+GHOSTS = (8, 9)
 
 
 def side(s, near):
@@ -94,21 +112,25 @@ def routes(T, topo):
 
 def message(T, m, s, r, near):
     n_ranks = len(T.cores)
-    if m >= 8:
+    if m in GHOSTS:
         w = T["W%d" % (m - 8)]
         d = (r - s) % n_ranks
         return w[:, 0:X], w[:, V + (d - 1) * X:V + d * X]
-    e, t = divmod(m, RO)
-    o, n = 160 * e + XO[t], NX[t]
+    o, n = columns(m)
     order = near_parts(r, near) + sum(far_parts(r, near), [])
     k = order.index(s) if s != r else 0
     at = land_at(m, k)
     return T.SND[:, o:o + n], T.LAND[:, at:at + n]
 
 
+def columns(m):
+    e, t = divmod(m, RO) if m < 8 else divmod(m - 10, RO - 1)
+    return (160 * e + XO[t], NX[t]) if m < 8 else (160 * e + CO[t + 1], NX[t])
+
+
 def land_at(m, k):
-    wide = [(n + 7) // 8 * 8 for n in NX]
-    return 5 * (sum(wide) * (m // RO) + sum(wide[:m % RO])) + k * wide[m % RO]
+    wide = lambda x: (columns(x)[1] + 7) // 8 * 8
+    return 5 * sum(wide(x) for x in range(m) if x not in GHOSTS) + k * wide(m)
 
 
 def fan_mask(topo, src_core, dst_cores):
@@ -124,13 +146,13 @@ def fan_count(topo, src_core, dst_cores):
 
 def relay_mask(T, topo, m, s, near, help_):
     cores = list(T.cores)
-    every = fan_mask(topo, cores[s], [h for h, _ in help_[m // 8][s]])
+    every = fan_mask(topo, cores[s], [h for h, _ in help_[m >= 8][s]])
     out = fan_mask(topo, cores[s], [cores[r] for r in near[s]])
     return every & ~out if m == 8 else out if m == 0 else every
 
 
 def near_by(m, s, near, help_):
-    free = [h for h, fars in help_[1][s] if len(fars) < 2] if m >= 8 else []
+    free = [h for h, fars in help_[1][s] if len(fars) < 2] if m > 8 else []
     by = {h: [r] for h, r in zip(free, near[s][1:])}
     by[None] = near[s][:len(near[s]) - len(by)] if not by else near[s][:1] + near[s][1 + len(by):]
     return by
@@ -151,8 +173,8 @@ def fan(g, T, topo, src_core, dsts, src, sem, mask=-1):
 def helper_program(g, core, T, topo, s, near, help_):
     cores = list(T.cores)
     sent = 0
-    for m in [0, 8, 1, 2, 3, 4, 9, 5, 6, 7]:
-        helpers = help_[m // 8][s]
+    for m in [0, 8, 10, 1, 11, 2, 12, 3, 4, 9, 13, 5, 14, 6, 15, 7]:
+        helpers = help_[m >= 8][s]
         for h, fars in helpers:
             if h == core:
                 g.wait_ge(T.sem["rl%d" % m], bin(relay_mask(T, topo, m, s, near, help_)).count("1"))
@@ -166,7 +188,7 @@ def helper_program(g, core, T, topo, s, near, help_):
 
 
 def depends(ops):
-    hist = {}
+    hist, lead = {}, {}
     for i, o in enumerate(ops):
         hard, soft = set(), set()
         for kind in ("rd", "wr"):
@@ -180,6 +202,8 @@ def depends(ops):
                             soft.add(j)
                     elif hit and ops[j]["sem"] != "none":
                         hard.add(j)
+        if lead.setdefault(o["grp"], i) != i and o["grp"]:
+            soft.add(lead[o["grp"]])
         o["hard"], o["soft"] = hard, soft - hard
         for kind in ("rd", "wr"):
             for nm, lo, hi in o[kind]:
@@ -209,7 +233,7 @@ def put_in_order(ops):
                 k = 0
                 while k < len(line) and line[k][1] <= t:
                     k += 1
-                while k < len(line) and line[k][0] < t + ops[i]["cost"] - 1e-9:
+                while k < len(line) and line[k][0] < t + ops[i]["cost"] * (ROOM if ops[i]["q"] == "s" else 1) - 1e-9:
                     t = max(t, line[k][1])
                     k += 1
                 line.insert(k, (t, t + ops[i]["cost"]))
@@ -350,7 +374,7 @@ def rank_program(g, core, T, topo):
     def send(m, src, to="hn", cost=0.3):
         def fn(e):
             ap = message(T, m, rank, rank, near)[0]
-            hs = help_[m // 8][rank]
+            hs = help_[m >= 8][rank]
             if hs and "h" in to:
                 sent[0] += fan(e, T, topo, core, [(h, ap) for h, _ in hs], ap, T.sem["rl%d" % m],
                                relay_mask(T, topo, m, rank, near, help_))
@@ -363,7 +387,7 @@ def rank_program(g, core, T, topo):
     col = lambda name, j: a(name, j, j + 1)
     v80, kv80 = a("BS", 0, 80), a("BS", 80, 160)
     cs = lambda j: a("CS", 128 * j, 128 * j + 128)
-    n8k, n24, cdv, i4k, mid_r, mid_l, half, quart = [cs(j) for j in range(8)]
+    n8k, n24, cdv, i4k, mid_r, mid_l, half, quart, i8 = [cs(j) for j in range(9)]
     ee = lambda j: a("EE", 128 * j, 128 * j + 128)
     thirds = [(0, 512), (512, 1024), (1024, V)]
     pieces = lambda lo, hi, n: [(x, min(x + n, hi)) for x in range(lo, hi, n)]
@@ -406,20 +430,29 @@ def rank_program(g, core, T, topo):
         for x0, x1 in pieces(lo, max(lo, min(hi, V - FINE)), 256) + pieces(max(lo, V - FINE), hi, 128):
             tr(a("TL", at + x0, at + x1), a(src, x0, x1))
 
+    def landed(m, call, late):
+        land = lambda k: a("LAND", land_at(m, k), land_at(m, k) + columns(m)[1])
+        nn, nf = len(src_near), len(src_far[0])
+        for k in range(nn):
+            arrive([land(k)], near_sem(src_near[k], near, m), cnt_near[k], (call, NEAR + STEP * k))
+        for j in range(2):
+            arrive([land(nn + j * nf + k) for k in range(nf)], "%s%d" % (sem_far[j], m), cnt_far[j], (call, FAR + STEP * j + late))
+        return [land(k) for k in range(NR - 1)]
+
     dma("y", [a("W0", 0, X)], [], T.W0[:, 0:X], T.w[:, 0:X], "lw0", 2.2)
-    dma("s", [a("W0", X, V)], [], T.W0[:, X:V], T.w[:, X:V], "lw1", 2.8)
+    in_row("y")
+    dma("y", [a("W0", X, V)], [], T.W0[:, X:V], T.w[:, X:V], "lw1", 2.8)
+    in_row("y")
     for i, (lo, hi) in enumerate(thirds):
         dma("y", [a("WA", WT + lo, WT + hi)], [], T.WA[:, WT + lo:WT + hi], T.kids[:, lo:hi], "lk%d" % i, 3.5 + i)
         in_row("y")
     iota(col("PI", 0), [[0, 1]], 0, 1, False)
     iota(a("J"), [[1, 128]])
-    iota(a("TH", 0, 65), [[0, 13], [1, 5]])
-    iota(a("SBP0", 0, 25), [[256, 5], [-(2 * V - 16), 5]], 3 * (2 * V - 16) + 63, 16)
-    iota(a("LC", 0, 75), [[2 * V, 3], [256, 5], [16, 5]], V + 15, 16)
     ghosts = [send(8, a("W0", 0, X), "h", 3.0)]
     ms(a("M8"), 1.0)
     ms(a("M16"), 0.0)
     ms(a("KT"), 0.0)
+    ms(a("SGN"), 1.0)
     p0 = col("PI", 0)
     ts(col("PI", 1), p0, 15, OP.bitwise_and)
     ts(col("PI", 2), p0, 4, OP.arith_shift_right)
@@ -427,7 +460,7 @@ def rank_program(g, core, T, topo):
     ts(col("PI", 4), p0, 4, OP.arith_shift_right, 1, OP.bitwise_and)
     ts(col("PI", 5), p0, 1, OP.bitwise_and)
     ts(col("PI", 6), p0, 31, OP.bitwise_and)
-    ms(a("M8", 0, 512, 8), 0.0)
+    ms(a("M8", 0, 256, 8), 0.0)
     ms(a("M16", 0, 64, 16), 1e9)
     cp(a("PF", 0, 7), a("PI", 0, 7))
     ms(a("D1"), -80.0)
@@ -451,12 +484,10 @@ def rank_program(g, core, T, topo):
     ts(a("TF", 4, 6), a("J", 0, 2), 0.0, OP.mult, odd, OP.add)
     cp(a("TF", 6, 8), a("J", 0, 2))
     ts(a("TF", 16, 20), a("BS", 0, 4), -2.0, OP.add, 0.2, OP.mult)
-    ts(a("SBP0", 0, 25), a("SBP0", 0, 25), col("PG", 1), OP.add)
     ts(a("BG"), a("TF", 4, 8), 16.0, OP.mult, col("PG", 4), OP.add)
     whole(a("TF", 20, 24), a("TF", 16, 20))
     for h in (0, 2, 3):
         ts(a("PEN0", 30 - 10 * h, 40 - 10 * h), a("J", 0, 10), 0.0, OP.mult, col("CC", h), OP.add)
-    ms(a("SBP0", 4, 25, 5), 0.0)
     ts(a("TF", 8, 12), a("TF", 20, 24), 6.0, OP.is_ge, -4.0, OP.mult)
     ts(a("TF", 24, 28), a("TF", 20, 24), 6.0, OP.mult, 5.0, OP.add)
     for j, (tgt, msk) in enumerate([(pp, col("PG", 3)), (col("PG", 5), col("PG", 3)), (col("PG", 5), hi_), (pp, hi_)]):
@@ -467,31 +498,40 @@ def rank_program(g, core, T, topo):
             act(a("M", 128 * k, 128 * k + 128), own, scale=-1.0, acc=col("SND", k))
         else:
             rowsum(col("SND", k), own)
-    sums = send(0, a("SND", 0, 10))
-    ghosts.append(send(8, a("W0", 0, X), "n"))
-    iota(a("JG"), [[1, 8], [0, 16]])
-    iota(a("CI"), [[4097, V]], V * 4097)
-    ops[-1]["after"].append((sends[-1], 0.0))
+    sums = send(0, a("SND", 0, 10), "h", 0.6)
+    for m, x in [(8, a("W0", 0, X)), (0, a("SND", 0, 10))][::GO]:
+        send(m, x, "n")
+    for x in ((a("JG"), [[1, 8], [0, 16]]), (a("TH", 0, 65), [[0, 13], [1, 5]]), (a("TH", 72, 162), [[0, 3], [8, 6], [0, 5]], 21),
+              (a("SBP0", 0, 25), [[256, 5], [-(2 * V - 16), 5]], 3 * (2 * V - 16) + 63, 16),
+              (a("LC", 0, 75), [[2 * V, 3], [256, 5], [16, 5]], V + 15, 16), (a("CI"), [[4097, V]], V * 4097),
+              (a("LY"), [[0, V]]), (a("LT", V, WT), [[0, WT - V]]))[:6 + GZ]:
+        iota(*x)
+        ops[-1]["after"].append((sends[-1], 0.0))
+        in_row("g")
+    act(a("SBP0", 0, 25), a("SBP0", 0, 25), bias=col("PG", 1))
+    act(a("SBP0", 4, 25, 5), a("J", 0, 5), scale=0.0)
     ts(ee(4), a("J"), pp, OP.is_equal)
-    ts(a("NEG"), a("ID"), -1.0, OP.mult)
+    act(a("NEG"), a("ID"), scale=-1.0)
     ms(a("KP", Z, WT), DV)
     ms(a("W0", Z, WT), 0.0)
     for i, (lo, hi) in enumerate(thirds):
         act(a("PD%d" % i, 0, hi - lo), a("W0", lo, hi), AF.Relu, bias=DV, scale=-DV)
     act(a("ONES", 0, 512), a("W0", 0, 512), bias=1.0, scale=0.0)
     tt(a("TF", 12, 16), a("TF", 8, 12), a("TF", 24, 28), OP.add)
-    ts(a("LC", 0, 75), a("LC", 0, 75), col("PG", 1), OP.add)
-    ts(a("TH", 0, 65), a("TH", 0, 65), -0.25, OP.mult, 0.5, OP.add)
-    iota(a("TH", 72, 162), [[0, 3], [8, 6], [0, 5]], 21)
-    ts(a("TH", 75, 162, 5), a("TH", 75, 162, 5), -1.125, OP.add)
-    ts(a("TH", 76, 162, 5), a("TH", 76, 162, 5), -2.0, OP.add)
+    act(a("LC", 0, 75), a("LC", 0, 75), bias=col("PG", 1))
+    act(a("TH", 0, 65), a("TH", 0, 65), bias=0.5, scale=-0.25)
+    act(a("TH", 75, 162, 5), a("TH", 75, 162, 5), bias=-1.125)
+    act(a("TH", 76, 162, 5), a("TH", 76, 162, 5), bias=-2.0)
     ts(col("PG", 13), col("PG", 10), 8.0, OP.mult, MAGIC + V / 64, OP.add)
     ts(col("PG", 15), odd, -16.0, OP.mult, 31.5, OP.add)
     ts(col("PG", 14), pa, 32.0, OP.mult, col("PG", 15), OP.add)
-    for nm, s_, x in (("SBP0", 2, V + 47.5), ("LC", 3, V + 31.5)):
-        ts(a("TF", 0, 5), a("J", 0, 5), 512.0, OP.mult, x, OP.add)
-        ts(a(nm, s_, 25, 5), a("TF", 0, 5), col("PG", 14), OP.add)
+    for j, (nm, s_, x) in enumerate((("SBP0", 2, V + 47.5), ("LC", 3, V + 31.5))):
+        ts(col("CC", 5 + j), col("PG", 14), x, OP.add)
+        act(a(nm, s_, 25, 5), a("J", 0, 5), bias=col("CC", 5 + j), scale=512.0)
     ts(a("PEN0", 20, 30), a("PEN0", 30, 40), 0.5, OP.add)
+    ts(col("CC", 4), col("CC", 0), -1.0, OP.mult)
+    for t in range(1, RO):
+        ms(a("SGN", 32 * t, 32 * t + EV[t]), -1.0)
     ts(a("GR"), a("TF", 12, 16), 63.0, OP.min)
     ms(a("NHT"), 0.0)
     ts(a("D1", 33, 54, 5), a("BS", 0, 5), 320.0, OP.add)
@@ -503,21 +543,19 @@ def rank_program(g, core, T, topo):
     for j, x in enumerate((-2.0 ** 19, 2.0 ** 19)):
         ts(a("BO", 128 * j, 128 * j + 128), a("JG"), pg, OP.is_equal, x, OP.mult)
     ts(cdv, a("J"), 0.0, OP.mult, col("PG", 8), OP.add)
-    for c_, x in ((n8k, -8192.0), (i4k, 4096.0), (mid_r, 1280.0), (mid_l, 0.3125), (half, 0.5), (quart, -0.25)):
-        ts(c_, a("ID"), x, OP.mult)
-    ms(a("SGN"), 1.0)
-    ts(kv80, v80, float(WT), OP.add)
+    for c_, x in ((n8k, -8192.0), (i4k, 4096.0), (mid_r, 1280.0), (mid_l, 0.3125), (half, 0.5), (quart, -0.25), (i8, 8.0)):
+        act(c_, a("ID"), scale=x)
+    for x in (a("LY"), a("LT", V, WT))[GZ:]:
+        for lo, hi in pieces(x["r"][0][1], x["r"][0][2], 224):
+            ms(a(x["r"][0][0], lo, hi), 0.0)
+    act(kv80, v80, bias=float(WT))
     ms(a("HD"), -80.0)
-    for w in ("W1", "ONES", "WB"):
-        ms(a(w, Z, WT), 0.0)
-    ts(a("HD", 3, 40, 8), a("J", 0, 5), 16.0, OP.mult, 240.0, OP.add)
-    ts(a("HD", 7, 40, 8), a("J", 0, 5), 16.0, OP.mult, 240.0, OP.add)
-    act(a("B0"), a("W0", 0, 400), scale=0.0)
-    act(a("B1"), a("W0", 0, 400), scale=0.0)
-    for lo, hi in pieces(512, Z, 512):
-        act(a("ONES", lo, hi), a("W0", (lo - 512) // 2, (lo - 512) // 2 + hi - lo), bias=1.0, scale=0.0)
-    for lo, hi in pieces(V, WT, 432):
-        act(a("LT", lo, hi), a("W0", 0, hi - lo), scale=0.0)
+    for w in ("W1", "WB"):
+        act(a(w, Z, WT), a("J", 0, 16), scale=0.0)
+    for lo in (3, 7):
+        act(a("HD", lo, 40, 8), a("J", 0, 5), bias=240.0, scale=16.0)
+    ms(a("B0", 0, 160), 0.0)
+    ms(a("B1", 0, 240), 0.0)
 
     def end_table(t):
         if t == 1:
@@ -525,9 +563,10 @@ def rank_program(g, core, T, topo):
         elif t == 2:
             iota(a("WB", 0, Z), [[4096, Z]])
         else:
-            add("g", [a("AA")], [a("ONES", 0, 2048)],
-                lambda en: en.affine_select(T.AA[:, 0:2048], T.ONES[:, 0:2048], [[-1000, 16], [-16, 8], [999, 16]],
-                                            OP.is_equal, 0.0, 0, 1), 3.9)
+            for i in range(4):
+                add("g", [a("AA", 512 * i, 512 * i + 512)], [a("ONES")],
+                    lambda en, i=i: en.affine_select(T.AA[:, 512 * i:512 * i + 512], T.ONES[:, 0:512], [[-1000, 4], [-16, 8], [1000, 16]],
+                                                     OP.is_equal, 0.0, -4000 * i, 1), 1.2, after=[(sends[-1], 0.0)])
         ops[-1]["after"].append((sends[-1], 0.0))
 
     for e in range(EP):
@@ -535,21 +574,26 @@ def rank_program(g, core, T, topo):
         Wt = a(W, 0, WT)
         kin = "WA" if e == 0 else "K2"
         ko = WT if e == 0 else 0
-        late = 3.0 * (1 - e)
-        cp(a("SBP", 0, 25), a("SBP0", 0, 25))
-        cp(a("PEN", 0, 70), a("PEN0", 0, 70))
+        late = L0 * (1 - e)
+        act(a("SBP", 0, 25), a("SBP0", 0, 25))
+        act(a("PEN", 0, 70), a("PEN0", 0, 70))
         part = lambda x, lo=0: mm(a("PU", lo, lo + x["n"]), [(a("ID32"), x)], grp="sum%d" % len(sends))
         part(a("SND", 160 * e, 160 * e + 10))
         part(a("PEN0", 30, 40))
-        for i, (lo, hi) in enumerate(thirds):
-            if e > 0:
-                absent("PD%d" % i, 0, W, lo, hi)
-            for x0, x1 in pieces(lo, hi, 256):
-                if e > 0:
-                    act(a("G1", x0, x1), ind(a("WB"), a("FL", 80 + x0 // 16, 80 + x1 // 16)))
-                    tt(a("K2", x0, x1), ind(a("WA"), a("FL", x0 // 16, x1 // 16)), a("G1", x0, x1), OP.add)
-                tt(a("KP", x0, x1), a(kin, ko + x0, ko + x1), a("PD%d" % i, x0 - lo, x1 - lo), OP.max)
-                act(a("G0", x0, x1), a("KP", x0, x1), bias=-C0, scale=1.0 / 4096)
+        for i, (lo, hi) in enumerate(thirds if e else []):
+            absent("PD%d" % i, 0, W, lo, hi)
+        for x0 in range(0, V + X, X):
+            if e > 0 and x0 < V:
+                act(a("G1", x0, x0 + X), ind(a("WB"), a("FL", 80 + x0 // 16, 96 + x0 // 16)))
+                tt(a("K2", x0, x0 + X), ind(a("WA"), a("FL", x0 // 16, 16 + x0 // 16)), a("G1", x0, x0 + X), OP.add)
+                if KROW:
+                    in_row("k")
+            if x0:
+                y0 = x0 - X
+                tt(a("KP", y0, x0), a(kin, ko + y0, ko + x0), a("PD%d" % (y0 // 512), y0 % 512, y0 % 512 + X), OP.max)
+                if KROW:
+                    in_row("k")
+                act(a("G0", y0, x0), a("KP", y0, x0), bias=-C0, scale=1.0 / 4096)
         turn("G0", 0, 0)
         dead_term(1)
         roots_ahead(W, 1)
@@ -575,47 +619,25 @@ def rank_program(g, core, T, topo):
         for t in range(1, RO + 1):
             m = RO * e + t - 1
             n = NX[t - 1]
-            land = lambda k: a("LAND", land_at(m, k), land_at(m, k) + n)
-            nn, nf = len(src_near), len(src_far[0])
-            for k in range(nn):
-                arrive([land(k)], near_sem(src_near[k], near, m), cnt_near[k], (sums, NEAR + STEP * k))
-            for j in range(2):
-                arrive([land(nn + j * nf + k) for k in range(nf)], "%s%d" % (sem_far[j], m), cnt_far[j],
-                       (sums, FAR + STEP * j + (late if t == 1 else 0)))
-            for k in range(NR - 2):
-                part(land(k))
-            last, at = land(NR - 2), land_at(m, NR - 2)
-            u = lambda h: a("US", 10 * (t - 1 - h), 10 * (t - h))
-            c = lambda i: a("US", 10 * (t + i), 10 * (t + i + 1))
-            mmx = lambda j: a("MM", 10 * j, 10 * j + 10)
+            parts = landed(m, sums, LATE[t - 1] + (late if t == 1 else 0))
+            nf = len(src_far[1])
+            for x in parts[:-nf]:
+                part(x)
+            last, (nm, at, _) = parts[-1], parts[-1]["r"][0]
+            if nf == 2:
+                last, nm, at = a("E4", 0, n), "E4", 0
+                tt(last, parts[-2], parts[-1], OP.add)
             kt = lambda par: a("KT", 32 * par + 5, 32 * par + 30, 6)
             if t == 1:
                 for par in range(2):
-                    tt(kt(par), a("PU", par, 10, 2), a("LAND", at + par, at + 10, 2), OP.add)
+                    tt(kt(par), a("PU", par, 10, 2), a(nm, at + par, at + 10, 2), OP.add)
                 tt(a("US", 0, n), a("PU", 0, n), last, OP.add)
             else:
                 tt(a("US", 0, n), a("PU", 0, n), last, OP.add)
-                if t == 2:
-                    tt(mmx(0), u(1), c(0), OP.max)
-                    xs = ("US", 10)
-                elif t == 3:
-                    tt(mmx(1), c(0), c(1), OP.max)
-                    tt(mmx(2), u(0), u(1), OP.min)
-                    tt(mmx(0), u(2), mmx(1), OP.max)
-                    xs = ("MM", 20)
-                else:
-                    tt(mmx(1), c(0), c(1), OP.max)
-                    tt(mmx(3), u(3), c(2), OP.max)
-                    tt(mmx(2), u(0), u(1), OP.min)
-                    tt(mmx(0), mmx(1), mmx(3), OP.max)
-                    tt(mmx(4), mmx(2), u(2), OP.min)
-                    xs = ("MM", 40)
+                if t > 2:
+                    tt(a("MM", 0, n - 20), a("US", 0, n - 20), a("US", 20, n), OP.min)
                 for par in range(2):
-                    tt(kt(par), a(xs[0], xs[1] + par, xs[1] + 10, 2), a("MM", par, 10, 2), OP.min)
-
-            def dropped():
-                ts(a("NHT", 5 - t, 40, 4), c(0) if t == 2 else mmx(1) if t == 3 else a("CM", 0, 10), 0.0, OP.is_gt)
-
+                    tt(kt(par), a("MM" if t > 2 else "US", par, 10, 2), a("MM" if t > 3 else "US", 10 + par, 20, 2), OP.min)
             tr(a("T1"), a("KT"))
             scan(a("S1"), a("M16"), a("T1"), OP.add, OP.min)
             nb = 32 if t == 1 else 64
@@ -644,14 +666,24 @@ def rank_program(g, core, T, topo):
             rr, ll = a("RL", 0, 80), a("RL", 80, 160)
             pr, pl = a("PR", 0, 80), a("PL", 0, 80)
             src = ind(tl, off)
-            whole(rr, src)
-            swap("PR", 0)
-            tt(ll, src, rr, OP.subtract)
-            swap("PL", 80)
 
             def expanded():
                 cp(a("XU", 80 * (t - 2), 80 * (t - 1)), ind(a(old), offx))
                 tt(a("EQ", 80 * (t - 2), 80 * (t - 1)), ind(a(old), offx), v80, OP.is_equal)
+
+            if t == RO:
+                tt(a("RM"), src, a("DMM"), OP.max)
+                ts(a("LY", 0, V, 16), a("RM"), 1279.75, OP.is_lt, 8192.0, OP.mult)
+                tr(a("LT", 0, V), a("LY"))
+            whole(rr, src)
+            if t == RO:
+                in_row("v")
+                expanded()
+            swap("PR", 0)
+            tt(ll, src, rr, OP.subtract)
+            if t == RO and EROW:
+                in_row("v")
+            swap("PL", 80)
 
             if t < RO:
                 so = 160 * e + XO[t]
@@ -671,7 +703,8 @@ def rank_program(g, core, T, topo):
                     for i in range(t):
                         tt(blk(new, i), blk(old, i), dz, OP.max)
                     cp(ind(a(new), offx), a("LB"))
-                    cp(lu(80, 80 + 80 * t), bold)
+                    if t in SROW:
+                        in_row("v")
                 chunks = chunks_of(t)
                 sp = chunks[SP[t] - 1][1] if SP[t] else ev
                 pe = ks + TAIL
@@ -686,9 +719,20 @@ def rank_program(g, core, T, topo):
                     for i in range(t if t > 1 else 0):
                         mm(a("PC", 10 * i, 10 * i + 10), [(a("BO", 128, 256), a("DM", b, 80, 8)) for b in range(8)], i == 0, False)
                     mm(a("PC", 0, 10 * t), [(a("BO", 0, 128), a("NEQ", b, 80 * t, 8)) for b in range(8)], t == 1, True)
-                    act(a("SND", so + nu, so + nu + 10 * t), a("PC", 0, 10 * t))
 
+                mc = 10 + (RO - 1) * e + t - 1
+                co = columns(mc)[0]
                 unit = lambda k0, k1: a("M", 128 * mo(k0), 128 * (mo(k0) + k1 - k0))
+                runs = [(0, 1), (1, ev)][:ev] + pieces(mid, nu, PIECE) + pieces(pe, mid, PIECE) + [(ks, pe)]
+                for i, (k0, k1) in enumerate(sum([unwrapped(*r) for r in runs], [])):
+                    if i == LP[t] and t > 1:
+                        cp(lu(80, 80 + 80 * t), bold)
+                        in_row("v")
+                    if i == NQ[t]:
+                        counts()
+                    r0 = 128 * (k0 % NP)
+                    tt(unit(k0, k1), ind(Wt, lu(8 * k0, 8 * k1)), a("RT", r0, r0 + 128 * (k1 - k0)), OP.min)
+                    in_row("v")
 
                 def short(i):
                     k0, k1 = chunks[i]
@@ -709,37 +753,39 @@ def rank_program(g, core, T, topo):
                     if i >= 4:
                         roots(W, i, k0, k1)
                     mm(a("PD%d" % (i % 4), 0, 128 * (k1 - k0)), [(a("NEG"), mk)], False, True)
+                    if i == CA[t]:
+                        act(a("SND", co, co + 10 * t), a("PC", 0, 10 * t))
+                        in_row("s")
+                        ahead = send(mc, a("SND", co, co + 10 * t))
                     if i:
                         short(i - 1)
                 short(len(chunks) - 1)
-                runs = [(0, 1), (1, ev)][:ev] + pieces(mid, nu, PIECE) + pieces(pe, mid, PIECE) + [(ks, pe)]
-                for i, (k0, k1) in enumerate(sum([unwrapped(*r) for r in runs], [])):
-                    if i == NQ[t]:
-                        counts()
-                    r0 = 128 * (k0 % NP)
-                    tt(unit(k0, k1), ind(Wt, lu(8 * k0, 8 * k1)), a("RT", r0, r0 + 128 * (k1 - k0)), OP.min)
-                    in_row("v")
-                for u0, u1 in ([(sp, mo(nu)), (0, sp)] if SP[t] else [(0, mo(nu))]):
+                cut = chunks[SP[t] - 2][1] if SP[t] > SPLIT else 0
+                for u0, u1 in ([(0, cut), (sp, mo(nu)), (cut, sp)] if SP[t] else [(0, mo(nu))]):
                     if u1 > u0:
                         colsum("PU", 8 * u0, "M", u0, u1, votes)
                 w8 = 8 * mo(nu)
                 scan(a("SC", 0, w8), a("M8", 0, w8), a("PU", 0, w8), OP.mult, OP.add)
                 if sp > ev:
-                    ms(a("SGN", 0, ev), -1.0)
-                    tt(a("SND", so, so + sp), a("SC", 7, 8 * sp, 8), a("SGN", 0, sp), OP.mult)
+                    tt(a("SND", so, so + sp), a("SC", 7, 8 * sp, 8), a("SGN", 32 * t, 32 * t + sp), OP.mult)
                 else:
                     ts(a("SND", so, so + ev), a("SC", 7, 8 * ev, 8), -1.0, OP.mult)
-                if mid < nu:
+                if mid < nu and ES:
+                    act(a("SND", so + mid, so + nu), a("SC", 8 * sp + 7, w8, 8), scale=-1.0)
+                    in_row("s")
+                elif mid < nu:
                     ts(a("SND", so + mid, so + nu), a("SC", 8 * sp + 7, w8, 8), -1.0, OP.mult)
                 w8 = 8 * (mid - pe)
                 colsum("PL", 128, "M", mo(pe), mo(pe) + mid - pe, "last%d" % m)
                 scan(a("SD", 0, w8), a("M8", 0, w8), a("PL", 128, 128 + w8), OP.mult, OP.add)
                 for k in range(ks, pe):
-                    rowsum(col("SND", so + k), unit(k, k + 1))
+                    if k < ks + TS[t]:
+                        act(unit(k, k + 1), unit(k, k + 1), scale=-1.0, acc=col("SND", so + k))
+                        in_row("s")
+                    else:
+                        rowsum(col("SND", so + k), unit(k, k + 1))
                 ts(a("SND", so + pe, so + mid), a("SD", 7, w8, 8), -1.0, OP.mult)
                 sums = send(m + 1, a("SND", so, so + NX[t]))
-                if t == RO - 1:
-                    ms(a("SGN", 0, ev), 1.0)
                 if e == 0:
                     end_table(t)
                 if t == 1:
@@ -749,7 +795,7 @@ def rank_program(g, core, T, topo):
                 else:
                     cp(a("LL"), a("LB"))
                     lists = [lu, lambda c0, c1: a("LL", c0, c1)]
-                sl, sr = (2 * t - 1) * V, 2 * t * V
+                sl, sr, kids = (2 * t - 1) * V, 2 * t * V, []
                 for gx, lst, slot in (("G0", lists[0], sr), ("G1", lists[1], sl)):
                     for lo, hi in pieces(0, V, 256):
                         if gx == "G1" and lo < GV[t]:
@@ -757,55 +803,55 @@ def rank_program(g, core, T, topo):
                         else:
                             act(a(gx, lo, hi), ind(a("KP"), lst(lo // 16, hi // 16)), bias=-C0, scale=1.0 / 4096)
                             in_row("s")
+                            kids.append(len(ops) - 1)
                     turn(gx, slot, 0)
-                ts(a("DM"), bt, float(Z), OP.is_ge)
+                act(a("DM"), bt, AF.Relu, bias=1.0 - Z)
+                if t > 1:
+                    tt(a("DMM"), rr, a("DMM"), OP.max)
+                else:
+                    cp(a("DMM"), rr)
                 if t > 1:
                     tt(a("EQH", 0, 25), a("GG", 1, 26), a("GG", 0, 25), OP.subtract)
-                    dropped()
                     tt(a("EQL", 0, 25), a("EQH", 0, 25), a("LC", 25 * (t - 1), 25 * t), OP.mult)
                     expanded()
-                    nh = a("NHT", 5 - t, 40, 4)
-                    if t == 3:
-                        cp(a("PEN", 50, 60), a("PEN", 40, 50))
-                    ts(a("PEN", 40 - 10 * t, 50 - 10 * t), nh, BIG, OP.mult, col("CC", t - 1), OP.add)
-                    ts(a("PEN", 40, 50), nh, -BIG, OP.mult, 2.0 ** 18, OP.add)
                     tt(a("SBP", 0, 25), a("SBP", 0, 25), a("EQL", 0, 25), OP.max)
-                else:
-                    cp(a("SBP", 3, 25, 5), a("LC", 3, 25, 5))
-                    for j in range((max(KS) + 9) // 10):
-                        ts(a("NU", 10 * j, 10 * j + 10), a("US", 0, 10), col("CC", 0), OP.subtract)
-                if t > 1:
                     tt(a("D1", 0, 24), a("SBP", 0, 24), a("SBP", 1, 25), OP.subtract)
+                else:
+                    act(a("SBP", 3, 25, 5), a("LC", 3, 25, 5))
+                    for j in range((max(KS) + 9) // 10):
+                        act(a("NU", 10 * j, 10 * j + 10), a("US", 0, 10), bias=col("CC", 4))
                 dead_term(t + 1)
                 if t + 1 < RO:
                     roots_ahead(W, t + 1)
                 part(a("SND", so, so + NX[t]))
-                part(a("PEN", 30 - 10 * t, 30 - 10 * t + NX[t]))
+                part(a("PEN", 30 - 10 * t, 40))
                 part(a("NU", ev, ks), ev)
+                for x in [a("SND", co, co + 10 * t), a("PEN", 70 - 10 * t, 70)] + landed(mc, ahead, CL[t]):
+                    mm(a("PC", 0, 10 * t), [(a("ID32"), x)], grp="counts%d" % m)
+                act(a("RC", 0, 10 * t), a("PC", 0, 10 * t), AF.Relu)
+                ops[-1]["after"].append((kids[RP[t]], 0.0))
+                zero = [a("RC", 10 * i, 10 * i + 10) for i in range(t)]
+                mm(a("PU", 0, 10), [(i8, x) for x in zero], grp="sum%d" % len(sends))
+                mm(a("PC", 32, 42), [(i8, x) for x in zero])
+                nh = a("NHT", 4 - t, 40, 4)
+                act(nh, a("PC", 32, 42), AF.Sign)
+                if t + 1 < RO:
+                    act(a("PEN", 30 - 10 * t, 40 - 10 * t), nh, bias=col("CC", t), scale=BIG)
+                    act(a("PEN", 60 - 10 * t, 70 - 10 * t), nh, bias=2.0 ** 18, scale=-BIG)
                 continue
 
-            tt(a("CM", 0, 10), mmx(1), c(2), OP.max)
-            dropped()
             scan(a("HS"), a("NHT"), a("HD"), OP.mult, OP.add)
             ts(a("HT", 0, 5), a("HS", 3, 40, 8), col("PG", 2), OP.mult, pa, OP.add)
             ts(a("HT", 8, 13), a("HS", 7, 40, 8), phi, OP.mult)
             tt(a("HT", 16, 21), a("HT", 0, 5), a("HT", 8, 13), OP.add)
             cp(a("OFB", 0, 5), a("HT", 16, 21))
-            ones, lt, bb = a("ONES"), a("LT"), a(old)
-            expanded()
-            ts(a("LL"), pr, float(Z), OP.min)
-            act(a("LT", LV, V), ind(ones, a("LL", LV // 16, 80)), scale=8192.0)
-            ts(a("LT", 0, LV), ind(ones, a("LL", 0, LV // 16)), 8192.0, OP.mult)
-            ts(a("LB"), pl, 4096.0, OP.mult, float(Z), OP.min)
-            ts(a(old, 0, 80), pr, float(Z), OP.min)
-            ts(a("DZB"), pr, float(Z), OP.is_ge, 32768.0, OP.mult)
-            cp(ind(bb, offx), a("LB"))
-            ts(a("BH"), ind(bb, a("OFB", 0, 5)), -1280.0, OP.add)
-            tt(a("AM"), a(old, 320, 400), a("BH"), OP.subtract)
+            lt, bb = a("LT"), a(old)
+            steps = [lambda: (ts(a("LB"), pl, 4096.0, OP.mult, float(Z), OP.min), ts(a(old, 0, 80), pr, float(Z), OP.min),
+                              ts(a("DZB"), pr, float(Z), OP.is_ge, 32768.0, OP.mult)),
+                     lambda: cp(ind(bb, offx), a("LB")),
+                     lambda: ts(a("BH"), ind(bb, a("OFB", 0, 5)), -1280.0, OP.add),
+                     lambda: tt(a("AM"), a(old, 320, 400), a("BH"), OP.subtract)]
             xu = lambda j, lo2, hi2: ind(lt, a("XU", 80 * j + lo2 // 16, 80 * j + hi2 // 16))
-            for j in range(3):
-                act(a("XS", V * (2 - j) + XV, V * (3 - j)), xu(j, XV, V))
-                in_row("s")
             for j in range(3):
                 for lo2, hi2 in pieces(0, XV, XV // 64 * 32):
                     mj = a("XS", lo2, hi2)
@@ -814,13 +860,25 @@ def rank_program(g, core, T, topo):
                     else:
                         cp(mj, xu(j, lo2, hi2))
                     in_row("v")
+                    if steps:
+                        steps.pop(0)()
+                        if EROW > 1:
+                            in_row("v")
+                act(a("XS", V * (2 - j) + XV, V * (3 - j)), xu(j, XV, V))
+                in_row("s")
             pc = a("PC", 0, 80)
             pick = lambda lo2, hi2: [(a("AA", 128 * i, 128 * i + 128), a("XS", lo2 + i, hi2, 16)) for i in range(16)]
-            mm(pc, [(n8k, a("EQ", 80 * j, 80 * j + 80)) for j in range(3)] + [(a("ID"), a("DZB"))], True, False)
-            mm(pc, [(ee(4), a("BH"))], False, False)
+            kill = "kill%d" % e
+            mm(pc, [(n8k, a("EQ", 80 * j, 80 * j + 80)) for j in range(2)], grp=kill)
+            mm(pc, [(n8k, a("EQ", 160, 240)), (a("ID"), a("DZB"))], grp=kill)
+            mm(pc, [(ee(4), a("BH"))], grp=kill)
             for j in (2, 1):
-                mm(a("PC", XV // 16, 80), pick(V * j + XV, V * j + V), False, False)
-            mm(pc, pick(0, V), False, True)
+                mm(a("PC", XV // 16, 80), pick(V * j + XV, V * j + V), grp=kill)
+            if PS2:
+                mm(a("PC", XV // 16, 80), pick(XV, V), grp=kill)
+                mm(a("PC", 0, XV // 16), pick(0, XV), grp=kill)
+            else:
+                mm(pc, pick(0, V), grp=kill)
             ts(a("FL", 80, 160), pc, 1280.0, OP.add, float(Z), OP.min)
             tt(a("XA", 0, 80), a("AM"), pc, OP.add)
             tt(a("XA", 80, 160), a("XA", 0, 80), kv80, OP.min)
@@ -845,6 +903,8 @@ def rank_program(g, core, T, topo):
                         in_row("v")
                 for lo2, hi2 in pieces(X, V, X):
                     new_w("W1", lo2, hi2)
+                    if KROW > 1:
+                        in_row("k")
                 ghosts = [send(9, a("W1", 0, X), "h")]
                 colsum("PU", 0, "AB", 0, 8, "ends", ee(4))
                 scan(a("SC", 0, 64), a("M8", 0, 64), a("PU", 0, 64), OP.mult, OP.add)
@@ -878,7 +938,8 @@ def rank_program(g, core, T, topo):
                 for i, x in enumerate((ind(Wt, fb(WS, V)), ind(a(W), fa(WS, V)))):
                     act(a("MS", V * i + WS, V * i + V), x)
                     in_row("s")
-                mm(a("PD0", 0, V - WS), [(quart, a("ONES", 0, V - WS)), (half, a("MS", WS, V)), (half, a("MS", V + WS, 2 * V))])
+                for pair in ((quart, a("ONES", 0, V - WS)), (half, a("MS", WS, V)), (half, a("MS", V + WS, 2 * V))):
+                    mm(a("PD0", 0, V - WS), [pair], grp="halves")
                 whole(a("YW", WS, V), a("PD0", 0, V - WS))
                 dma("y", [], [a("YW", WS, V)], T.yw[:, WS:V], T.YW[:, WS:V], "o5", 2.2)
 

from concourse.bass import DstId, RemoteDMATransfer
from concourse.mybir import AluOpType as OP, ActivationFunctionType as AF, AxisListType as AX

V, X, NP, RO, EP = 1280, 256, 10, 4, 2
Z = 2560
WT = 2576
DV = float(Z * 4097)
BIG = float(2 ** 21)
MAGIC = 12582912.0
MID = 98304.0
C0 = 1280.3125
NX = [10, 20, 30, 40]
XO = [0, 10, 30, 60]
CO = [0, 100, 110, 130]
EV = [0, 2, 3, 3]
KS = [0, 10, 15, 20]
SP = [0, 1, 2, 3]
LV = 512
XV = 512
GV = [0, 512, 512, 512]
NQ = [0, 1, 2, 2]
WS = 960
CL = [0, 1.0, 1.0, 1.0]
CA = [0, 1, 2, 3]
RP = [0, -1, -2, -3]
SPLIT = 2
PS2 = 0
GZ = 2
L0 = 2.0
GO = -1
EROW = 0
SROW = (3,)
LP = [0, 0, 2, 1]
ES = 0
TS = [0, 0, 0, 0]
LATE = [1.0, 0.3, 0.0, 0.0]
KROW = 2
GA = 1.6
GF = [0.5, 0.3]
GN = [0.0, 0.8]
PF = 0.01
TAIL = 2
LAST = 8
PIECE = 10
FINE = 512

CY = 1.0e-3
SEM = 0.14
SWEEPS = 0
ROOM = 2
NEAR = 1.6
STEP = 0.5
FAR = 2.2

F, B16, I32, U16, H16 = "float32", "bfloat16", "int32", "uint16", "float16"
SB_ = {
    "W0": (WT + V, B16), "W1": (WT + V, B16), "ONES": (512, B16), "LT": (WT, B16), "YW": (V, B16), "RT": (V, B16),
    "KP": (WT, F), "WA": (WT + V, I32), "K2": (V, I32), "WB": (WT, F), "CI": (V, F), "TL": (7 * V, F),
    "G0": (V, F), "G1": (V, F), "GB": (V, F), "M": (5 * V, B16), "MS": (3 * V, B16), "XS": (3 * V, B16), "AA": (2048, B16),
    "SND": (320, F), "LAND": (1840, F), "US": (40, F), "E4": (40, F), "SGN": (128, F), "ID32": (128, F),
    "PEN": (72, F), "PEN0": (72, F), "NU": (32, F), "MM": (64, F), "KT": (64, F), "T1": (64, F), "S1": (64, F),
    "BI": (64, F), "BJ": (64, F), "C6": (64, F), "GG": (64, F), "D1": (64, F), "S2": (64, F), "OFF": (12, U16),
    "RL": (160, H16), "RM": (80, F), "DMM": (80, H16), "LY": (V, B16), "DM": (80, B16), "EE": (640, H16), "AB": (V, H16), "LB": (80, F), "B0": (400, F), "B1": (400, F),
    "LU": (400, U16), "LL": (80, U16), "DZB": (80, B16), "NEQ": (240, B16), "XU": (240, U16),
    "EQ": (240, B16), "SC": (512, F), "SD": (128, F), "SBP": (32, F), "SBP0": (32, F), "LC": (80, F), "EQH": (32, F), "EQL": (32, F),
    "NHT": (40, F), "HD": (40, F), "HS": (40, F), "HT": (24, F), "OFB": (6, U16), "CM": (16, F),
    "XA": (160, F), "BH": (80, H16), "AM": (80, F), "FL": (160, U16), "BS": (160, F),
    "PI": (8, I32), "PF": (8, F), "PG": (16, F), "CC": (8, F), "J": (128, F), "JG": (128, F), "TH": (168, F), "LI": (160, U16),
    "ID": (128, B16), "NEG": (128, B16), "BO": (256, B16), "CS": (1152, B16), "RC": (32, B16), "M8": (256, F), "M16": (64, F),
    "BG": (4, U16), "GR": (4, U16), "TF": (32, F),
}
PS_ = ["PU", "PC", "PR", "PL", "PD0", "PD1", "PD2", "PD3"]
SCRATCH = {k: ("sbuf", [128, n], d) for k, (n, d) in SB_.items()}
SCRATCH.update({k: ("psum", [128, 512], F) for k in PS_})
SEMAPHORES = (["qv", "qs", "qp", "qg", "lw0", "lw1", "lk0", "lk1", "lk2", "ck", "o0", "o1", "o2", "o3", "o4", "o5", "sent"]
              + ["%s%d" % (nm, i) for nm in ("n0m", "n1m", "n2m", "n3m", "af", "ag", "rl") for i in range(16)])
GHOSTS = (8, 9)


def side(s, near):
    peers = sorted(near[s] + [s])
    return 2 * peers.index(s) // len(peers)


def near_parts(r, near):
    return sorted(near[r], key=lambda q: near[q].index(r))


def near_sem(s, near, m):
    return "n%dm%d" % (sorted(near[s] + [s]).index(s), m)


def far_parts(r, near):
    far = [q for q in range(len(near)) if q != r and r not in near[q]]
    return [[q for q in far if side(q, near) == side(r, near) ^ j] for j in range(2)]


def routes(T, topo):
    cores = list(T.cores)
    near, help_ = [], ([], [])
    for s, c in enumerate(cores):
        near.append([r for r, d in enumerate(cores) if r != s and topo.may_write(c, d)])
        near[s] = [r for r in near[s] if r > s] + [r for r in near[s] if r < s]
    for s, c in enumerate(cores):
        far = [r for r in range(len(cores)) if r != s and r not in near[s]][::-1 if side(s, near) else 1]
        able = [h for h in topo.cores_of(c) if T.rank_of(h) is None and all(topo.may_write(h, cores[r]) for r in far)]
        for kind in range(2):
            hs = [h for h in able if (topo.die(h) == topo.die(c)) == (kind == 0)][:2]
            help_[kind].append([(h, far[i::len(hs)]) for i, h in enumerate(hs)])
    return near, help_


def message(T, m, s, r, near):
    n_ranks = len(T.cores)
    if m in GHOSTS:
        w = T["W%d" % (m - 8)]
        d = (r - s) % n_ranks
        return w[:, 0:X], w[:, V + (d - 1) * X:V + d * X]
    o, n = columns(m)
    order = near_parts(r, near) + sum(far_parts(r, near), [])
    k = order.index(s) if s != r else 0
    at = land_at(m, k)
    return T.SND[:, o:o + n], T.LAND[:, at:at + n]


def columns(m):
    e, t = divmod(m, RO) if m < 8 else divmod(m - 10, RO - 1)
    return (160 * e + XO[t], NX[t]) if m < 8 else (160 * e + CO[t + 1], NX[t])


def land_at(m, k):
    wide = lambda x: (columns(x)[1] + 7) // 8 * 8
    return 5 * sum(wide(x) for x in range(m) if x not in GHOSTS) + k * wide(m)


def fan_mask(topo, src_core, dst_cores):
    mask = -1
    for d in dst_cores:
        mask &= topo.mask(src_core, d)
    return mask


def fan_count(topo, src_core, dst_cores):
    return bin(fan_mask(topo, src_core, dst_cores)).count("1")


def relay_mask(T, topo, m, s, near, help_):
    cores = list(T.cores)
    every = fan_mask(topo, cores[s], [h for h, _ in help_[m >= 8][s]])
    out = fan_mask(topo, cores[s], [cores[r] for r in near[s]])
    return every & ~out if m == 8 else out if m == 0 else every


def near_by(m, s, near, help_):
    free = [h for h, fars in help_[1][s] if len(fars) < 2] if m > 8 else []
    by = {h: [r] for h, r in zip(free, near[s][1:])}
    by[None] = near[s][:len(near[s]) - len(by)] if not by else near[s][:1] + near[s][1 + len(by):]
    return by


def fan(g, T, topo, src_core, dsts, src, sem, mask=-1):
    mask &= fan_mask(topo, src_core, [d for d, _ in dsts])
    ad = [topo.addr(d, src_core) for d, _ in dsts]
    if len(dsts) == 1:
        g.remote_dma(dsts[0][1], src, sem, T.sem.sent, ad[0][1], ad[0][0], mask)
    else:
        g.remote_dma_fused([RemoteDMATransfer(dst_ids=[DstId(rid=r, pnc=p) for r, p in ad], dma_engine_mask=mask,
                                              remote_sem=sem, srcs=[src], dsts=[p for _, p in dsts])],
                           local_sem=T.sem.sent)
    return bin(mask).count("1")


def helper_program(g, core, T, topo, s, near, help_):
    cores = list(T.cores)
    sent = 0
    for m in [0, 8, 10, 1, 11, 2, 12, 3, 4, 9, 13, 5, 14, 6, 15, 7]:
        helpers = help_[m >= 8][s]
        for h, fars in helpers:
            if h == core:
                g.wait_ge(T.sem["rl%d" % m], bin(relay_mask(T, topo, m, s, near, help_)).count("1"))
                src = message(T, m, s, s, near)[0]
                sent += fan(g, T, topo, core, [(cores[r], message(T, m, s, r, near)[1]) for r in fars], src,
                            T.sem["a%s%d" % ("fg"[side(s, near)], m)])
                for r in near_by(m, s, near, help_).get(h, []):
                    sent += fan(g, T, topo, core, [(cores[r], message(T, m, s, r, near)[1])], src, T.sem[near_sem(s, near, m)])
    if sent:
        g.wait_ge(T.sem.sent, sent)


def depends(ops):
    hist, lead = {}, {}
    for i, o in enumerate(ops):
        hard, soft = set(), set()
        for kind in ("rd", "wr"):
            for nm, lo, hi in o[kind]:
                for l2, h2, k2, j in hist.get(nm, []):
                    hit = (kind == "wr" or k2 == "wr") and lo < h2 and l2 < hi
                    if nm in PS_ and ops[j]["q"] != o["q"]:
                        hard.add(j)
                    elif nm in PS_ and o["q"] == "p":
                        if o["grp"] is None or o["grp"] != ops[j]["grp"]:
                            soft.add(j)
                    elif hit and ops[j]["sem"] != "none":
                        hard.add(j)
        if lead.setdefault(o["grp"], i) != i and o["grp"]:
            soft.add(lead[o["grp"]])
        o["hard"], o["soft"] = hard, soft - hard
        for kind in ("rd", "wr"):
            for nm, lo, hi in o[kind]:
                hist.setdefault(nm, []).append((lo, hi, kind, i))


def put_in_order(ops):
    edges = []
    for o in ops:
        edges.append([(j, ops[j]["cost"] + ops[j]["lat"] + SEM) for j in o["hard"]] + [(j, ops[j]["cost"]) for j in o["soft"]]
                     + [(j, ops[j]["cost"] + d) for j, d in o["after"]])
    ahead = [o["cost"] + o["lat"] for o in ops]
    for i in range(len(ops) - 1, -1, -1):
        for j, d in edges[i]:
            ahead[j] = max(ahead[j], d + ahead[i])
    back = [[] for _ in ops]
    for i, o in enumerate(ops):
        for j, d in edges[i]:
            back[j].append((i, d + o["cost"] - ops[j]["cost"]))

    def place(order, before, least):
        start, busy = {}, {}
        for i in order:
            t = max([start[j] + d for j, d in before[i]] + [least[i]])
            if ops[i]["q"] != "x":
                line = busy.setdefault(ops[i]["q"], [])
                k = 0
                while k < len(line) and line[k][1] <= t:
                    k += 1
                while k < len(line) and line[k][0] < t + ops[i]["cost"] * (ROOM if ops[i]["q"] == "s" else 1) - 1e-9:
                    t = max(t, line[k][1])
                    k += 1
                line.insert(k, (t, t + ops[i]["cost"]))
            start[i] = t
        return start

    every = range(len(ops))
    zero, lats = [0.0] * len(ops), [o["lat"] for o in ops]
    end = lambda st, i: st[i] + ops[i]["cost"]
    start = best = place(sorted(every, key=lambda i: (-ahead[i], i)), edges, zero)
    span = lambda st: max(end(st, i) + lats[i] for i in every)
    for _ in range(SWEEPS):
        rev = place(sorted(every, key=lambda i: (-end(start, i) - lats[i], -i)), back, lats)
        start = place(sorted(every, key=lambda i: (-end(rev, i), i)), edges, zero)
        if span(start) < span(best):
            best = start
    return sorted(every, key=lambda i: (best[i], i))


def rank_program(g, core, T, topo):
    near, help_ = routes(T, topo)
    rank = T.rank_of(core)
    if rank is None:
        for s, c in enumerate(T.cores):
            if core in topo.cores_of(c):
                helper_program(g, core, T, topo, s, near, help_)
        return
    cores = list(T.cores)
    NR = len(cores)
    src_near = near_parts(rank, near)
    src_far = far_parts(rank, near)
    cnt_near = [fan_count(topo, cores[q], [cores[r] for r in near[q]]) for q in src_near]
    cnt_far = [sum(fan_count(topo, h, [cores[r] for r in fars]) for q in part for h, fars in help_[0][q] if rank in fars)
               for part in src_far]
    sem_far = ["a" + "fg"[side(rank, near) ^ j] for j in range(2)]

    ops = []

    def a(name, lo=0, hi=None, st=1):
        if hi is None:
            hi = SB_[name][0]
        ap = T[name][:, lo:hi] if st == 1 else T[name][:, lo:hi:st]
        return {"ap": ap, "r": [(name, lo, hi)], "n": len(range(lo, hi, st)), "ps": name in PS_,
                "two": name not in PS_ and SB_[name][1] in (B16, H16, U16)}

    def ind(win, off):
        return {"ap": win["ap"].indirect(off["ap"]), "r": win["r"] + off["r"], "w": win["r"], "o": off["r"],
                "n": 16 * off["n"], "ps": False, "two": False}

    def val(x):
        return x["ap"] if isinstance(x, dict) else x

    def add(q, outs, ins, fn, cost, sem=None, lat=0.0, after=(), grp=None):
        rd, wr = [], []
        for x in ins:
            if isinstance(x, dict):
                rd += x["r"]
        for x in outs:
            wr += x.get("w", x["r"])
            rd += x.get("o", [])
        ops.append({"q": q, "rd": rd, "wr": wr, "fn": fn, "sem": sem, "cost": cost, "lat": lat, "after": list(after), "grp": grp})
        return len(ops) - 1

    rows = {}

    def in_row(name):
        if name in rows:
            ops[-1]["after"].append((rows[name], 0.0))
        rows[name] = len(ops) - 1

    def vcost(o, x, rate=None):
        if "o" in o:
            return 0.05 + 3 * CY * x["n"]
        if "o" in x:
            return 0.05 + GA * CY * x["n"]
        if rate is None:
            rate = 0.5 if o["two"] and x["two"] else 1
        return CY * max(64, rate * x["n"])

    def arrive(outs, sem, n, after):
        add("x", outs, [], None, 0.01, (sem, n), after=[after])

    def tt(o, x, y, op):
        add("v", [o], [x, y], lambda e: e.tensor_tensor(o["ap"], x["ap"], y["ap"], op), vcost(o, x, 1 if x["ps"] or y["ps"] else 2))

    def ts(o, x, s1, op0, s2=None, op1=None):
        if op1 is None:
            add("v", [o], [x, s1], lambda e: e.tensor_scalar(o["ap"], x["ap"], val(s1), None, op0), vcost(o, x))
        else:
            add("v", [o], [x, s1, s2], lambda e: e.tensor_scalar(o["ap"], x["ap"], val(s1), val(s2), op0, op1), vcost(o, x))

    def whole(o, x):
        ts(o, x, MAGIC, OP.add, MAGIC, OP.subtract)

    def cp(o, x):
        add("v", [o], [x], lambda e: e.tensor_copy(o["ap"], x["ap"]), vcost(o, x))

    def ms(o, c):
        add("v", [o], [], lambda e: e.memset(o["ap"], c), vcost(o, o))

    def tr(o, x):
        add("v", [o], [x], lambda e: e.transpose(o["ap"], x["ap"]), vcost(o, x))

    def scan(o, d0, d1, op0, op1):
        add("v", [o], [d0, d1], lambda e: e.tensor_tensor_scan(o["ap"], d0["ap"], d1["ap"], 0.0, op0, op1), vcost(o, d1))

    def rowsum(o, x, negate=True):
        add("v", [o], [x], lambda e: e.tensor_reduce(o["ap"], x["ap"], AX.X, OP.add, negate=negate), vcost(o, x, 1))

    def act(o, x, f=AF.Identity, bias=0.0, scale=1.0, acc=None):
        cost = 0.065 + GA * CY * x["n"] if "o" in x else 0.09 + CY * x["n"]
        if acc is None:
            add("s", [o], [x, bias], lambda e: e.activation(o["ap"], x["ap"], f, bias=val(bias), scale=scale), cost)
        else:
            add("s", [o, acc], [x], lambda e: e.activation(o["ap"], x["ap"], f, scale=scale, accum_out=acc["ap"]), cost + 0.02)

    def mm(o, pairs, start=True, stop=True, grp=None):
        def fn(e, first=start, final=stop):
            last = None
            for i, (l, r) in enumerate(pairs):
                last = e.matmul(o["ap"], l["ap"], r["ap"], first and i == 0, final and i == len(pairs) - 1)
            return last
        cost = sum(PF + 0.5 * CY * max(64, r["n"]) * (1 if r["two"] else 4) for l, r in pairs)
        add("p", [o], [x for p in pairs for x in p], fn, cost, grp=grp)

    def iota(o, pat, base=0, cm=0, fl=True):
        cost = 0.13 + 2 * CY * o["n"]
        if fl:
            add("g", [o], [], lambda e: e.iota(o["ap"], pat, base, cm, allow_small_or_imprecise_dtypes=True), cost)
        else:
            add("g", [o], [], lambda e: e.iota(o["ap"], pat, base, cm), cost)

    def dma(q, outs, ins, o, i, sem, lat):
        add(q, outs, ins, lambda e: e.dma_start(o, i), 0.1, (sem, 16), lat=lat)

    sent, sends = [0], []

    def send(m, src, to="hn", cost=0.3):
        def fn(e):
            ap = message(T, m, rank, rank, near)[0]
            hs = help_[m >= 8][rank]
            if hs and "h" in to:
                sent[0] += fan(e, T, topo, core, [(h, ap) for h, _ in hs], ap, T.sem["rl%d" % m],
                               relay_mask(T, topo, m, rank, near, help_))
            if near[rank] and "n" in to:
                sent[0] += fan(e, T, topo, core, [(cores[r], message(T, m, rank, r, near)[1]) for r in near_by(m, rank, near, help_)[None]],
                               ap, T.sem[near_sem(rank, near, m)])
        sends.append(add("g", [], [src], fn, cost * len(to), "none", after=[(j, 0.0) for j in sends[-1:]]))
        return sends[-1]

    col = lambda name, j: a(name, j, j + 1)
    v80, kv80 = a("BS", 0, 80), a("BS", 80, 160)
    cs = lambda j: a("CS", 128 * j, 128 * j + 128)
    n8k, n24, cdv, i4k, mid_r, mid_l, half, quart, i8 = [cs(j) for j in range(9)]
    ee = lambda j: a("EE", 128 * j, 128 * j + 128)
    thirds = [(0, 512), (512, 1024), (1024, V)]
    pieces = lambda lo, hi, n: [(x, min(x + n, hi)) for x in range(lo, hi, n)]

    def colsum(ps, at, src, u0, u1, grp, one=None):
        for j in range(4):
            mm(a(ps, at, at + 8 * (u1 - u0)), [(one or a("ID"), a(src, 128 * u0 + i, 128 * u1, 16)) for i in range(4 * j, 4 * j + 4)], grp=grp)
            in_row("p")

    def absent(ps, at, w, lo, hi):
        mm(a(ps, at, at + hi - lo), [(cdv, a("ONES", 0, hi - lo)), (n24, a(w, lo, hi))])

    def chunks_of(t):
        n = KS[t] - EV[t]
        nch = max(min(4, (n + 2) // 3), (n + 3) // 4)
        return [(EV[t] + n * i // nch, EV[t] + n * (i + 1) // nch) for i in range(nch)]

    def unwrapped(k0, k1):
        cuts = [k0] + [k for k in range(k0 + 1, k1) if k % NP == 0] + [k1]
        return list(zip(cuts, cuts[1:]))

    def roots(w, i, k0, k1):
        for n, (x0, x1) in enumerate(unwrapped(k0, k1)):
            mm(a("PD%d" % (i % 4), 128 * (x0 - k0), 128 * (x1 - k0)),
               [(a("ID"), a(w, 128 * (x0 % NP), 128 * (x0 % NP + x1 - x0)))], n == 0, False)

    def roots_ahead(w, t):
        for i, (k0, k1) in enumerate(chunks_of(t)[:4]):
            roots(w, i, k0, k1)

    def dead_term(t):
        for ps, mid_, big in (("PR", mid_r, i4k), ("PL", mid_l, a("ID"))):
            mm(a(ps, 0, 80), [(mid_, a("ONES", 0, 80))] + ([(big, a("DM"))] if t > 1 else []), True, False)

    def swap(ps, lo):
        for par in range(2):
            mm(a(ps, par, 80, 2), [(ee(2 * par + q), a("RL", lo + q, lo + 80, 2)) for q in range(2)], False, par == 1)

    def turn(src, at, lo, hi=V):
        for x0, x1 in pieces(lo, max(lo, min(hi, V - FINE)), 256) + pieces(max(lo, V - FINE), hi, 128):
            tr(a("TL", at + x0, at + x1), a(src, x0, x1))

    def landed(m, call, late):
        land = lambda k: a("LAND", land_at(m, k), land_at(m, k) + columns(m)[1])
        nn, nf = len(src_near), len(src_far[0])
        for k in range(nn):
            arrive([land(k)], near_sem(src_near[k], near, m), cnt_near[k], (call, NEAR + STEP * k))
        for j in range(2):
            arrive([land(nn + j * nf + k) for k in range(nf)], "%s%d" % (sem_far[j], m), cnt_far[j], (call, FAR + STEP * j + late))
        return [land(k) for k in range(NR - 1)]

    dma("y", [a("W0", 0, X)], [], T.W0[:, 0:X], T.w[:, 0:X], "lw0", 2.2)
    in_row("y")
    dma("y", [a("W0", X, V)], [], T.W0[:, X:V], T.w[:, X:V], "lw1", 2.8)
    in_row("y")
    for i, (lo, hi) in enumerate(thirds):
        dma("y", [a("WA", WT + lo, WT + hi)], [], T.WA[:, WT + lo:WT + hi], T.kids[:, lo:hi], "lk%d" % i, 3.5 + i)
        in_row("y")
    iota(col("PI", 0), [[0, 1]], 0, 1, False)
    iota(a("J"), [[1, 128]])
    ghosts = [send(8, a("W0", 0, X), "h", 3.0)]
    ms(a("M8"), 1.0)
    ms(a("M16"), 0.0)
    ms(a("KT"), 0.0)
    ms(a("SGN"), 1.0)
    p0 = col("PI", 0)
    ts(col("PI", 1), p0, 15, OP.bitwise_and)
    ts(col("PI", 2), p0, 4, OP.arith_shift_right)
    ts(col("PI", 3), p0, 3, OP.arith_shift_right, 1, OP.bitwise_and)
    ts(col("PI", 4), p0, 4, OP.arith_shift_right, 1, OP.bitwise_and)
    ts(col("PI", 5), p0, 1, OP.bitwise_and)
    ts(col("PI", 6), p0, 31, OP.bitwise_and)
    ms(a("M8", 0, 256, 8), 0.0)
    ms(a("M16", 0, 64, 16), 1e9)
    cp(a("PF", 0, 7), a("PI", 0, 7))
    ms(a("D1"), -80.0)
    ms(a("PEN0"), 2.0 ** 18)
    pp, pa, pg, phi, hi_, odd, p32 = [col("PF", j) for j in range(7)]
    ts(a("ID"), a("J"), pp, OP.is_equal)
    ts(a("ID32"), a("J"), pp, OP.is_equal)
    ts(col("PG", 0), hi_, -32.0, OP.mult, 16.0, OP.add)
    ts(col("PG", 1), pg, -256.0, OP.mult)
    ts(col("PG", 2), phi, -1.0, OP.mult, 1.0, OP.add)
    ts(col("PG", 3), hi_, -1.0, OP.mult, 1.0, OP.add)
    ts(col("PG", 4), phi, 32.0, OP.mult, 15.0, OP.add)
    ts(col("PG", 9), p32, -5.0, OP.add, 1.0 / 6, OP.mult)
    ts(col("PG", 12), pa, 16.0, OP.mult, 31.5, OP.add)
    ts(a("TF", 0, 4), a("J", 0, 4), 16.0, OP.mult, 64 * MID - 31.5, OP.add)
    ts(v80, a("J", 0, 80), 16.0, OP.mult, pa, OP.add)
    tt(col("PG", 5), col("PG", 0), pp, OP.add)
    whole(col("PG", 10), col("PG", 9))
    ts(col("PG", 11), col("PG", 10), 4.0, OP.mult, MAGIC, OP.add)
    ts(a("CC", 0, 4), a("TF", 0, 4), pa, OP.add, 1.0 / 64, OP.mult)
    ts(a("TF", 4, 6), a("J", 0, 2), 0.0, OP.mult, odd, OP.add)
    cp(a("TF", 6, 8), a("J", 0, 2))
    ts(a("TF", 16, 20), a("BS", 0, 4), -2.0, OP.add, 0.2, OP.mult)
    ts(a("BG"), a("TF", 4, 8), 16.0, OP.mult, col("PG", 4), OP.add)
    whole(a("TF", 20, 24), a("TF", 16, 20))
    for h in (0, 2, 3):
        ts(a("PEN0", 30 - 10 * h, 40 - 10 * h), a("J", 0, 10), 0.0, OP.mult, col("CC", h), OP.add)
    ts(a("TF", 8, 12), a("TF", 20, 24), 6.0, OP.is_ge, -4.0, OP.mult)
    ts(a("TF", 24, 28), a("TF", 20, 24), 6.0, OP.mult, 5.0, OP.add)
    for j, (tgt, msk) in enumerate([(pp, col("PG", 3)), (col("PG", 5), col("PG", 3)), (col("PG", 5), hi_), (pp, hi_)]):
        ts(ee(j), a("J"), tgt, OP.is_equal, msk, OP.mult)
    for k in range(NP):
        own = a("W0", 128 * k, 128 * k + 128)
        if k in (0, 1, 4, 6, 8):
            act(a("M", 128 * k, 128 * k + 128), own, scale=-1.0, acc=col("SND", k))
        else:
            rowsum(col("SND", k), own)
    sums = send(0, a("SND", 0, 10), "h", 0.6)
    for m, x in [(8, a("W0", 0, X)), (0, a("SND", 0, 10))][::GO]:
        send(m, x, "n")
    for x in ((a("JG"), [[1, 8], [0, 16]]), (a("TH", 0, 65), [[0, 13], [1, 5]]), (a("TH", 72, 162), [[0, 3], [8, 6], [0, 5]], 21),
              (a("SBP0", 0, 25), [[256, 5], [-(2 * V - 16), 5]], 3 * (2 * V - 16) + 63, 16),
              (a("LC", 0, 75), [[2 * V, 3], [256, 5], [16, 5]], V + 15, 16), (a("CI"), [[4097, V]], V * 4097),
              (a("LY"), [[0, V]]), (a("LT", V, WT), [[0, WT - V]]))[:6 + GZ]:
        iota(*x)
        ops[-1]["after"].append((sends[-1], 0.0))
        in_row("g")
    act(a("SBP0", 0, 25), a("SBP0", 0, 25), bias=col("PG", 1))
    act(a("SBP0", 4, 25, 5), a("J", 0, 5), scale=0.0)
    ts(ee(4), a("J"), pp, OP.is_equal)
    act(a("NEG"), a("ID"), scale=-1.0)
    ms(a("KP", Z, WT), DV)
    ms(a("W0", Z, WT), 0.0)
    for i, (lo, hi) in enumerate(thirds):
        act(a("PD%d" % i, 0, hi - lo), a("W0", lo, hi), AF.Relu, bias=DV, scale=-DV)
    act(a("ONES", 0, 512), a("W0", 0, 512), bias=1.0, scale=0.0)
    tt(a("TF", 12, 16), a("TF", 8, 12), a("TF", 24, 28), OP.add)
    act(a("LC", 0, 75), a("LC", 0, 75), bias=col("PG", 1))
    act(a("TH", 0, 65), a("TH", 0, 65), bias=0.5, scale=-0.25)
    act(a("TH", 75, 162, 5), a("TH", 75, 162, 5), bias=-1.125)
    act(a("TH", 76, 162, 5), a("TH", 76, 162, 5), bias=-2.0)
    ts(col("PG", 13), col("PG", 10), 8.0, OP.mult, MAGIC + V / 64, OP.add)
    ts(col("PG", 15), odd, -16.0, OP.mult, 31.5, OP.add)
    ts(col("PG", 14), pa, 32.0, OP.mult, col("PG", 15), OP.add)
    for j, (nm, s_, x) in enumerate((("SBP0", 2, V + 47.5), ("LC", 3, V + 31.5))):
        ts(col("CC", 5 + j), col("PG", 14), x, OP.add)
        act(a(nm, s_, 25, 5), a("J", 0, 5), bias=col("CC", 5 + j), scale=512.0)
    ts(a("PEN0", 20, 30), a("PEN0", 30, 40), 0.5, OP.add)
    ts(col("CC", 4), col("CC", 0), -1.0, OP.mult)
    for t in range(1, RO):
        ms(a("SGN", 32 * t, 32 * t + EV[t]), -1.0)
    ts(a("GR"), a("TF", 12, 16), 63.0, OP.min)
    ms(a("NHT"), 0.0)
    ts(a("D1", 33, 54, 5), a("BS", 0, 5), 320.0, OP.add)
    ms(a("D1", 34, 55, 5), 0.0)
    ts(col("PG", 6), pp, 0.0, OP.is_equal, 4096.0 * Z, OP.mult)
    ts(col("PG", 7), pp, 1.0, OP.is_equal, float(Z), OP.mult)
    ts(n24, a("ID"), -2.0 ** 24, OP.mult)
    tt(col("PG", 8), col("PG", 6), col("PG", 7), OP.add)
    for j, x in enumerate((-2.0 ** 19, 2.0 ** 19)):
        ts(a("BO", 128 * j, 128 * j + 128), a("JG"), pg, OP.is_equal, x, OP.mult)
    ts(cdv, a("J"), 0.0, OP.mult, col("PG", 8), OP.add)
    for c_, x in ((n8k, -8192.0), (i4k, 4096.0), (mid_r, 1280.0), (mid_l, 0.3125), (half, 0.5), (quart, -0.25), (i8, 8.0)):
        act(c_, a("ID"), scale=x)
    for x in (a("LY"), a("LT", V, WT))[GZ:]:
        for lo, hi in pieces(x["r"][0][1], x["r"][0][2], 224):
            ms(a(x["r"][0][0], lo, hi), 0.0)
    act(kv80, v80, bias=float(WT))
    ms(a("HD"), -80.0)
    for w in ("W1", "WB"):
        act(a(w, Z, WT), a("J", 0, 16), scale=0.0)
    for lo in (3, 7):
        act(a("HD", lo, 40, 8), a("J", 0, 5), bias=240.0, scale=16.0)
    ms(a("B0", 0, 160), 0.0)
    ms(a("B1", 0, 240), 0.0)

    def end_table(t):
        if t == 1:
            iota(a("WA", 0, WT), [[1, WT]], 0, 0, False)
        elif t == 2:
            iota(a("WB", 0, Z), [[4096, Z]])
        else:
            for i in range(4):
                add("g", [a("AA", 512 * i, 512 * i + 512)], [a("ONES")],
                    lambda en, i=i: en.affine_select(T.AA[:, 512 * i:512 * i + 512], T.ONES[:, 0:512], [[-1000, 4], [-16, 8], [1000, 16]],
                                                     OP.is_equal, 0.0, -4000 * i, 1), 1.2, after=[(sends[-1], 0.0)])
        ops[-1]["after"].append((sends[-1], 0.0))

    for e in range(EP):
        W = "W%d" % e
        Wt = a(W, 0, WT)
        kin = "WA" if e == 0 else "K2"
        ko = WT if e == 0 else 0
        late = L0 * (1 - e)
        act(a("SBP", 0, 25), a("SBP0", 0, 25))
        act(a("PEN", 0, 70), a("PEN0", 0, 70))
        part = lambda x, lo=0: mm(a("PU", lo, lo + x["n"]), [(a("ID32"), x)], grp="sum%d" % len(sends))
        part(a("SND", 160 * e, 160 * e + 10))
        part(a("PEN0", 30, 40))
        for i, (lo, hi) in enumerate(thirds if e else []):
            absent("PD%d" % i, 0, W, lo, hi)
        for x0 in range(0, V + X, X):
            if e > 0 and x0 < V:
                act(a("G1", x0, x0 + X), ind(a("WB"), a("FL", 80 + x0 // 16, 96 + x0 // 16)))
                tt(a("K2", x0, x0 + X), ind(a("WA"), a("FL", x0 // 16, 16 + x0 // 16)), a("G1", x0, x0 + X), OP.add)
                if KROW:
                    in_row("k")
            if x0:
                y0 = x0 - X
                tt(a("KP", y0, x0), a(kin, ko + y0, ko + x0), a("PD%d" % (y0 // 512), y0 % 512, y0 % 512 + X), OP.max)
                if KROW:
                    in_row("k")
                act(a("G0", y0, x0), a("KP", y0, x0), bias=-C0, scale=1.0 / 4096)
        turn("G0", 0, 0)
        dead_term(1)
        roots_ahead(W, 1)
        for lo, hi in pieces(0, V, 320):
            act(a("RT", lo, hi), a(W, lo, hi))
        gh = lambda q: V + ((rank - q) % NR - 1) * X
        for j in range(2):
            arrive([a(W, gh(q), gh(q) + X) for q in src_far[j]], "%s%d" % (sem_far[j], 8 + e), cnt_far[j],
                   (sums, FAR + late + GF[e] + STEP * j))
        for k, q in enumerate(src_near):
            arrive([a(W, gh(q), gh(q) + X)], near_sem(q, near, 8 + e), cnt_near[k], (sums, FAR + late + GN[e] + STEP * k))
        kinds = [src_near, src_far[0] + src_far[1]][::-1 if e else 1]
        for ps, two in zip(("PC", "PD3", "PD3"), [kind[i:i + 2] for kind in kinds for i in range(0, len(kind), 2)]):
            for i, q in enumerate(two):
                absent(ps, X * i, W, gh(q), gh(q) + X)
            for i, q in enumerate(two):
                for x0 in (0, 128):
                    tt(a("KP", gh(q) + x0, gh(q) + x0 + 128), a("CI", gh(q) - V + x0, gh(q) - V + x0 + 128),
                       a(ps, X * i + x0, X * i + x0 + 128), OP.max)
        for lo, hi in pieces(0, V, 320):
            act(a(W, WT + lo, WT + hi), a(W, lo, hi), scale=2.0)

        for t in range(1, RO + 1):
            m = RO * e + t - 1
            n = NX[t - 1]
            parts = landed(m, sums, LATE[t - 1] + (late if t == 1 else 0))
            nf = len(src_far[1])
            for x in parts[:-nf]:
                part(x)
            last, (nm, at, _) = parts[-1], parts[-1]["r"][0]
            if nf == 2:
                last, nm, at = a("E4", 0, n), "E4", 0
                tt(last, parts[-2], parts[-1], OP.add)
            kt = lambda par: a("KT", 32 * par + 5, 32 * par + 30, 6)
            if t == 1:
                for par in range(2):
                    tt(kt(par), a("PU", par, 10, 2), a(nm, at + par, at + 10, 2), OP.add)
                tt(a("US", 0, n), a("PU", 0, n), last, OP.add)
            else:
                tt(a("US", 0, n), a("PU", 0, n), last, OP.add)
                if t > 2:
                    tt(a("MM", 0, n - 20), a("US", 0, n - 20), a("US", 20, n), OP.min)
                for par in range(2):
                    tt(kt(par), a("MM" if t > 2 else "US", par, 10, 2), a("MM" if t > 3 else "US", 10 + par, 20, 2), OP.min)
            tr(a("T1"), a("KT"))
            scan(a("S1"), a("M16"), a("T1"), OP.add, OP.min)
            nb = 32 if t == 1 else 64
            best = ind(a("S1"), a("BG", 0, nb // 16))
            ts(a("BI", 0, nb), best, MAGIC, OP.add, col("PG", 9 + 2 * t) if t < 3 else MAGIC, OP.subtract)
            tt(a("BJ", 0, nb), best, a("BI", 0, nb), OP.subtract)
            tr(a("C6", 0, nb), a("BJ", 0, nb))
            if t < 3:
                ts(a("OFF", 0, 5), a("C6", 5, 30, 6), 64.0, OP.mult, col("PG", 10 + 2 * t), OP.add)
            if t > 1:
                lo = 30 if t == 2 else 0
                tt(a("GG"), ind(a("C6"), a("GR")), a("TH", 72 * (t == 2), 72 * (t == 2) + 64), OP.is_gt)
                if t > 2:
                    act(a("D1", 4, 25, 5), a("C6", 5, 30, 6), bias=-31.5, scale=64.0)
                scan(a("S2", lo, 55), a("GG", lo, 55), a("D1", lo, 55), OP.mult, OP.add)
                cp(a("OFF", lo // 5, 11), a("S2", lo + 4, 55, 5))
            if e > 0 and t == 2:
                dma("y", [a("WA", WT, WT + V)], [a("K2"), a("OFF")], T.WA[:, WT:WT + V], T.K2[:, 0:V], "ck", 4.0)
            off, offx = a("OFF", 0, 5), a("OFF", 6, 11)
            tl = a("TL", 0, (2 * t - 1) * V)
            old, new = ("B1", "B0") if t % 2 == 0 else ("B0", "B1")
            if t == RO:
                new = old
            hp = lambda h: 80 * (RO - h)
            lu = lambda c0, c1: a("LU", hp(t) + c0, hp(t) + c1)
            rr, ll = a("RL", 0, 80), a("RL", 80, 160)
            pr, pl = a("PR", 0, 80), a("PL", 0, 80)
            src = ind(tl, off)

            def expanded():
                cp(a("XU", 80 * (t - 2), 80 * (t - 1)), ind(a(old), offx))
                tt(a("EQ", 80 * (t - 2), 80 * (t - 1)), ind(a(old), offx), v80, OP.is_equal)

            if t == RO:
                tt(a("RM"), src, a("DMM"), OP.max)
                ts(a("LY", 0, V, 16), a("RM"), 1279.75, OP.is_lt, 8192.0, OP.mult)
                tr(a("LT", 0, V), a("LY"))
            whole(rr, src)
            if t == RO:
                in_row("v")
                expanded()
            swap("PR", 0)
            tt(ll, src, rr, OP.subtract)
            if t == RO and EROW:
                in_row("v")
            swap("PL", 80)

            if t < RO:
                so = 160 * e + XO[t]
                nu, ks, ev = 10 * (t + 1), KS[t], EV[t]
                bt, bold = a(new, hp(t), hp(t) + 80), a(new, hp(t - 1), 400)
                blk = lambda nm, i: a(nm, hp(t - 1 - i), hp(t - 1 - i) + 80)
                ts(lu(0, 80), pr, float(Z), OP.min)
                if t == 1:
                    ts(lu(80, 160), pl, 4096.0, OP.mult, float(Z), OP.min)
                    ts(bold, pl, 4096.0, OP.mult, float(Z), OP.min)
                    ts(bt, pr, float(Z), OP.min)
                else:
                    dz = a("PR", 80, 160)
                    ts(dz, pr, float(Z), OP.is_ge, float(Z), OP.mult)
                    ts(bt, pr, float(Z), OP.min)
                    ts(a("LB"), pl, 4096.0, OP.mult, float(Z), OP.min)
                    for i in range(t):
                        tt(blk(new, i), blk(old, i), dz, OP.max)
                    cp(ind(a(new), offx), a("LB"))
                    if t in SROW:
                        in_row("v")
                chunks = chunks_of(t)
                sp = chunks[SP[t] - 1][1] if SP[t] else ev
                pe = ks + TAIL
                mid = min(pe + LAST, nu)
                mo = lambda k: k if k < ks else k - mid + sp if k >= mid else k - ks + 36
                votes = "votes%d" % m

                def counts():
                    for i in range(t):
                        tt(a("NEQ", 80 * i, 80 * i + 80), blk(new, i), pr, OP.not_equal)
                        in_row("v")
                    for i in range(t if t > 1 else 0):
                        mm(a("PC", 10 * i, 10 * i + 10), [(a("BO", 128, 256), a("DM", b, 80, 8)) for b in range(8)], i == 0, False)
                    mm(a("PC", 0, 10 * t), [(a("BO", 0, 128), a("NEQ", b, 80 * t, 8)) for b in range(8)], t == 1, True)

                mc = 10 + (RO - 1) * e + t - 1
                co = columns(mc)[0]
                unit = lambda k0, k1: a("M", 128 * mo(k0), 128 * (mo(k0) + k1 - k0))
                runs = [(0, 1), (1, ev)][:ev] + pieces(mid, nu, PIECE) + pieces(pe, mid, PIECE) + [(ks, pe)]
                for i, (k0, k1) in enumerate(sum([unwrapped(*r) for r in runs], [])):
                    if i == LP[t] and t > 1:
                        cp(lu(80, 80 + 80 * t), bold)
                        in_row("v")
                    if i == NQ[t]:
                        counts()
                    r0 = 128 * (k0 % NP)
                    tt(unit(k0, k1), ind(Wt, lu(8 * k0, 8 * k1)), a("RT", r0, r0 + 128 * (k1 - k0)), OP.min)
                    in_row("v")

                def short(i):
                    k0, k1 = chunks[i]
                    pd = "PD%d" % (i % 4)
                    if i < SP[t]:
                        act(unit(k0, k1), a(pd, 0, 128 * (k1 - k0)), AF.Relu)
                        in_row("s")
                    else:
                        for k in range(k0, k1):
                            act(a("MS", 128 * k, 128 * k + 128), a(pd, 128 * (k - k0), 128 * (k - k0 + 1)), AF.Relu,
                                acc=col("SND", so + k))
                            in_row("s")

                for i, (k0, k1) in enumerate(chunks):
                    mk = a("MS", 128 * k0, 128 * k1)
                    act(mk, ind(Wt, lu(8 * k0, 8 * k1)))
                    in_row("s")
                    if i >= 4:
                        roots(W, i, k0, k1)
                    mm(a("PD%d" % (i % 4), 0, 128 * (k1 - k0)), [(a("NEG"), mk)], False, True)
                    if i == CA[t]:
                        act(a("SND", co, co + 10 * t), a("PC", 0, 10 * t))
                        in_row("s")
                        ahead = send(mc, a("SND", co, co + 10 * t))
                    if i:
                        short(i - 1)
                short(len(chunks) - 1)
                cut = chunks[SP[t] - 2][1] if SP[t] > SPLIT else 0
                for u0, u1 in ([(0, cut), (sp, mo(nu)), (cut, sp)] if SP[t] else [(0, mo(nu))]):
                    if u1 > u0:
                        colsum("PU", 8 * u0, "M", u0, u1, votes)
                w8 = 8 * mo(nu)
                scan(a("SC", 0, w8), a("M8", 0, w8), a("PU", 0, w8), OP.mult, OP.add)
                if sp > ev:
                    tt(a("SND", so, so + sp), a("SC", 7, 8 * sp, 8), a("SGN", 32 * t, 32 * t + sp), OP.mult)
                else:
                    ts(a("SND", so, so + ev), a("SC", 7, 8 * ev, 8), -1.0, OP.mult)
                if mid < nu and ES:
                    act(a("SND", so + mid, so + nu), a("SC", 8 * sp + 7, w8, 8), scale=-1.0)
                    in_row("s")
                elif mid < nu:
                    ts(a("SND", so + mid, so + nu), a("SC", 8 * sp + 7, w8, 8), -1.0, OP.mult)
                w8 = 8 * (mid - pe)
                colsum("PL", 128, "M", mo(pe), mo(pe) + mid - pe, "last%d" % m)
                scan(a("SD", 0, w8), a("M8", 0, w8), a("PL", 128, 128 + w8), OP.mult, OP.add)
                for k in range(ks, pe):
                    if k < ks + TS[t]:
                        act(unit(k, k + 1), unit(k, k + 1), scale=-1.0, acc=col("SND", so + k))
                        in_row("s")
                    else:
                        rowsum(col("SND", so + k), unit(k, k + 1))
                ts(a("SND", so + pe, so + mid), a("SD", 7, w8, 8), -1.0, OP.mult)
                sums = send(m + 1, a("SND", so, so + NX[t]))
                if e == 0:
                    end_table(t)
                if t == 1:
                    for i in range(4):
                        cp(a("LI", i, 160, 4), a("LU", hp(i // 2) + i % 2, hp(i // 2) + 80, 2))
                    lists = [lambda c0, c1, x=x: a("LI", x + c0, x + c1) for x in (80, 0)]
                else:
                    cp(a("LL"), a("LB"))
                    lists = [lu, lambda c0, c1: a("LL", c0, c1)]
                sl, sr, kids = (2 * t - 1) * V, 2 * t * V, []
                for gx, lst, slot in (("G0", lists[0], sr), ("G1", lists[1], sl)):
                    for lo, hi in pieces(0, V, 256):
                        if gx == "G1" and lo < GV[t]:
                            ts(a(gx, lo, hi), ind(a("KP"), lst(lo // 16, hi // 16)), 1.0 / 4096, OP.mult, -C0, OP.add)
                        else:
                            act(a(gx, lo, hi), ind(a("KP"), lst(lo // 16, hi // 16)), bias=-C0, scale=1.0 / 4096)
                            in_row("s")
                            kids.append(len(ops) - 1)
                    turn(gx, slot, 0)
                act(a("DM"), bt, AF.Relu, bias=1.0 - Z)
                if t > 1:
                    tt(a("DMM"), rr, a("DMM"), OP.max)
                else:
                    cp(a("DMM"), rr)
                if t > 1:
                    tt(a("EQH", 0, 25), a("GG", 1, 26), a("GG", 0, 25), OP.subtract)
                    tt(a("EQL", 0, 25), a("EQH", 0, 25), a("LC", 25 * (t - 1), 25 * t), OP.mult)
                    expanded()
                    tt(a("SBP", 0, 25), a("SBP", 0, 25), a("EQL", 0, 25), OP.max)
                    tt(a("D1", 0, 24), a("SBP", 0, 24), a("SBP", 1, 25), OP.subtract)
                else:
                    act(a("SBP", 3, 25, 5), a("LC", 3, 25, 5))
                    for j in range((max(KS) + 9) // 10):
                        act(a("NU", 10 * j, 10 * j + 10), a("US", 0, 10), bias=col("CC", 4))
                dead_term(t + 1)
                if t + 1 < RO:
                    roots_ahead(W, t + 1)
                part(a("SND", so, so + NX[t]))
                part(a("PEN", 30 - 10 * t, 40))
                part(a("NU", ev, ks), ev)
                for x in [a("SND", co, co + 10 * t), a("PEN", 70 - 10 * t, 70)] + landed(mc, ahead, CL[t]):
                    mm(a("PC", 0, 10 * t), [(a("ID32"), x)], grp="counts%d" % m)
                act(a("RC", 0, 10 * t), a("PC", 0, 10 * t), AF.Relu)
                ops[-1]["after"].append((kids[RP[t]], 0.0))
                zero = [a("RC", 10 * i, 10 * i + 10) for i in range(t)]
                mm(a("PU", 0, 10), [(i8, x) for x in zero], grp="sum%d" % len(sends))
                mm(a("PC", 32, 42), [(i8, x) for x in zero])
                nh = a("NHT", 4 - t, 40, 4)
                act(nh, a("PC", 32, 42), AF.Sign)
                if t + 1 < RO:
                    act(a("PEN", 30 - 10 * t, 40 - 10 * t), nh, bias=col("CC", t), scale=BIG)
                    act(a("PEN", 60 - 10 * t, 70 - 10 * t), nh, bias=2.0 ** 18, scale=-BIG)
                continue

            scan(a("HS"), a("NHT"), a("HD"), OP.mult, OP.add)
            ts(a("HT", 0, 5), a("HS", 3, 40, 8), col("PG", 2), OP.mult, pa, OP.add)
            ts(a("HT", 8, 13), a("HS", 7, 40, 8), phi, OP.mult)
            tt(a("HT", 16, 21), a("HT", 0, 5), a("HT", 8, 13), OP.add)
            cp(a("OFB", 0, 5), a("HT", 16, 21))
            lt, bb = a("LT"), a(old)
            steps = [lambda: (ts(a("LB"), pl, 4096.0, OP.mult, float(Z), OP.min), ts(a(old, 0, 80), pr, float(Z), OP.min),
                              ts(a("DZB"), pr, float(Z), OP.is_ge, 32768.0, OP.mult)),
                     lambda: cp(ind(bb, offx), a("LB")),
                     lambda: ts(a("BH"), ind(bb, a("OFB", 0, 5)), -1280.0, OP.add),
                     lambda: tt(a("AM"), a(old, 320, 400), a("BH"), OP.subtract)]
            xu = lambda j, lo2, hi2: ind(lt, a("XU", 80 * j + lo2 // 16, 80 * j + hi2 // 16))
            for j in range(3):
                for lo2, hi2 in pieces(0, XV, XV // 64 * 32):
                    mj = a("XS", lo2, hi2)
                    if j:
                        tt(mj, xu(j, lo2, hi2), mj, OP.add)
                    else:
                        cp(mj, xu(j, lo2, hi2))
                    in_row("v")
                    if steps:
                        steps.pop(0)()
                        if EROW > 1:
                            in_row("v")
                act(a("XS", V * (2 - j) + XV, V * (3 - j)), xu(j, XV, V))
                in_row("s")
            pc = a("PC", 0, 80)
            pick = lambda lo2, hi2: [(a("AA", 128 * i, 128 * i + 128), a("XS", lo2 + i, hi2, 16)) for i in range(16)]
            kill = "kill%d" % e
            mm(pc, [(n8k, a("EQ", 80 * j, 80 * j + 80)) for j in range(2)], grp=kill)
            mm(pc, [(n8k, a("EQ", 160, 240)), (a("ID"), a("DZB"))], grp=kill)
            mm(pc, [(ee(4), a("BH"))], grp=kill)
            for j in (2, 1):
                mm(a("PC", XV // 16, 80), pick(V * j + XV, V * j + V), grp=kill)
            if PS2:
                mm(a("PC", XV // 16, 80), pick(XV, V), grp=kill)
                mm(a("PC", 0, XV // 16), pick(0, XV), grp=kill)
            else:
                mm(pc, pick(0, V), grp=kill)
            ts(a("FL", 80, 160), pc, 1280.0, OP.add, float(Z), OP.min)
            tt(a("XA", 0, 80), a("AM"), pc, OP.add)
            tt(a("XA", 80, 160), a("XA", 0, 80), kv80, OP.min)
            cp(a("FL", 0, 80), a("XA", 80, 160))
            fa = lambda lo2, hi2: a("FL", lo2 // 16, hi2 // 16)
            fb = lambda lo2, hi2: a("FL", 80 + lo2 // 16, 80 + hi2 // 16)

            def both_w(lo2, hi2):
                act(a("GB", lo2, hi2), ind(Wt, fb(lo2, hi2)), bias=2047.5)
                in_row("s")
                tt(a("AB", lo2, hi2), ind(a(W), fa(lo2, hi2)), a("GB", lo2, hi2), OP.add)
                in_row("v")

            def new_w(name, lo2, hi2):
                ts(a(name, lo2, hi2), a("AB", lo2, hi2), 0.5, OP.mult, -1024.0, OP.add)

            if e < EP - 1:
                for i, (lo2, hi2) in enumerate([(0, 128), (128, X)] + pieces(X, V, X)):
                    both_w(lo2, hi2)
                    if i == 2:
                        new_w("W1", 0, X)
                        in_row("v")
                for lo2, hi2 in pieces(X, V, X):
                    new_w("W1", lo2, hi2)
                    if KROW > 1:
                        in_row("k")
                ghosts = [send(9, a("W1", 0, X), "h")]
                colsum("PU", 0, "AB", 0, 8, "ends", ee(4))
                scan(a("SC", 0, 64), a("M8", 0, 64), a("PU", 0, 64), OP.mult, OP.add)
                for k in range(8, NP):
                    rowsum(col("SC", 8 * k + 7), a("AB", 128 * k, 128 * k + 128), False)
                ts(a("SND", 160, 170), a("SC", 7, 80, 8), -0.5, OP.mult, 128 * 1024.0, OP.add)
                sums = send(RO, a("SND", 160, 170))
                ghosts.append(send(9, a("W1", 0, X), "n"))
            else:
                def new_kids(i, lo2, hi2, n):
                    for x0, x1 in pieces(lo2, hi2, n):
                        act(a("G1", x0, x1), ind(a("WB"), fb(x0, x1)))
                        in_row("s")
                        tt(a("G0", x0, x1), ind(a("WA"), fa(x0, x1)), a("G1", x0, x1), OP.add)
                        in_row("v")
                    dma("y", [], [a("G0", lo2, hi2)], T.yk[:, lo2:hi2], T.G0[:, lo2:hi2], "o%d" % i, 2.0 + (hi2 - lo2) / 512)

                def store_w(i, lo2, hi2):
                    new_w("YW", lo2, hi2)
                    in_row("v")
                    dma("y", [], [a("YW", lo2, hi2)], T.yw[:, lo2:hi2], T.YW[:, lo2:hi2], "o%d" % i, 2.0 + (hi2 - lo2) / 1024)

                new_kids(0, 0, X, 128)
                new_kids(1, X, 768, X)
                new_kids(2, 768, V, X)
                both_w(0, 384)
                both_w(384, 640)
                store_w(3, 0, 384)
                both_w(640, WS)
                store_w(4, 384, WS)
                for i, x in enumerate((ind(Wt, fb(WS, V)), ind(a(W), fa(WS, V)))):
                    act(a("MS", V * i + WS, V * i + V), x)
                    in_row("s")
                for pair in ((quart, a("ONES", 0, V - WS)), (half, a("MS", WS, V)), (half, a("MS", V + WS, 2 * V))):
                    mm(a("PD0", 0, V - WS), [pair], grp="halves")
                whole(a("YW", WS, V), a("PD0", 0, V - WS))
                dma("y", [], [a("YW", WS, V)], T.yw[:, WS:V], T.YW[:, WS:V], "o5", 2.2)

    depends(ops)
    order = put_in_order(ops)
    place = {i: n for n, i in enumerate(order)}
    eng = {"g": g, "v": g.vector, "s": g.scalar, "p": g.tensor, "y": g.sync}
    known = {q: {} for q in eng}
    first, final = {}, {}
    for i in order:
        o = ops[i]
        q = o["q"]
        o["key"] = ("own", i) if isinstance(o["sem"], tuple) else q
        o["waits"] = []
        if q != "x":
            for j in sorted(o["hard"], key=lambda j: -place[j]):
                if known[q].get(ops[j]["key"], -1) >= place[j]:
                    continue
                o["waits"].append(j)
                ops[j]["need"] = True
                for k2, v2 in ops[j]["snap"].items():
                    if known[q].get(k2, -1) < v2:
                        known[q][k2] = v2
            o["snap"] = dict(known[q])
        else:
            o["snap"] = {}
        o["snap"][o["key"]] = place[i]
        first.setdefault(o["grp"], i)
        final[o["grp"]] = i
    count = {q: 0 for q in eng}
    for i in order:
        o = ops[i]
        q = o["q"]
        if isinstance(o["sem"], tuple):
            o["tok"] = o["sem"]
        elif o.get("need"):
            count[q] += 1
            o["tok"] = ("q" + q, count[q])
        if q == "x":
            continue
        for j in o["waits"]:
            eng[q].wait_ge(T.sem[ops[j]["tok"][0]], ops[j]["tok"][1])
        ins = o["fn"](eng[q], first[o["grp"]] == i, final[o["grp"]] == i) if o["grp"] else o["fn"](eng[q])
        if isinstance(o["sem"], tuple):
            ins.then_inc(T.sem[o["sem"][0]], o["sem"][1])
        elif o.get("need"):
            ins.then_inc(T.sem["q" + q], 1)
    for i in range(6):
        g.sync.wait_ge(T.sem["o%d" % i], 16)
    g.wait_ge(T.sem.sent, sent[0])
